import numpy as np, ml_dtypes
CORES = [25,29,65,69,153,157,193,197]
N = 8
BF = ml_dtypes.bfloat16
def gentries(a):
    return np.ascontiguousarray(a.reshape(8, 16, -1).transpose(0, 2, 1)).reshape(8, -1)
def gtable(e):
    e = np.asarray(e); return np.ascontiguousarray(e.reshape(8, -1, 16).transpose(0, 2, 1)).reshape(128, -1).astype(np.int32)
W, L, C, VIS, SLOT, Q = 3072, 4096, 256, 3, 192, 7
GM = 255 * L
def cuts(rng, tot, k):
    return np.diff(np.concatenate([[0], np.sort(rng.integers(0, tot + 1, k - 1)), [tot]]))
def some(rng, tot, k):
    n = np.zeros(C, np.int64); n[rng.permutation(C)[:k]] = cuts(rng, tot, k)
    return n
def pack(x, o, n, gt):
    return {"aud": np.ascontiguousarray(x.reshape(N, 128, W)).astype(np.float32).astype(BF), "spots": np.stack([gtable(a) for a in o]),
            "lens": np.ascontiguousarray(n).astype(np.int32), "gua": np.ascontiguousarray(gt.reshape(N, 128, C)).astype(np.int32)}
def contrast(rng, sizes):
    st = rng.choice(np.array(sizes), (N, 8, 1, 1)); tot = rng.integers(13 * L // 16, 15 * L // 16, (N, 8))
    for g in range(8):
        q = int(rng.integers(0, N)); st[q, g] = sizes[-1]; st[(q + 1) % N, g] = sizes[0]; tot[(q + 1) % N, g] = L
    return st, tot
def parts(rng):
    st, tot = contrast(rng, [0.45, 0.6, 0.8, 1.0])
    x = (255 * st * (0.25 + 0.75 * rng.random((N, 8, 1, W))) * (0.5 + 0.5 * rng.random((N, 8, 16, W)))).astype(np.int64)
    o = rng.integers(0, W, (N, 8, L))
    n = np.stack([np.stack([cuts(rng, int(tot[r, g]), C) for g in range(8)]) for r in range(N)])
    gt = 84 * (n[:, :, None] - 2 + 5 * rng.random((N, 8, 1, C))) * (0.85 + 0.3 * rng.random((N, 8, 16, C)))
    return x, o, n, np.minimum(np.maximum(gt, 0).astype(np.int64), GM)
def exact(rng, xg, o, n, R, S, low=False):
    tot = int(np.add.reduce(n)); end = np.add.accumulate(n); beg = end - n; own = np.repeat(np.arange(C), n)
    cs = np.concatenate([np.zeros((16, 1), np.int64), np.add.accumulate(xg[:, o[:tot]], axis=1)], axis=1)
    who = rng.permutation(C)
    if low: who = who[np.argsort(n[who], kind="stable")]
    short = np.zeros(C, bool); short[who[:S]] = True
    pool = np.nonzero(~short[own])[0]; cut = np.bincount(own[rng.permutation(pool)[:R]], minlength=C)
    coin = rng.random(C) < 0.5; pr = np.argsort(rng.random((16, C)), axis=0); lift = rng.choice(np.array([1, 40, GM]), C)
    hold = cs[:, end - cut] - cs[:, beg]; full = cs[:, end] - cs[:, beg]
    v = hold + lift * (coin & (pr < Q - 1)); u = np.where(pr < Q, full + 1, np.where(coin, 0, full + 1))
    return np.minimum(np.where(short, u, v), GM)
def hunger(rng, x, o, n, gt, g):
    for r in range(N):
        pr = np.argsort(rng.random((16, C)), axis=0); u = rng.integers(1, 512, (1, C)); k = rng.integers(Q, 17, C)
        o[r, g] = rng.integers(0, W, L); n[r, g] = 0
        if r % 2 == 0:
            c = int(rng.integers(0, C)); n[r, g, c] = L; k[c] = 0
        if r % 4 == 3: k[rng.permutation(C)[int(rng.integers(1, 4)):]] = Q - 1
        gt[r, g] = u * (pr < k)
def filled(rng, x, o, n, gt, g):
    xv = x[:, g]
    for r in range(N):
        bl = r + N * rng.permutation(W // N); pr = np.argsort(rng.random((16, C)), axis=0)
        o[r, g] = bl[rng.integers(0, W // N, L)]; n[r, g] = 0; gt[r, g] = 0
        if r % 4 == 0:
            top = rng.integers(200, 256, (16, W // N))
            for p in range(N): xv[p][:, bl] = top if p == r else top >> 2
            who = np.sort(rng.permutation(C)[:7]); n[r, g, who[1:]] = L // 8 + rng.integers(0, 16, 6)
            n[r, g, who[0]] = L - int(np.add.reduce(n[r, g]))
            end = np.add.accumulate(n[r, g])
            cs = np.concatenate([np.zeros((16, 1), np.int64), np.add.accumulate(xv[r][:, o[r, g]], axis=1)], axis=1)
            full = cs[:, end] - cs[:, end - n[r, g]]
            for j in range(6):
                c = int(who[j + 1])
                gt[r, g][:, c] = np.where(pr[:, c] < Q, full[:, c] + 1, 0) if j % 2 == 0 else np.where(pr[:, c] < Q - 1, GM, full[:, c])
        if r % 4 == 1:
            xv[:, :, bl] = 255; n[r, g, 0] = L
            gt[r, g] = (pr < Q) * rng.integers(0, 300, (1, C)); gt[r, g][:, 0] = GM
        if r % 4 == 2:
            xv[:, :, bl] = 0; xv[(r + VIS - 1) % N][:, bl] = 255
            c = int(rng.integers(0, C)); n[r, g, c] = L // 2; gt[r, g][:, c] = 255
        if r % 4 == 3:
            n[r, g] = cuts(rng, L, C); gt[r, g] = GM
def few(rng, x, o, n, gt, g):
    xv = x[:, g]; sh = int(rng.integers(0, 4))
    for r in range(N):
        v = (r + sh) % 4; u = r + N * rng.permutation(W // N)[:3]; low = rng.integers(1, 64, (16, 3)); pr = np.argsort(rng.random(16))
        xv[:, :, u] = low; goal = np.add.reduce(low[:, :v], axis=1); a, b = rng.permutation(C)[:2]
        if v: xv[(r + 1) % N][:, u[0]] = goal
        n[r, g] = 0; n[r, g, a] = v; o[r, g, :v] = u[:v]
        gt[r, g] = 0; gt[r, g][:, a] = goal; gt[r, g][:, b] = pr < Q
def setup_inputs(rng):
    return pack(*parts(rng))
def setup_inputs_spread(rng):
    st, tot = contrast(rng, [0.25, 0.5, 1.0])
    x = np.minimum((st * np.exp2(8 * rng.random((N, 8, 1, W))) * (0.25 + 0.75 * rng.random((N, 8, 16, W)))).astype(np.int64), 255)
    o = rng.integers(0, W, (N, 8, L)); n = np.zeros((N, 8, C), np.int64)
    for r in range(N):
        for g in range(8):
            k = int(tot[r, g]); c = np.sort((k * rng.random(C - 1) ** 3).astype(np.int64))
            n[r, g] = np.diff(np.concatenate([[0], c, [k]]))
    m = n[:, :, None]; e = rng.random((N, 8, 1, C))
    gt = np.where(m > 0, 17 * m * np.exp2(-3 + 3.7 * e), np.exp2(8 * e) - 1) * (0.7 + 0.6 * rng.random((N, 8, 16, C)))
    gt = np.where(rng.random((N, 8, 1, C)) < 0.0625, np.exp2(20 * rng.random((N, 8, 16, C))), gt)
    return pack(x, o, n, np.minimum(gt.astype(np.int64), GM))
def setup_inputs_ends(rng):
    x = 255 * ((rng.random((N, 8, 1, W)) < 0.6) ^ (rng.random((N, 8, 16, W)) < 0.05)).astype(np.int64)
    o = np.zeros((N, 8, L), np.int64); n = np.zeros((N, 8, C), np.int64); gt = np.zeros((N, 8, 16, C), np.int64)
    for r in range(N):
        vs = rng.permutation(5)
        for g in range(8):
            one = int(rng.integers(0, 2)); lone = (r + g) % 2 == 0
            x[r, g, :, 0] = 255 if lone else 255 * one; x[r, g, :, W - 1] = 255 if lone else 255 * (1 - one)
            pr = np.argsort(rng.random((16, C)), axis=0); live = rng.random(C) < 0.3; live[C - C // 16:] = False
            k = rng.integers(0, Q, C); k[C - C // 16:] = rng.integers(Q, 17, C // 16)
            ends = rng.choice(np.array([0, W - 1]), L)
            if lone: o[r, g] = ends
            else:
                o[r, g] = np.where(rng.random(L) < 0.8, ends, rng.integers(0, W, L)); s = np.argsort(rng.random(C) - 0.5 * live)[:3 * C // 10]
                n[r, g, s] = cuts(rng, 7 * L // 8, len(s))
            j = rng.integers(1, 4, C) if lone else 1 + (rng.random(C) * (n[r, g] + 1)).astype(np.int64)
            gt[r, g] = np.where(live, 255 * j, GM * (pr < k))
            if lone:
                c = int(rng.choice(np.array([0, C // 2 + 1, C - 1]))); v = int(vs[g // 2])
                if r == N - 1 and g == 7: c = C - 1; v = 0
                if r == 0 and g == 0: v = 1
                n[r, g, c] = L; h = pr[:, c]
                gt[r, g, :, c] = (GM * (h >= 0), (GM - 255) * (h >= 0), GM * (h < Q - 1), GM * (h < Q), 255 * (h >= 0))[v]
    return pack(x, o, n, np.minimum(gt, GM))
def setup_inputs_corners(rng):
    assert SLOT + 4 <= C
    x, o, n, gt = parts(rng)
    cases = [(SLOT, SLOT, L), (SLOT + 1, SLOT + 1, L - SLOT), (SLOT - 1, SLOT, L - SLOT), (1, 1, L), (0, C, L), (-1, 0, 0), (SLOT, 1, L), (3 * SLOT, SLOT + 1, L - SLOT + 1)]
    for r in range(0, N, 2):
        sh = int(rng.integers(0, 8)); q = r + 1
        for g in range(8):
            d, e, tot = cases[(g + sh) % 8]; s = int(rng.integers(0, C // 8))
            if d < 0: n[r, g] = some(rng, L, C - C // 8); gt[r, g] = exact(rng, x[r, g], o[r, g], n[r, g], L, C // 8, True)
            else: n[r, g] = cuts(rng, 15 * L // 16, C); gt[r, g] = exact(rng, x[r, g], o[r, g], n[r, g], s + d, s)
            k = 0 if e == 0 or e == C else int(rng.integers(0, 4))
            n[q, g] = cuts(rng, tot, C); gt[q, g] = exact(rng, x[q, g], o[q, g], n[q, g], k, e + k)
    return pack(x, o, n, gt)
def setup_inputs_crowd(rng):
    x, o, n, gt = parts(rng)
    for r in range(N):
        w = W - N + r
        for g in range(8):
            role = (g - r) % 8; o[r, g] = w
            if role in (1, 3): o[r, g, int(rng.integers(0, L))] = int(rng.integers(4, W - N))
            if role in (6, 7): o[r, g] = rng.choice(np.array([0, 1, 2, 3, w]), L)
            if role in (4, 5):
                n[r, g] = 0; c = int(rng.integers(0, C)); n[r, g, c] = L
                x[r, g, :, w] = 0; x[(r + 1) % N, g, :, w] = 255
                gt[r, g] = 255 * rng.integers(0, 2, (1, C)); gt[r, g, :, c] = 255 + (role == 5)
                continue
            n[r, g] = cuts(rng, L, C) if role < 2 else some(rng, L, C - C // 4) if role < 4 else cuts(rng, 7 * L // 8, C)
            R, S = ((0, C), (0, C - 1), (L, C // 4), (L - 1, C // 4), (0, 0), (0, 0), (C // 4, C // 4), (C // 8 + SLOT, C // 8))[role]
            gt[r, g] = exact(rng, x[r, g], o[r, g], n[r, g], R, S, role in (2, 3))
    two = rng.permutation(8)[:2]
    hunger(rng, x, o, n, gt, int(two[0])); filled(rng, x, o, n, gt, int(two[1]))
    return pack(x, o, n, gt)
def setup_inputs_calm(rng):
    x = np.repeat(rng.integers(100, 256, (1, 8, 16, W)), N, axis=0); base = x[0].copy()
    o = rng.integers(0, W, (N, 8, L)); n = np.zeros((N, 8, C), np.int64); gt = np.zeros((N, 8, 16, C), np.int64)
    for r in range(N):
        for g in range(8):
            bl = r + N * rng.permutation(W // N); R = rng.integers(0, 4, N); S = rng.integers(0, 4, N); R[1] = g % 4; S[1] = (g // 4 + r) % 4
            tau = np.concatenate([np.repeat(np.arange(N), R), np.repeat(np.arange(N), S)]); m = len(tau); h = int(np.add.reduce(R)); rel = np.arange(m) < h
            sc = rng.permutation(C)[:m]; a = bl[:m]; b = bl[m:m + h]; rest = bl[m + h:]
            pr = np.argsort(rng.random((16, m)), axis=0); xv = x[:, g]; xv[:, :, b] = 1
            for p in range(N):
                late = (p - r) % N >= tau
                xv[p][:, a] = base[g][:, a] - (pr < Q - (late == rel))
            tot = 3 * L // 4; nb = cuts(rng, tot, C); nm = rest[rng.integers(0, len(rest), tot)]; end = np.add.accumulate(nb); beg = end - nb
            cs = np.concatenate([np.zeros((16, 1), np.int64), np.add.accumulate(base[g][:, nm], axis=1)], axis=1); full = cs[:, end] - cs[:, beg]
            gt[r, g] = full + ((rng.random(C) < 0.5) & (np.argsort(rng.random((16, C)), axis=0) < Q - 1)); gt[r, g][:, sc] = full[:, sc] + base[g][:, a]
            names = np.concatenate([nm, a, b]); camp = np.concatenate([np.repeat(np.arange(C), nb), sc, sc[:h]])
            o[r, g, :len(names)] = names[np.argsort(camp, kind="stable")]; n[r, g] = np.bincount(camp, minlength=C)
    few(rng, x, o, n, gt, int(rng.integers(0, 8)))
    return pack(x, o, n, gt)
def check_inputs(d):
    bad = []
    for k, lo, hi in (("aud", 0, 255), ("spots", 0, W - 1), ("lens", 0, L), ("gua", 0, GM)):
        a = np.asarray(d[k]).astype(np.float64)
        if not np.all((a >= lo) & (a <= hi)): bad.append("range of " + k)
    a = np.asarray(d["aud"]).astype(np.float64)
    if np.any(a != np.floor(a)): bad.append("whole numbers in aud")
    if np.max(np.add.reduce(np.asarray(d["lens"]).astype(np.int64), axis=2)) > L: bad.append("sum of lens in a group")
    return bad
def reference(aud, spots, lens, gua):
    x = aud.astype(np.float32).astype(np.int64).reshape(N, 8, 16, W); gt = gua.astype(np.int64).reshape(N, 8, 16, C)
    nm = np.stack([gentries(a) for a in spots]).astype(np.int64); ln = lens.astype(np.int64)
    for t in range(VIS):
        kept, sent = {}, {}
        for r in range(N):
            p = (r + t) % N
            for g in range(8):
                k = ln[r, g]; tot = int(np.add.reduce(k)); o = nm[r, g, :tot]; own = np.repeat(np.arange(C), k)
                end = np.add.accumulate(k); beg = end - k
                cs = np.concatenate([np.zeros((16, 1), np.int64), np.add.accumulate(x[p, g][:, o], axis=1)], axis=1)
                before = cs[:, :tot] - cs[:, beg[own]]; full = cs[:, end] - cs[:, beg]
                need = np.add.reduce((before < gt[r, g][:, own]).astype(np.int64), axis=0) >= Q
                short = np.nonzero(np.add.reduce((full < gt[r, g]).astype(np.int64), axis=0) >= Q)[0]
                rel = o[~need]; a = min(len(rel), len(short))
                more = np.full(C, -1, np.int64); more[short[:a]] = rel[:a]
                kept[r, g] = (o[need], own[need], more, short[a:]); sent[r, g] = rel[a:a + SLOT]
        new, nl = np.full((N, 8, L), -1, np.int64), np.zeros((N, 8, C), np.int64)
        for r in range(N):
            for g in range(8):
                o, own, more, rest = kept[r, g]; come = sent[(r - 1) % N, g]; a = min(len(come), len(rest))
                more[rest[:a]] = come[:a]; c = np.nonzero(more >= 0)[0]
                camp = np.concatenate([own, c]); w = np.argsort(camp, kind="stable")[:L]
                new[r, g, :len(w)] = np.concatenate([o, more[c]])[w]; nl[r, g] = np.bincount(camp[w], minlength=C)
        nm, ln = new, nl
    return {"yo": np.stack([gtable(a) for a in nm]).astype(np.float32), "yn": ln.astype(np.float32)}

@@ -1,0 +1,818 @@
+import numpy as np
+from concourse.bass import DstId, RemoteDMATransfer
+from concourse.mybir import AluOpType as OP, ActivationFunctionType as AF
+
+N, W, L, C, SLOT = 8, 3072, 4096, 256, 192
+NQ = C + SLOT
+SH = 1536.0
+EW = 3 * C
+NEG = EW + L
+DUMP = L + 2 * C
+F32, BF, F16, I32, U16 = "float32", "bfloat16", "float16", "int32", "uint16"
+M1W, M1S = 144, 106
+M2S = (28, 44, 60)
+CY, GATH, SCAT, GAP, FLY = 0.83e-3 * 1.25, 1.56, 3.8, 0.15, 4.5
+PLAN, SEED, TRIES, MOVES = {}, 1, 600, 30000
+
+SCRATCH = {
+    "audb": ("sbuf", [128, W + 16], BF), "win": ("sbuf", [128, NEG + 8], F32), "yb": ("sbuf", [128, L + C], F32),
+    "ib": ("sbuf", [128, L + C], F32), "h0": ("sbuf", [128, DUMP + 2 * C], F32), "hf": ("sbuf", [128, DUMP + 2 * C], F32),
+    "mk0": ("sbuf", [128, L + C], BF), "mk1": ("sbuf", [128, L + C], BF), "mk2": ("sbuf", [128, L + C], BF),
+    "sg": ("sbuf", [128, L], BF), "rs": ("sbuf", [128, 2048], BF),
+    "sf": ("sbuf", [128, 12600], F32), "sb": ("sbuf", [128, 4400], BF), "sh": ("sbuf", [128, 2600], F16),
+    "si": ("sbuf", [128, 1700], I32), "su": ("sbuf", [128, 640], U16),
+    "spi": ("sbuf", [128, C], I32), "gi": ("sbuf", [128, C], I32), "li": ("sbuf", [128, C], I32),
+}
+for _t in range(3):
+    SCRATCH["lu%d" % _t] = ("sbuf", [128, C], U16)
+    SCRATCH["lo%d" % _t] = ("sbuf", [128, 32], U16)
+    SCRATCH["lf%d" % _t] = ("sbuf", [128, C + 80], F32)
+    SCRATCH["lb%d" % _t] = ("sbuf", [128, C], BF)
+    SCRATCH["sp%d" % _t] = ("sbuf", [128, C], F32)
+    for _r in "sab":
+        SCRATCH["m1%s%d" % (_r, _t)] = ("sbuf", [128, M1W], F32)
+        SCRATCH["m2%s%d" % (_r, _t)] = ("sbuf", [128, 64], U16)
+for _b in range(8):
+    SCRATCH["ps%d" % _b] = ("psum", [128, 512], F32)
+
+POOLS = {"v": 44, "a": 20, "t": 16, "g": 10, "d": 30}
+ARR = ["lu1", "lu2", "lf1", "lf2", "lb1", "lb2"] + ["m%d%s%d" % (k, r, t) for t in range(3) for k in (1, 2) for r in "ab"]
+SEMAPHORES = ["%s%d" % (e, i) for e in POOLS for i in range(POOLS[e])] + ["r" + a for a in ARR] + ["sent"]
+
+
+def messages():
+    out = [("lu0", C, [("lu1", 1), ("lu2", 2)]), ("lf0", C + 80, [("lf1", 1), ("lf2", 2)]),
+           ("lb0", C, [("lb1", 1), ("lb2", 2)])]
+    for t in range(3):
+        a, b = (1, 2) if t < 2 else (-2, -1)
+        out.append(("m1s%d" % t, M1S, [("m1a%d" % t, a), ("m1b%d" % t, b)]))
+        out.append(("m2s%d" % t, M2S[t], [("m2a%d" % t, a), ("m2b%d" % t, b)]))
+    return out
+
+
+def hop(T, topo, r, k, step):
+    src, dst = T.cores[r], T.cores[(r + step) % N]
+    if topo.may_write(src, dst):
+        return dst, dst
+    rel = [c for c in topo.cores_of(src) if topo.die(c) == topo.die(src) and T.rank_of(c) is None and topo.may_write(c, dst)]
+    return rel[k % len(rel)], dst
+
+
+def bits(engs):
+    return sum(1 << e for e in engs)
+
+
+def relay_program(g, core, T, topo):
+    n = 0
+    for r in range(N):
+        for src, cols, dsts in messages():
+            for k, (buf, step) in enumerate(dsts):
+                first, dst = hop(T, topo, r, k, step)
+                if first == core and first != dst:
+                    g.wait_ge(T.sem["r" + buf], 8)
+                    rid, pid = topo.addr(dst, core)
+                    e = topo.engines(core, dst)[:8]
+                    g.remote_dma(T[buf][:, 0:cols], T[buf][:, 0:cols], T.sem["r" + buf], T.sem.sent, pid, rid, bits(e))
+                    n += len(e)
+    if n:
+        g.wait_ge(T.sem.sent, n)
+
+
+def rank_program(g, core, T, topo):
+    rank = T.rank_of(core)
+    if rank is None:
+        relay_program(g, core, T, topo)
+        return
+    Q = {"v": g.vector, "a": g.scalar, "t": g.tensor, "g": g, "s": g.sync}
+    ops, acc, known = [], {}, {q: set() for q in Q}
+    last = {}
+    waited = {}
+    top = {"sf": 0, "sb": 0, "sh": 0, "si": 0, "su": 0}
+
+    def new(buf, n):
+        c = top[buf]
+        top[buf] = c + (n + 15) // 16 * 16
+        assert top[buf] <= SCRATCH[buf][1][1], buf
+        return (buf, c, c + n, 1, None)
+
+    def B(name, a, b, step=1, p=None):
+        return (name, a, b, step, p)
+
+    def S(x, a, b, step=1, p=None):
+        return (x[0], x[1] + a, x[1] + b, step, p)
+
+    def IND(w, off):
+        return ("ind", w, off)
+
+    def ap(x):
+        if not isinstance(x, tuple):
+            return x
+        if x[0] == "ind":
+            return ap(x[1]).indirect(ap(x[2]))
+        p = x[4] or (0, 128, 1)
+        ps = slice(p[0], p[1]) if p[2] == 1 else slice(p[0], p[1], p[2])
+        cs = slice(x[1], x[2]) if x[3] == 1 else slice(x[1], x[2], x[3])
+        return T[x[0]][ps, cs]
+
+    def op(q, rd, wr, emit, busy, lat=0.0, pool=None, inc=1, after=()):
+        tt_ = []
+        for x, w in [(x, False) for x in rd] + [(x, True) for x in wr]:
+            if not isinstance(x, tuple):
+                continue
+            if x[0] == "ind":
+                tt_ += [(x[1], w), (x[2], False)]
+            else:
+                tt_.append((x, w))
+        reg = [((x[0], 0, 512, True) if x[0].startswith("ps") else (x[0], x[1], x[2], w)) for x, w in tt_]
+        need = set()
+        for b, c0, c1, w in reg:
+            for d0, d1, i, v in acc.get(b, []):
+                if (w or v) and d0 < c1 and c0 < d1:
+                    need.add(i)
+        i = len(ops)
+        ind = any(isinstance(x, tuple) and x[0] == "ind" for x in list(rd) + list(wr))
+        ops.append(dict(q=q, w=reg[-1][:2], ind=ind, need=need, after=set(after), emit=emit, busy=busy, lat=lat, pool=pool or q, inc=inc))
+        for b, c0, c1, w in reg:
+            acc.setdefault(b, []).append((c0, c1, i, w))
+        return i
+
+    def wd(x):
+        return 16 * wd(x[2]) if x[0] == "ind" else (x[2] - x[1] + x[3] - 1) // x[3]
+
+    def two(x):
+        return SCRATCH[x[0]][2] in (BF, F16, U16)
+
+    def cost(o, ins, per=None):
+        if o[0] == "ind":
+            return 0.05 + wd(o) * SCAT * CY
+        if ins and ins[0][0] == "ind":
+            return 0.05 + wd(o) * GATH * CY
+        if per is None:
+            per = 0.5 if all(two(x) for x in [o] + ins) else 1.0
+        return max(64, wd(o) * per) * CY
+
+    def cp(o, a):
+        op("v", [a], [o], lambda: [g.vector.tensor_copy(ap(o), ap(a))], cost(o, [a]))
+
+    def tt(o, a, b, f):
+        op("v", [a, b], [o], lambda: [g.vector.tensor_tensor(ap(o), ap(a), ap(b), f)], cost(o, [a, b], 1 if a[0][:2] == "ps" else 2))
+
+    def ts(o, a, s1, f1, s2=None, f2=None):
+        if f2 is None:
+            op("v", [a, s1], [o], lambda: [g.vector.tensor_scalar(ap(o), ap(a), ap(s1), None, f1)], cost(o, [a]))
+        else:
+            op("v", [a, s1, s2], [o], lambda: [g.vector.tensor_scalar(ap(o), ap(a), ap(s1), ap(s2), f1, f2)], cost(o, [a]))
+
+    def scan(o, d0, d1, init, f0, f1):
+        op("v", [d0, d1, init], [o], lambda: [g.vector.tensor_tensor_scan(ap(o), ap(d0), ap(d1), ap(init), f0, f1)], cost(o, [d0, d1]))
+
+    def ms(o, c):
+        op("v", [], [o], lambda: [g.vector.memset(ap(o), c)], cost(o, []))
+
+    def act(o, a, f=AF.Identity, bias=0.0, scale=1.0):
+        op("a", [a, bias], [o], lambda: [g.scalar.activation(ap(o), ap(a), f, bias=ap(bias), scale=scale)], 0.05 + cost(o, [a], 1))
+
+    def mm(items):
+        op("t", [x for m in items for x in m[1:3]], [m[0] for m in items],
+           lambda: [g.tensor.matmul(ap(o), ap(l), ap(r), a, z) for o, l, r, a, z in items],
+           sum(max(64, wd(m[2])) * (1 if two(m[2]) else 4) * CY for m in items))
+
+    def iota(o, pat, base, cm):
+        if o[0] == "si":
+            op("g", [], [o], lambda: [g.iota(ap(o), pat, base, cm)], 0.13 + 2 * wd(o) * CY)
+        else:
+            op("g", [], [o], lambda: [g.iota(ap(o), pat, base, cm, allow_small_or_imprecise_dtypes=True)], 0.13 + 2 * wd(o) * CY)
+
+    def pick(o, a, pat, f, base, cm):
+        op("g", [a], [o], lambda: [g.affine_select(ap(o), ap(a), pat, f, 0.0, base, cm)], 0.17 + 2 * wd(o) * CY)
+
+    def fill(o, c, step=544):
+        for lo in range(0, wd(o), step):
+            hi = min(wd(o), lo + step)
+            iota(S(o, lo, hi), [[0, hi - lo]], c, 0)
+
+    def dma(q, o, a, us=2.1):
+        op(q, [a], [o], lambda: [Q[q].dma_start(ap(o), ap(a))], 0.1, us, pool="d", inc=16)
+
+    msgs = {m[0]: m for m in messages()}
+    sent, sends = [0], []
+
+    def send(name):
+        src, cols, dsts = msgs[name]
+
+        def emit():
+            tr = []
+            for k, (buf, step) in enumerate(dsts):
+                first, dst = hop(T, topo, rank, k, step)
+                rid, pid = topo.addr(first, core)
+                e = topo.engines(core, first)[8 * k:8 * k + 8]
+                tr.append(RemoteDMATransfer(dst_ids=[DstId(rid=rid, pnc=pid)], dma_engine_mask=bits(e), remote_sem=T.sem["r" + buf],
+                                            src=T[src][:, 0:cols], dst=T[buf][:, 0:cols]))
+                sent[0] += len(e)
+            g.remote_dma_fused(tr, local_sem=T.sem.sent)
+            return []
+        i = op("g", [B(src, 0, cols)], [], emit, 0.5, after=sends[-1:], pool="-")
+        sends.append(i)
+        for buf, step in dsts:
+            op(None, [], [B(buf, 0, 512)], None, 0.0, FLY + cols * (2 if two((src,)) else 4) * 0.004, pool="r" + buf, after=[i])
+
+    def finish():
+        n = len(ops)
+        pre = [o["need"] | o["after"] for o in ops]
+        rank_ = [0.0] * n
+        for i in range(n - 1, -1, -1):
+            rank_[i] += ops[i]["busy"] + ops[i]["lat"] + GAP
+            for j in pre[i]:
+                rank_[j] = max(rank_[j], rank_[i])
+        post = [[] for _ in ops]
+        for i in range(n):
+            for j in pre[i]:
+                post[j].append(i)
+
+        def plan(prio, back=False):
+            start, end, slots = [0.0] * n, [0.0] * n, {q: [] for q in Q}
+            up, down = (post, pre) if back else (pre, post)
+            left = [len(p) for p in up]
+            ready = [i for i in range(n) if not left[i]]
+            while ready:
+                i = max(ready, key=lambda i: prio[i])
+                ready.remove(i)
+                o = ops[i]
+                t = max([end[j] + GAP for j in up[i]] + [0.0]) + (o["lat"] if back else 0.0)
+                if o["q"]:
+                    sl = slots[o["q"]]
+                    k = 0
+                    for a, b in sl:
+                        if b > t:
+                            if t + o["busy"] <= a:
+                                break
+                            t = b
+                        k += 1
+                    sl.insert(k, (t, t + o["busy"]))
+                start[i], end[i] = t, t + o["busy"] + (0.0 if back else o["lat"])
+                for j in down[i]:
+                    left[j] -= 1
+                    if not left[j]:
+                        ready.append(j)
+            return end, sorted(range(n), key=lambda i: (start[i] if i > 1 else -1.0, i))
+
+        def span(order, fi, fl, gap):
+            end, free = [0.0] * n, {q: 0.0 for q in Q}
+            for i in order:
+                o = ops[i]
+                t = max([end[j] + gap for j in pre[i]] + [free.get(o["q"], 0.0)])
+                b = o["busy"] * (fi if o["ind"] else 1.0)
+                if o["q"]:
+                    free[o["q"]] = t + b
+                end[i] = t + b + o["lat"] * (fl if o["q"] is None else 1.0)
+            return max(end)
+
+        if "order" not in PLAN:
+            rng = np.random.default_rng(SEED)
+            best, prio = None, list(rank_)
+            PLAN["dbg"] = (ops, pre, rank_)
+            for it in range(TRIES):
+                e = rng.normal(0, 1.0, n) * (rng.random(n) < 0.05) * (it > 0)
+                if it % 2:
+                    k = int(rng.integers(0, n))
+                    e = np.zeros(n)
+                    e[k:k + int(rng.integers(2, 40))] = rng.normal(0, 3.0)
+                p = [x + float(y) for x, y in zip(prio, e)]
+                for rep in range(2):
+                    end, order = plan(p)
+                    v = sum(span(order, *s) for s in ((1, 1, GAP), (0.75, 0.8, 0.1), (1.3, 1.4, 0.25)))
+                    if best is None or v <= best:
+                        best, prio, PLAN["order"], PLAN["us"] = v, p, order, v / 3
+                    if rep == 0:
+                        p = plan(end, True)[0]
+            rows_ = [(list(pre[i]), "vatgs".find(o["q"] or "-"), [o["busy"] * (f if o["ind"] else 1.0) for f in (1, 0.75, 1.3)],
+                      [o["lat"] * (f if o["q"] is None else 1.0) for f in (1, 0.8, 1.4)]) for i, o in enumerate(ops)]
+
+            def span3(order):
+                tot = 0.0
+                for s, gap in enumerate((GAP, 0.1, 0.25)):
+                    end, free = [0.0] * n, [0.0] * 6
+                    for i in order:
+                        p, q, b, l = rows_[i]
+                        t = free[q]
+                        for j in p:
+                            if end[j] > t:
+                                t = end[j]
+                        t += b[s]
+                        if q >= 0:
+                            free[q] = t
+                        end[i] = t + l[s] + gap
+                    tot += max(end) + 0.01 * sum(end) / n
+                return tot
+            order = PLAN["order"]
+            best = span3(order)
+            for it in range(MOVES):
+                k = int(rng.integers(2, n))
+                i = order[k]
+                lo, hi = k, k
+                while lo > 2 and order[lo - 1] not in pre[i] and k - lo < 60:
+                    lo -= 1
+                while hi < n - 1 and i not in pre[order[hi + 1]] and hi - k < 60:
+                    hi += 1
+                same = [m for m in range(lo, hi + 1) if m != k and rows_[order[m]][1] == rows_[i][1]]
+                if not same:
+                    continue
+                m = same[int(rng.integers(0, len(same)))]
+                cand = order[:k] + order[k + 1:]
+                cand.insert(m, i)
+                v = span3(cand)
+                if v <= best:
+                    best, order = v, cand
+            PLAN["order"], PLAN["us"] = order, best / 3
+        order = PLAN["order"]
+        done = {}
+        pos_ = {i: k for k, i in enumerate(order)}
+
+        def wait(q, i):
+            if i in known[q] or ops[i]["pool"] == "-":
+                return
+            sem, val, snap = done[i]
+            Q[q].wait_ge(T.sem[sem], val)
+            waited[sem] = max(waited.get(sem, 0), val)
+            known[q].add(i)
+            known[q].update(snap)
+
+        for i in order:
+            o = ops[i]
+            q, pool = o["q"], o["pool"]
+            if q is None:
+                done[i] = (pool, 8, frozenset())
+                last[pool] = [8, i]
+                continue
+            for j in sorted(o["need"], key=lambda j: -pos_[j]):
+                wait(q, j)
+            if pool == "-":
+                o["emit"]()
+                continue
+            names = ["%s%d" % (pool, k) for k in range(POOLS[pool])]
+            free = [s for s in names if s not in last or last[s][1] in known[q]]
+            if not free:
+                free = [min(names, key=lambda s: pos_[last[s][1]])]
+                wait(q, last[free[0]][1])
+            s = free[0]
+            val = last[s][0] if s in last else 0
+            for ins in o["emit"]():
+                ins.then_inc(T.sem[s], o["inc"])
+                val += o["inc"]
+            last[s] = [val, i]
+            done[i] = (s, val, frozenset(known[q]))
+        g.wait_ge(T.sem.sent, sent[0])
+        for s in sorted(last, key=lambda s: pos_[last[s][1]]):
+            if waited.get(s, 0) < last[s][0]:
+                wait("g", last[s][1])
+
+    PS = [B("ps%d" % b, 0, 512) for b in range(8)]
+    AUD = B("audb", 0, W + 8)
+    ROW = (0, 128, 16)
+
+    def wrap(o, z, src, n, first=True, final=True):
+        return [(o, S(z, 15 - i, 143 - i), S(src, i, 16 * n, 16), first and i == 0, final and i == 15) for i in range(16)]
+
+    def spread(bank, src, n):
+        mm([(S(bank, i, 16 * n, 16), B("rs", 128 * i, 128 * i + 128), src, True, True) for i in range(16)])
+
+    dma("s", B("li", 0, C, 1, (0, 8, 1)), T.lens[:])
+    dma("a", B("spi", 0, C), T.spots[:])
+    dma("s", B("audb", 0, W // 2), T.aud[:, 0:W // 2], 4.0)
+    dma("a", B("audb", W // 2, W), T.aud[:, W // 2:W], 4.0)
+    dma("s", B("gi", 0, C), T.gua[:], 2.7)
+
+    pi_, pmi = new("si", 1), new("si", 1)
+    pf, pm, pg, row0 = new("sf", 1), new("sf", 1), new("sf", 1), new("sf", 1)
+    selv, sel = new("sf", 128), new("sf", 128)
+    cmod, K = new("sf", NQ), new("sf", NQ)
+    xs, m16 = new("sf", 144), new("sf", 128)
+    s16, cio, jv0, jv = new("sf", 32), new("sf", C), new("sf", C), new("sf", C)
+    P8 = (0, 8, 1)
+    iota(pi_, [[0, 1]], 0, 1)
+    iota(S(selv, 0, 128, 1, P8), [[-1, 8], [0, 16]], 0, 1)
+    iota(cmod, [[0, NQ // 16], [1, 16]], 0, 0)
+    iota(s16, [[16, 32]], 0, 0)
+    iota(xs, [[1, 144]], -15, 0)
+    iota(cio, [[1, C]], 0, 0)
+    iota(jv0, [[1, 16], [256, 16]], 0, 0)
+
+    ones, lf_, ef = new("sf", NQ), new("sf", C + 1), new("sf", C + 1)
+    zb, onb = new("sb", C), new("sb", 1024)
+    for q in range(4):
+        ms(B("mk0", 1088 * q, 1088 * q + 1088), 1.0)
+    ms(ones, 1.0)
+    ms(S(lf_, 0, 1), 0.0)
+    ts(pmi, pi_, 15, OP.bitwise_and)
+    cp(pf, pi_)
+    ms(zb, 0.0)
+    cp(pm, pmi)
+    ts(S(sel, 0, 128, 1, P8), S(selv, 0, 128, 1, P8), 0.0, OP.is_equal)
+    cp(S(lf_, 1, C + 1, 1, P8), B("li", 0, C, 1, P8))
+    ts(K, cmod, pm, OP.is_equal, 2.0e7, OP.mult)
+    scan(S(ef, 0, C + 1, 1, P8), S(ones, 0, C + 1, 1, P8), S(lf_, 0, C + 1, 1, P8), 0.0, OP.mult, OP.add)
+    mm([(S(PS[1], 0, C + 1), S(sel, 0, 128, 1, P8), S(ef, 0, C + 1, 1, P8), True, True)])
+    cp(B("lu0", 0, C), B("spi", 0, C))
+    tt(pg, pf, pm, OP.subtract)
+    d1, d2 = new("sf", 16), new("sf", 32)
+    ts(d1, S(s16, 0, 16), pm, OP.add, float(L), OP.add)
+    d1p = new("sf", 16)
+    act(d1p, d1, bias=1.0)
+    ts(d2, s16, pm, OP.add, float(DUMP), OP.add)
+    ms(B("audb", W, W + 16), 0.0)
+    ms(B("win", L, L + C), 0.0)
+    fill(B("win", L + C, NEG), 0)
+    cp(B("lf0", 0, C), B("gi", 0, C))
+    zwb = new("sb", 144)
+    ts(zwb, xs, pg, OP.is_equal)
+    kb, ke, endw, e0, key0 = new("sf", C), new("sf", C), new("sf", 16), new("sf", 16), new("sf", 16)
+    BEG = [B("lf%d" % t, C, C + 16) for t in range(3)]
+    LEN = [B("lf%d" % t, C + 16, C + 32) for t in range(3)]
+    ZZ = [B("lf%d" % t, C + 32, C + 48) for t in range(3)]
+    G = [B("lf%d" % t, 0, C) for t in range(3)]
+    BOFF = [B("lo%d" % t, 0, 16) for t in range(3)]
+    KEND = [B("lo%d" % t, 16, 32) for t in range(3)]
+    sgz = new("sb", C)
+    act(sgz, G[0], AF.Sign, bias=-0.5)
+    scan(kb, S(K, 0, C), S(PS[1], 0, C), 0.0, OP.max, OP.min)
+    scan(ke, S(K, 0, C), S(PS[1], 1, C + 1), 0.0, OP.max, OP.min)
+    mm(wrap(S(PS[2], 0, 16), zwb, sgz, 16))
+    eqi, eqj, ei, ej = new("si", C), new("si", C), new("si", 16), new("si", 16)
+    send("lu0")
+    endw = B("lf0", C + 48, C + 64)
+    cp(BEG[0], S(kb, 15, C, 16))
+    tt(LEN[0], S(ke, 15, C, 16), S(kb, 15, C, 16), OP.subtract)
+    cp(ei, S(ke, 15, C, 16))
+    ts(e0, LEN[0], 0.5, OP.is_lt, 1.0e5, OP.mult)
+    ts(ej, ei, 4, OP.logical_shift_right)
+    tt(key0, S(kb, 15, C, 16), e0, OP.add)
+    cp(KEND[0], ej)
+    cp(B("lf0", C + 64, C + 80), ej)
+    tt(endw, key0, d1, OP.min)
+    ts(ZZ[0], S(PS[2], 0, 16), -2.5, OP.is_ge)
+    cp(BOFF[0], endw)
+    send("lf0")
+
+    Y = [B("win", 0, L + C), B("yb", 0, L + C), B("hf", 0, L + C)]
+    MK = [B("mk%d" % t, 0, L + C) for t in range(3)]
+    IB = B("ib", 0, L + C)
+    II = [IB, IB, B("yb", 0, L + C)]
+    WIN = B("win", 0, NEG + 8)
+
+    def gather(t, lo, hi, eng="a"):
+        src = IND(AUD, B("lu%d" % t, lo // 16, hi // 16))
+        (act if eng == "a" else cp)(S(Y[t], lo, hi), src)
+
+    def starts(t):
+        tmp = S(lf_, 0, C)
+        (act if t else cp)(tmp, IND(Y[t], BOFF[t]))
+        tt(IND(Y[t], BOFF[t]), tmp, G[t], OP.subtract)
+
+    def sums(t, q):
+        lo, hi = 1024 * q, 1024 * q + 1024
+        scan(S(II[t], lo, hi), S(MK[t], lo, hi), S(Y[t], lo, hi), 0.0 if q == 0 else S(II[t], lo - 1, lo), OP.mult, OP.add)
+        act(B("sg", lo, hi), S(II[t], lo, hi), AF.Sign, bias=0.5)
+        mm(wrap(S(PS[0], 64 * q, 64 * q + 64), zwb, B("sg", lo, hi), 64))
+
+    gather(0, 0, 2560)
+    for q in range(5, 8):
+        gather(0, 512 * q, 512 * q + 512, "v")
+    cp(IND(MK[0], BOFF[0]), zb)
+    starts(0)
+    fill(MK[1], 1)
+    for q in range(4):
+        sums(0, q)
+
+    cp(eqi, S(PS[1], 1, C + 1))
+    blk, tri, gt_ = new("sf", 128), new("sf", 128), new("sf", 128)
+    blkb = new("sb", 128)
+    zw = zwb
+    Fb, Rx, Z1, Z2 = new("sb", C + 2), new("sb", C + 2), new("sb", C + 2), new("sb", C + 2)
+    pick(gt_, S(ones, 0, 128), [[-16, 8], [0, 16]], OP.is_ge, 0, 1)
+    pick(blk, gt_, [[16, 8], [0, 16]], OP.is_ge, 15, -1)
+    ts(eqj, eqi, 15, OP.bitwise_and)
+    fill(onb, 1)
+    pick(tri, blk, [[1, 128]], OP.is_gt, 0, -1)
+    act(blkb, blk)
+    ts(B("lb0", 0, C), eqj, pm, OP.is_gt)
+    send("lb0")
+    ts(row0, pm, 0.0, OP.is_equal)
+    ms(S(Fb, C, C + 2), 0.0)
+    ms(S(Rx, 0, 1), 0.0)
+    ms(S(Rx, C + 1, C + 2), 0.0)
+    ms(S(Z1, 0, 2), 0.0)
+    ms(S(Z2, 0, 2), 0.0)
+    rm18 = new("sf", 54)
+    iota(rm18, [[0, 3], [1, 18]], 0, 0)
+    act(rm18, rm18, AF.Sign)
+    for t in range(3):
+        fill(B("m1s%d" % t, 0, M1W), 0)
+    spack = new("sf", 2 * C)
+    k1, k2 = new("sf", C), new("sf", C)
+    AX, RW = new("sf", C + NQ + 8), new("sf", C + NQ + 8)
+
+    def rows(t):
+        dma("s", B("win", EW, NEG, 1, ROW), B("sp%d" % t, 0, C))
+
+    ts(B("sp0", 0, C), B("lu0", 0, C), SH, OP.subtract)
+    rows(0)
+    act(S(spack, 0, C), cio, scale=32768.0, bias=16.0 * EW + 2048.0)
+    act(B("h0", 0, NQ), B("mk0", 0, NQ), scale=0.0)
+
+    def needed(t):
+        M = new("sf", 16)
+        ts(S(Fb, 0, C), S(PS[0], 0, C), 2.5, OP.is_le)
+        scan(S(Rx, 1, C + 1), S(onb, 0, C), S(Fb, 0, C), 0.0, OP.mult, OP.add)
+        tt(S(Z2, 2, C + 2), IND(Fb, KEND[t]), B("lb%d" % t, 0, C), OP.mult)
+        act(S(Z1, 2, C + 2), IND(Rx, KEND[t]))
+        mm([(S(PS[1], 0, C + 1), blkb, S(Z2, 1, C + 2), True, False), (S(PS[1], 0, C + 1), blkb, S(Z1, 1, C + 2), False, True)])
+        scan(k1, S(K, 0, C), S(PS[1], 0, C), 0.0, OP.max, OP.min)
+        scan(k2, S(K, 0, C), S(PS[1], 1, C + 1), 0.0, OP.max, OP.min)
+        M0 = new("sf", 16)
+        tt(M0, ZZ[t], S(k1, 15, C, 16), OP.subtract)
+        tt(M, M0, S(k2, 15, C, 16), OP.add)
+        return M
+
+    def release(t, M, a, ne, f1, lo):
+        m = B("m1s%d" % t, 0, M1W)
+        a1, n1, sh, rel, b = S(m, 56, 72), S(m, 72, 88), S(m, 89, 105), S(m, 107, 123), S(m, 125, 141)
+        uv, r16, begm, rx = new("sf", 32), new("sh", 32), new("sf", 16), new("sf", 54)
+        act(begm, BEG[t], bias=-2048.0)
+        tt(a1, M, a, OP.min)
+        if t == 0:
+            tt(sh, M, a, OP.is_gt)
+            tt(b, M, a, OP.min)
+            tt(rel, a, a1, OP.subtract)
+            tt(S(r16, 0, 16), begm, a1, OP.add)
+            uv = rel
+        else:
+            f0 = new("sf", 16)
+            tt(f0, M, a, OP.is_gt)
+            tt(S(uv, 0, 16), a, a1, OP.subtract)
+            if f1 is not None:
+                f2 = new("sf", 16)
+                tt(f2, f0, f1, OP.add)
+                f0 = f2
+            tt(S(r16, 0, 16), begm, a1, OP.add)
+            tt(n1, ne, f0, OP.min)
+            tt(S(uv, 16, 32), ne, n1, OP.subtract)
+            tt(b, a1, n1, OP.add)
+            tt(S(r16, 16, 32), lo, n1, OP.add)
+            tt(rel, S(uv, 0, 16), S(uv, 16, 32), OP.add)
+        n = 16 if t == 0 else 32
+        e = new("sf", n)
+        ts(e, S(uv, 0, n), 0.5, OP.is_lt, 1.0e5, OP.mult)
+        for lo_, hi, bank in ((0, 54, 6),) if t == 0 else ((18, 54, 6), (0, 18, 3)):
+            scan(S(rx, lo_, hi), S(rm18, lo_, hi), S(m, 88 + lo_, 88 + hi), 0.0, OP.mult, OP.add)
+            o = S(PS[bank], lo_, hi - 1)
+            mm([(o, blk, S(rx, lo_, hi - 1), True, False), (o, tri, S(m, 89 + lo_, 88 + hi), False, True)])
+            if bank == 6:
+                offu = offsets(S(PS[6], 18, 34), S(uv, 0, 16), e, n)
+            cp(S(m, lo_, hi - 1), o)
+        spread(PS[7], S(r16, 0, n), n)
+        send("m1s%d" % t)
+        return m, offu, n
+
+    def offsets(st0, u, e, n):
+        key, off, offu = new("sf", n), new("sf", n), new("su", n)
+        tt(S(key, 0, 16), st0, S(e, 0, 16), OP.add)
+        if n == 32:
+            ue = new("sf", 16)
+            tt(ue, u, S(e, 16, 32), OP.add)
+            tt(S(key, 16, 32), st0, ue, OP.add)
+        tt(off, key, S(d2, 0, n), OP.min)
+        cp(offu, off)
+        return offu
+
+    def place(src, n, e=None):
+        vi, lo, hi, l2, s1, pos = new("si", n), new("si", n), new("si", n), new("sf", n), new("sf", n), new("su", n)
+        st = [lambda: cp(vi, src), lambda: ts(lo, vi, 15, OP.bitwise_and),
+              lambda: ts(hi, vi, 4, OP.logical_shift_right, 1023, OP.bitwise_and),
+              lambda: ts(l2, lo, 256.0, OP.mult), lambda: tt(s1, l2, hi, OP.add)]
+        if e is None:
+            st.append(lambda: cp(pos, s1))
+        else:
+            s2 = new("sf", n)
+            st += [lambda: tt(s2, s1, e, OP.max), lambda: ts(pos, s2, float(NEG), OP.min)]
+        return pos, st
+
+    pack, hA, hK, relh = new("sf", 2 * C), new("sf", NQ), new("sf", NQ), new("sh", NQ)
+    ltb, nxb = new("sb", 2 * C), new("sf", 2 * C)
+    H0 = B("h0", 0, DUMP + 2 * C)
+
+    def lookup(t, offu, n, between):
+        act(S(pack, 0, 16 * n), S(PS[7], 0, 16 * n))
+        tt(IND(H0, offu), S(pack, 0, 16 * n), S(spack, 0, 16 * n), OP.add)
+        scan(hA, ones, S(H0, 0, NQ), -1.0, OP.add, OP.max)
+        if t < 2:
+            act(S(H0, 0, NQ), B("mk0", 0, NQ), scale=0.0)
+        scan(hK, K, hA, 0.0, OP.max, OP.min)
+        pos, st = place(S(hK, 15, NQ, 16), NQ // 16)
+        for k in range(max(len(st), len(between))):
+            if k < len(st):
+                st[k]()
+            if k < len(between):
+                between[k]()
+        ts(relh, IND(WIN, pos), -SH, OP.max, row0, OP.mult)
+        mm(wrap(S(PS[7], 0, NQ // 16), zw, relh, NQ // 16))
+
+    def lookup2(t):
+        ts(B("m2s%d" % t, 0, NQ // 16), S(PS[7], 0, NQ // 16), SH, OP.add)
+        send("m2s%d" % t)
+
+    def cut(t):
+        ma, mb = B("m1a%d" % (t - 1), 0, M1W), B("m1b%d" % (t - 1), 0, M1W)
+        sr, Ss, R, Pb, a1, n1, sh = S(ma, 0, 16), S(ma, 16, 17), S(ma, 34, 35), S(ma, 36, 52), S(ma, 56, 72), S(ma, 72, 88), S(ma, 89, 105)
+        c = [new("sf", 1) for _ in range(5)]
+        w = [new("sf", 16) for _ in range(17)]
+        qu = new("su", 16)
+        ts(c[0], S(mb, 16, 17), S(mb, 34, 35), OP.subtract, -float(SLOT), OP.max)
+        ts(c[4], S(mb, 16, 17), R, OP.subtract, float(C), OP.add)
+        ts(w[0], Pb, -1.0, OP.mult, float(L), OP.add)
+        act(w[1], sr, bias=-float(C + NQ))
+        ts(c[2], c[0], 0.0, OP.min, R, OP.subtract)
+        ts(w[2], sr, R, OP.is_ge, c[4], OP.mult)
+        act(w[16], n1, scale=-1.0, bias=float(t - 1))
+        tt(w[3], w[0], sr, OP.subtract)
+        ts(w[4], sr, c[2], OP.add, -0.5, OP.is_lt)
+        tt(w[5], w[1], w[2], OP.add)
+        ts(w[6], w[0], c[2], OP.add, 0.0, OP.max)
+        tt(w[7], w[4], sh, OP.mult)
+        tt(w[8], w[6], w[3], OP.max)
+        tt(w[9], w[7], n1, OP.add)
+        an = new("sf", 32)
+        a, ne = S(an, 0, 16), S(an, 16, 32)
+        tt(a, a1, w[8], OP.min)
+        tt(w[10], w[8], a, OP.subtract)
+        tt(ne, w[9], w[10], OP.min)
+        tt(w[11], ne, n1, OP.is_gt)
+        tt(w[12], w[11], w[5], OP.mult)
+        ts(qu, w[12], float(C + NQ), OP.add)
+        return dict(an=an, a=a, ne=ne, qu=qu, lo=w[16], rp=w[8], Rn=c[2], S=Ss, tot=S(ma, 52, 53), a1=a1)
+
+    def arrive(t):
+        k = t - 1
+        ma, mb = "m2a%d" % k, "m2b%d" % k
+        h = new("sh", 16 + 32 + 32)
+        ts(S(h, 0, 16), B(ma, 0, 16), SH, OP.subtract)
+        ts(S(h, 16, 44), B(mb, 0, 28), SH, OP.subtract)
+        if k:
+            ts(S(h, 48, 48 + 16 * k), B(ma, 28, 28 + 16 * k), SH, OP.subtract)
+        spread(PS[4], S(h, 0, 16), 16)
+        spread(PS[5], S(h, 16, 44), 28)
+        if k:
+            spread(PS[0] if k == 2 else S(PS[4], C, 2 * C), S(h, 48, 48 + 16 * k), 16 * k)
+
+    def arrive2(t, qu):
+        k = t - 1
+        act(S(RW, 0, C), S(PS[4], 0, C))
+        act(S(RW, C, C + NQ), S(PS[5], 0, NQ))
+        if k:
+            act(B("win", 0, C * k), PS[0] if k == 2 else S(PS[4], C, 2 * C))
+        act(B("win", C * k, C * k + C), IND(RW, qu))
+
+    M = needed(0)
+    for q in range(4):
+        pick(B("rs", 512 * q, 512 * q + 512), S(onb, 0, 512), [[-1, 4], [-16, 8], [0, 16]], OP.is_equal, -4 * q, 1)
+    for q in range(8):
+        gather(1, 512 * q, 512 * q + 512)
+    fill(B("yb", L, L + C), 0)
+    fill(B("hf", L, L + C), 0)
+    for t in (1, 2):
+        cp(B("lo%d" % t, 0, 32), B("lf%d" % t, C + 48, C + 80))
+    for q in range(8):
+        gather(2, 512 * q, 512 * q + 512)
+    fill(B("win", NEG, NEG + 8), int(-1 - SH))
+    fill(S(AX, C + NQ, C + NQ + 8), 0)
+    fill(S(RW, C + NQ, C + NQ + 8), int(W - SH))
+    m, offu, n = release(0, M, LEN[0], None, None, None)
+    lookup(0, offu, n, [])
+    act(S(spack, C, 2 * C), cio, scale=32784.0, bias=16384.0)
+
+    for t in (1, 2):
+        k = t - 1
+        cp(IND(MK[t], BOFF[t]), zb)
+        lookup2(k)
+        if t == 1:
+            fill(MK[2], 1)
+        ts(B("sp%d" % t, 0, C), B("lu%d" % t, 0, C), SH, OP.subtract)
+        rows(t)
+        starts(t)
+        act(S(II[t], L, L + C), G[t], scale=-1.0)
+        sums(t, 0)
+        u = cut(t)
+        sums(t, 1)
+        a, ne = u["a"], u["ne"]
+        bm, t1, t2, t3, t4, offp = new("sf", 16), new("sf", 16), new("sf", 16), new("sf", 16), new("sf", 16), new("su", 16)
+        tt(bm, BEG[t], d1p, OP.subtract)
+        ts(t2, a, 0.5, OP.is_gt)
+        tt(t3, a, bm, OP.add)
+        sums(t, 2)
+        act(S(AX, 0, C), IND(AUD, B("m2a%d" % k, 0, 16)), scale=-1.0)
+        act(S(AX, C, C + NQ), IND(AUD, B("m2b%d" % k, 0, 28)), scale=-1.0)
+        tt(t1, t3, t2, OP.mult)
+        arrive(t)
+        tt(t4, t1, d1, OP.add)
+        nx, lt = nxb, ltb
+        if t == 2:
+            of, e1, o1, ou = new("sf", 16), new("sf", 16), new("sf", 16), new("su", 16)
+            cp(of, B("m2a1", 28, 44))
+            ts(e1, ne, 0.5, OP.is_lt, float(W), OP.mult)
+            cp(offp, t4)
+            tt(o1, of, e1, OP.max)
+            cp(ou, o1)
+            act(S(nx, 0, C), IND(AUD, ou), scale=-1.0)
+        else:
+            cp(offp, t4)
+            act(S(nx, 0, C), IND(AX, u["qu"]))
+        sums(t, 3)
+        if t == 2:
+            tt(S(nx, C, 2 * C), IND(AX, u["qu"]), S(nx, 0, C), OP.add)
+        tt(S(lt, C * k, C * t), IND(II[t], offp), S(nx, C * k, C * t), OP.is_lt)
+        f1 = None
+        if t == 2:
+            f1 = new("sf", 16)
+            s1, s2, s3, s4, offq = new("sf", 16), new("sf", 16), new("sf", 16), new("sf", 16), new("su", 16)
+            ts(s1, u["a1"], 0.5, OP.is_gt)
+            tt(s2, u["a1"], bm, OP.add)
+            tt(s3, s1, s2, OP.mult)
+            tt(s4, s3, d1, OP.add)
+            cp(offq, s4)
+            act(kb, IND(AUD, B("m2a1", 28, 44)), scale=-1.0)
+            tt(S(lt, 0, C), IND(II[t], offq), kb, OP.is_lt)
+            mm(wrap(S(PS[2], 0, 16), zwb, S(lt, 0, C), 16))
+            ts(f1, S(PS[2], 0, 16), 6.5, OP.is_ge)
+        mm(wrap(S(PS[3], 0, 16), zwb, S(lt, C * k, C * t), 16))
+        M = needed(t)
+        arrive2(t, u["qu"])
+        ts(B("m1s%d" % t, 89, 105), S(PS[3], 0, 16), 6.5, OP.is_ge)
+        if t == 2:
+            for q in range(8):
+                act(B("hf", 512 * q, 512 * q + 512), B("mk0", 512 * q, 512 * q + 512), scale=0.0)
+        eh = new("sh", C)
+        ts(eh, B("win", C * k, C * k + C), row0, OP.mult)
+        mm(wrap(S(PS[2], 0, 16), zw, eh, 16))
+        m, offu, n = release(t, M, a, ne, f1, u["lo"])
+        n1, ew = S(m, 72, 88), S(PS[2], 0, 16)
+        x = [new("sf", 16) for _ in range(6)]
+        if t == 1:
+            steps = [lambda: ts(x[0], ew, SH, OP.subtract), lambda: tt(x[1], x[0], n1, OP.mult),
+                     lambda: ts(B("m2s1", 28, 44), x[1], float(W), OP.add)]
+        else:
+            steps = [lambda: (ts(x[0], ew, SH, OP.add), tt(x[1], u["lo"], n1, OP.add)),
+                     lambda: (tt(x[2], of, x[0], OP.subtract), ts(x[3], x[1], 1.0, OP.is_equal)),
+                     lambda: (tt(x[4], x[2], x[3], OP.mult), cp(B("m2s2", 28, 44), of)),
+                     lambda: tt(x[5], x[4], x[0], OP.add), lambda: cp(B("m2s2", 44, 60), x[5])]
+        lookup(t, offu, n, steps)
+
+    r16, begm = new("sh", 32), new("sf", 16)
+    ts(S(r16, 0, 16), BEG[0], 2048.0, OP.subtract)
+    act(jv, jv0, scale=0.0625, bias=pm)
+    lookup2(2)
+    rows(0)
+    u = cut(3)
+    cp(S(r16, 16, 32), u["lo"])
+    spread(PS[7], r16, 32)
+    nb, e, c0, c1, ev, yh, yv = new("sf", 16), new("sf", 32), new("sf", 1), new("sf", 1), kb, new("sh", 16), new("sf", 16)
+    ts(nb, u["rp"], -1.0, OP.mult, float(L), OP.add)
+    ts(e, u["an"], 0.5, OP.is_lt, 1.0e5, OP.mult)
+    offu = offsets(nb, u["a"], e, 32)
+    HF = B("hf", 0, DUMP + 2 * C)
+    act(pack, PS[7])
+    ts(c0, u["Rn"], -1.0, OP.mult, u["S"], OP.min)
+    tt(yv, u["a"], u["ne"], OP.add)
+    tt(IND(HF, offu), pack, spack, OP.add)
+    tt(c1, c0, u["tot"], OP.add)
+    ts(yh, yv, 2048.0, OP.subtract)
+    spread(PS[3], yh, 16)
+    ts(c0, c1, 0.0625, OP.mult)
+    arrive(3)
+    yr = ke
+    act(yr, S(PS[3], 0, C), bias=2048.0)
+    dma("s", T.yn[:], S(yr, 0, C, 1, ROW))
+    for q in range(4):
+        lo = 1024 * q
+        scan(S(IB, lo, lo + 1024), onb, S(HF, lo, lo + 1024), -1.0 if q == 0 else S(IB, lo - 1, lo), OP.add, OP.max)
+    arrive2(3, u["qu"])
+    ts(ev, jv, c0, OP.is_ge, 8000.0, OP.mult)
+    pend = []
+    for q in range(5):
+        for j in range(4):
+            if q < 4:
+                i = 4 * q + j
+                scan(B("yb", C * i, C * i + C), S(K, 0, C), S(IB, i, L, 16), 0.0, OP.max, OP.min)
+            for f in pend[2 * j:2 * j + 2]:
+                f()
+        if q > 0:
+            lo = 1024 * (q - 1)
+            half = 1024 if q < 4 else 512
+            act(S(H0, lo, lo + half), IND(WIN, S(pos, 0, half // 16)), bias=SH)
+            if half < 1024:
+                ts(S(H0, lo + half, lo + 1024), IND(WIN, S(pos, half // 16, 64)), SH, OP.add)
+            for j in range(4):
+                i = 4 * (q - 1) + j
+                dma("s" if q < 4 or j >= 2 else "a", T.yo[i:128:16, :], S(H0, C * i, C * i + C, 1, ROW))
+        if q < 4:
+            pos, pend = place(B("yb", 1024 * q + 15, 1024 * q + 1024, 16), 64, S(ev, 64 * q, 64 * q + 64))
+
+    finish()

@@ -1,3 +1,4 @@
+import math
 import numpy as np
 from concourse.bass import DstId, RemoteDMATransfer
 from concourse.mybir import AluOpType as OP, ActivationFunctionType as AF
@@ -5,77 +6,238 @@ from concourse.mybir import AluOpType as OP, ActivationFunctionType as AF
 N, W, L, C, SLOT = 8, 3072, 4096, 256, 192
 NQ = C + SLOT
 SH = 1536.0
-EW = 3 * C
-NEG = EW + L
-DUMP = L + 2 * C
+NS = 5
+NEG = L + NS * C
+DUMP = L + C
+TAG = 8192
+BIG = 1.0e5
+QW = W // 4
 F32, BF, F16, I32, U16 = "float32", "bfloat16", "float16", "int32", "uint16"
-M1W, M1S = 144, 106
-M2S = (28, 44, 60)
-CY, GATH, SCAT, GAP, FLY = 0.83e-3 * 1.25, 1.56, 3.8, 0.15, 4.5
-PLAN, SEED, TRIES, MOVES = {}, 1, 600, 30000
+CY, GATH, SCAT, GAP, NEAR, FAR = 0.83e-3 * 1.1, 1.56, 3.8, 0.12, 2.5, 5.0
+PLAN, SEED, TRIES, MOVES = {}, 1, 40, 20000
+LEAD = {"set": 1.0, "sums0": 4.0, "visit1": 1.0, "visit2": 2.0}
+PIECE = [1024, 512, 512]
+ONV = [(4, 5, 6, 7), (5, 6, 7), ()]
 
 SCRATCH = {
-    "audb": ("sbuf", [128, W + 16], BF), "win": ("sbuf", [128, NEG + 8], F32), "yb": ("sbuf", [128, L + C], F32),
-    "ib": ("sbuf", [128, L + C], F32), "h0": ("sbuf", [128, DUMP + 2 * C], F32), "hf": ("sbuf", [128, DUMP + 2 * C], F32),
-    "mk0": ("sbuf", [128, L + C], BF), "mk1": ("sbuf", [128, L + C], BF), "mk2": ("sbuf", [128, L + C], BF),
-    "sg": ("sbuf", [128, L], BF), "rs": ("sbuf", [128, 2048], BF),
-    "sf": ("sbuf", [128, 12600], F32), "sb": ("sbuf", [128, 4400], BF), "sh": ("sbuf", [128, 2600], F16),
-    "si": ("sbuf", [128, 1700], I32), "su": ("sbuf", [128, 640], U16),
+    "win": ("sbuf", [128, NEG + 16], F32), "h0": ("sbuf", [128, DUMP + 2 * C], F32), "hf": ("sbuf", [128, DUMP + 2 * C], F32),
+    "mk": ("sbuf", [128, L + C], BF), "sg": ("sbuf", [128, L], BF), "rs": ("sbuf", [128, 2048], BF),
+    "sf": ("sbuf", [128, 12100], F32), "sb": ("sbuf", [128, 4400], BF), "sh": ("sbuf", [128, 1200], F16),
+    "si": ("sbuf", [128, 1100], I32), "su": ("sbuf", [128, 900], U16),
     "spi": ("sbuf", [128, C], I32), "gi": ("sbuf", [128, C], I32), "li": ("sbuf", [128, C], I32),
 }
 for _t in range(3):
-    SCRATCH["lu%d" % _t] = ("sbuf", [128, C], U16)
-    SCRATCH["lo%d" % _t] = ("sbuf", [128, 32], U16)
-    SCRATCH["lf%d" % _t] = ("sbuf", [128, C + 80], F32)
-    SCRATCH["lb%d" % _t] = ("sbuf", [128, C], BF)
-    SCRATCH["sp%d" % _t] = ("sbuf", [128, C], F32)
-    for _r in "sab":
-        SCRATCH["m1%s%d" % (_r, _t)] = ("sbuf", [128, M1W], F32)
-        SCRATCH["m2%s%d" % (_r, _t)] = ("sbuf", [128, 64], U16)
+    SCRATCH["aud%d" % _t] = ("sbuf", [128, W + 16], BF)
+    for _r in "si":
+        SCRATCH["c%s%d" % (_r, _t)] = ("sbuf", [128, 4], F32)
+        SCRATCH["r%s%d" % (_r, _t)] = ("sbuf", [128, 32], U16)
+for _t in range(2):
+    SCRATCH["y%d" % _t] = ("sbuf", [128, L + C], F32)
+    SCRATCH["ii%d" % _t] = ("sbuf", [128, L + C], F32)
 for _b in range(8):
     SCRATCH["ps%d" % _b] = ("psum", [128, 512], F32)
 
-POOLS = {"v": 44, "a": 20, "t": 16, "g": 10, "d": 30}
-ARR = ["lu1", "lu2", "lf1", "lf2", "lb1", "lb2"] + ["m%d%s%d" % (k, r, t) for t in range(3) for k in (1, 2) for r in "ab"]
-SEMAPHORES = ["%s%d" % (e, i) for e in POOLS for i in range(POOLS[e])] + ["r" + a for a in ARR] + ["sent"]
-
-
-def messages():
-    out = [("lu0", C, [("lu1", 1), ("lu2", 2)]), ("lf0", C + 80, [("lf1", 1), ("lf2", 2)]),
-           ("lb0", C, [("lb1", 1), ("lb2", 2)])]
-    for t in range(3):
-        a, b = (1, 2) if t < 2 else (-2, -1)
-        out.append(("m1s%d" % t, M1S, [("m1a%d" % t, a), ("m1b%d" % t, b)]))
-        out.append(("m2s%d" % t, M2S[t], [("m2a%d" % t, a), ("m2b%d" % t, b)]))
-    return out
-
-
-def hop(T, topo, r, k, step):
-    src, dst = T.cores[r], T.cores[(r + step) % N]
-    if topo.may_write(src, dst):
-        return dst, dst
-    rel = [c for c in topo.cores_of(src) if topo.die(c) == topo.die(src) and T.rank_of(c) is None and topo.may_write(c, dst)]
-    return rel[k % len(rel)], dst
+POOLS = {"v": 58, "a": 30, "t": 22, "g": 12, "d": 9}
+ARR = ["q0", "q1", "q2", "q3", "a2"] + ["%s%d" % (k, t) for t in range(3) for k in "cr"]
+SEMAPHORES = ["%s%d" % (e, i) for e in POOLS for i in range(POOLS[e])] + ["r" + a for a in ARR] + ["l%d" % k for k in range(7)] + ["sent"]
+COLS = {"c": 3, "r": NQ // 16}
 
 
 def bits(engs):
     return sum(1 << e for e in engs)
 
 
+def ports(T, topo, r):
+    src, far = T.cores[r], T.cores[(r - 2) % N]
+    return [c for c in topo.cores_of(src) if T.rank_of(c) is None and topo.may_write(c, far)]
+
+
+def direct(T, topo, r):
+    return topo.may_write(T.cores[r], T.cores[(r + 1) % N])
+
+
+def hop(T, topo, r, kind):
+    if direct(T, topo, r):
+        return T.cores[(r + 1) % N]
+    return [c for c in ports(T, topo, r) if topo.die(c) == topo.die(T.cores[r])]["cr".index(kind)]
+
+
+def transfer(T, topo, core, dst, engs, src, out, sem):
+    rid, pid = topo.addr(dst, core)
+    return RemoteDMATransfer(dst_ids=[DstId(rid=rid, pnc=pid)], dma_engine_mask=bits(engs), remote_sem=T.sem[sem], src=src, dst=out)
+
+
 def relay_program(g, core, T, topo):
     n = 0
-    for r in range(N):
-        for src, cols, dsts in messages():
-            for k, (buf, step) in enumerate(dsts):
-                first, dst = hop(T, topo, r, k, step)
-                if first == core and first != dst:
-                    g.wait_ge(T.sem["r" + buf], 8)
-                    rid, pid = topo.addr(dst, core)
-                    e = topo.engines(core, dst)[:8]
-                    g.remote_dma(T[buf][:, 0:cols], T[buf][:, 0:cols], T.sem["r" + buf], T.sem.sent, pid, rid, bits(e))
-                    n += len(e)
+    mine = [r for r in range(N) if core in ports(T, topo, r)]
+    for r in sorted(mine, key=lambda r: not direct(T, topo, r)):
+        j = ports(T, topo, r).index(core)
+        cs = slice(QW * j, QW * j + QW)
+        one, two = T.cores[(r - 1) % N], T.cores[(r - 2) % N]
+        off = topo.engines(core, two)
+        if direct(T, topo, r):
+            g.wait_ge(T.sem.rq0, 16)
+            tr = [transfer(T, topo, core, one, off, T.aud1[:, cs], T.aud1[:, cs], "rq%d" % j)]
+        else:
+            g.wait_ge(T.sem.ra2, 16)
+            on = [e for e in topo.engines(core, one) if e not in off]
+            tr = [transfer(T, topo, core, one, on, T.aud2[:, cs], T.aud1[:, cs], "rq%d" % j),
+                  transfer(T, topo, core, two, off, T.aud2[:, cs], T.aud2[:, cs], "ra2")]
+        g.remote_dma_fused(tr, local_sem=T.sem.sent)
+        n += 8 * len(tr)
+    for t in range(3):
+        for r in mine:
+            for k in "cr":
+                if hop(T, topo, r, k) == core:
+                    dst, b = T.cores[(r + 1) % N], T["%si%d" % (k, t)][:, 0:COLS[k]]
+                    g.wait_ge(T.sem["r%s%d" % (k, t)], 8)
+                    g.remote_dma_fused([transfer(T, topo, core, dst, topo.engines(core, dst), b, b, "r%s%d" % (k, t))], local_sem=T.sem.sent)
+                    n += 8
     if n:
         g.wait_ge(T.sem.sent, n)
+
+
+def schedule(both):
+    n0 = len(both[0][0])
+    ops = both[0][0] + both[1][0]
+    n = len(ops)
+    pre, qs = [], []
+    for i, o in enumerate(ops):
+        k = int(i >= n0)
+        p = {j + k * n0 for j in o["need"] | o["after"]}
+        p |= {both[kk][1][name] + kk * n0 for kk, name in o["link"]}
+        pre.append(sorted(p))
+        qs.append(5 * k + "vatgs".index(o["q"]) if o["q"] else 10)
+    hard = [[j for j in pre[i] if qs[j] != qs[i] or j - int(i >= n0) * n0 in ops[i]["need"]] for i in range(n)]
+    post = [[] for _ in ops]
+    for i in range(n):
+        for j in pre[i]:
+            post[j].append(i)
+    left = [len(p) for p in pre]
+    topo_ = [i for i in range(n) if not left[i]]
+    for i in topo_:
+        for j in post[i]:
+            left[j] -= 1
+            if not left[j]:
+                topo_.append(j)
+    at = {i: k for k, i in enumerate(topo_)}
+    rank_ = [0.0] * n
+    for i in reversed(topo_):
+        rank_[i] += ops[i]["busy"] + ops[i]["lat"] + GAP
+        for j in pre[i]:
+            rank_[j] = max(rank_[j], rank_[i])
+
+    def plan(prio, back=False):
+        start, end, slots = [0.0] * n, [0.0] * n, [[] for _ in range(10)]
+        up, down = (post, pre) if back else (pre, post)
+        left = [len(p) for p in up]
+        ready = [i for i in range(n) if not left[i]]
+        while ready:
+            i = max(ready, key=lambda i: prio[i])
+            ready.remove(i)
+            o = ops[i]
+            t = max([end[j] + (GAP if (i in hard[j] if back else j in hard[i]) else 0.0) for j in up[i]] + [0.0])
+            t += o["lat"] if back else 0.0
+            if qs[i] < 10:
+                sl = slots[qs[i]]
+                k = 0
+                for a, b in sl:
+                    if b > t:
+                        if t + o["busy"] <= a:
+                            break
+                        t = b
+                    k += 1
+                sl.insert(k, (t, t + o["busy"]))
+            start[i], end[i] = t, t + o["busy"] + (0.0 if back else o["lat"])
+            for j in down[i]:
+                left[j] -= 1
+                if not left[j]:
+                    ready.append(j)
+        return end, sorted(range(n), key=lambda i: (start[i], at[i]))
+
+    sets = ((0.93, 0.93, 1.0, 1.0, 0.1), (1.2, 1.4, 1.2, 1.4, 0.16))
+    busy = [[o["busy"] * (s[1] if o["ind"] else s[0]) for o in ops] for s in sets]
+    lat = [[o["lat"] * (s[3] if o["lat"] > FAR and not o["q"] else s[2]) + s[4] for o in ops] for s in sets]
+
+    def run(order, s):
+        end, free, bs, ls = [0.0] * n, [0.0] * 11, busy[s], lat[s]
+        for i in order:
+            q = qs[i]
+            t = free[q]
+            for j in hard[i]:
+                if end[j] > t:
+                    t = end[j]
+            t += bs[i]
+            if q < 10:
+                free[q] = t
+            end[i] = t + ls[i]
+        return end
+
+    def span(order):
+        ends = [run(order, s) for s in range(len(sets))]
+        return sum(max(e) + 0.02 * sum(e) / n for e in ends), ends
+
+    def held(order, end, s):
+        before, last = {}, {}
+        for i in order:
+            before[i] = last.get(qs[i])
+            last[qs[i]] = i
+        i, out = max(range(n), key=lambda i: end[i]), []
+        while True:
+            t = end[i] - lat[s][i] - busy[s][i]
+            p = [j for j in hard[i] if end[j] >= t - 1e-9]
+            if p:
+                i = p[0]
+            elif qs[i] < 10 and before[i] is not None and t > 1e-9:
+                out.append((before[i], i))
+                i = before[i]
+            else:
+                return out
+
+    rng = np.random.default_rng(SEED)
+    best, p = None, [rank_[i] + LEAD.get(ops[i]["part"], 0.0) for i in range(n)]
+    for it in range(TRIES):
+        end, cand = plan(p)
+        v, ends = span(cand)
+        if best is None or v < best:
+            best, order, ee = v, cand, ends
+        p = [x + float(y) for x, y in zip(plan(end, True)[0], rng.normal(0, 0.3, n))]
+    cur, top, keep = best, best, order
+    pairs, dice, far, slack = None, rng.random((MOVES, 2)).tolist(), rng.geometric(0.4, MOVES).tolist(), rng.exponential(1.0, MOVES).tolist()
+    for it in range(MOVES):
+        if pairs is None:
+            pairs = [x for s in range(len(sets)) for x in held(order, ee[s], s)]
+        u, v = pairs[int(dice[it][0] * len(pairs))]
+        a, b = order.index(u), order.index(v)
+        if dice[it][1] < 0.5:
+            same = [k for k in range(max(0, a - 150), a + 1) if qs[order[k]] == qs[v]]
+            a = same[max(0, len(same) - far[it])]
+            seg, take = order[a:b + 1], {v}
+            for i in reversed(seg):
+                if i in take:
+                    take.update(pre[i])
+            if seg[0] in take:
+                continue
+            seg = [i for i in seg if i in take] + [i for i in seg if i not in take]
+        else:
+            same = [k for k in range(b, min(n, b + 150)) if qs[order[k]] == qs[v]]
+            b = same[min(len(same), far[it]) - 1]
+            seg, take = order[a:b + 1], {u}
+            for i in seg:
+                if i in take:
+                    take.update(post[i])
+            if seg[-1] in take:
+                continue
+            seg = [i for i in seg if i not in take] + [i for i in seg if i in take]
+        cand = order[:a] + seg + order[b + 1:]
+        val, ends = span(cand)
+        if val <= cur + 0.2 * (1.0 - it / MOVES) * slack[it]:
+            cur, ee, pairs = val, ends, None
+            order = sorted(cand, key=lambda i: ends[0][i] - lat[0][i] - busy[0][i])
+            if cur < top:
+                top, keep = cur, order
+    PLAN["us"] = [max(e) for e in span(keep)[1]]
+    return [[i for i in keep if i < n0], [i - n0 for i in keep if i >= n0]]
 
 
 def rank_program(g, core, T, topo):
@@ -83,17 +245,71 @@ def rank_program(g, core, T, topo):
     if rank is None:
         relay_program(g, core, T, topo)
         return
+    if "order" not in PLAN:
+        kinds = [[r for r in range(N) if direct(T, topo, r) == d][0] for d in (True, False)]
+        PLAN["order"] = schedule([record(g, T, topo, r) for r in kinds])
+    ops, names, sent = record(g, T, topo, rank)
+    order = PLAN["order"][0 if direct(T, topo, rank) else 1]
     Q = {"v": g.vector, "a": g.scalar, "t": g.tensor, "g": g, "s": g.sync}
-    ops, acc, known = [], {}, {q: set() for q in Q}
-    last = {}
-    waited = {}
+    known, last, waited, done = {q: set() for q in Q}, {}, {}, {}
+    pos_ = {i: k for k, i in enumerate(order)}
+
+    def wait(q, i):
+        if i in known[q] or ops[i]["pool"] == "-":
+            return
+        sem, val, snap = done[i]
+        Q[q].wait_ge(T.sem[sem], val)
+        waited[sem] = max(waited.get(sem, 0), val)
+        known[q].add(i)
+        known[q].update(snap)
+
+    for i in order:
+        o = ops[i]
+        q, pool = o["q"], o["pool"]
+        if q is None:
+            done[i] = (pool, o["inc"], frozenset())
+            last[pool] = [o["inc"], i]
+            continue
+        for j in sorted(o["need"], key=lambda j: -pos_[j]):
+            wait(q, j)
+        if pool == "-":
+            o["emit"]()
+            continue
+        pn = ["%s%d" % (pool, k) for k in range(POOLS[pool])]
+        free = [s for s in pn if s not in last or last[s][1] in known[q]]
+        if not free:
+            free = [min(pn, key=lambda s: pos_[last[s][1]])]
+            wait(q, last[free[0]][1])
+        s = free[0]
+        val = last[s][0] if s in last else 0
+        for ins in o["emit"]():
+            ins.then_inc(T.sem[s], o["inc"])
+            val += o["inc"]
+        last[s] = [val, i]
+        done[i] = (s, val, frozenset(known[q]))
+    g.wait_ge(T.sem.sent, sent[0])
+    for s in sorted(last, key=lambda s: pos_[last[s][1]]):
+        if waited.get(s, 0) < last[s][0]:
+            wait("g", last[s][1])
+
+
+def record(g, T, topo, rank):
+    core = T.cores[rank]
+    near = direct(T, topo, rank)
+    me = 0 if near else 1
+    Q = {"v": g.vector, "a": g.scalar, "t": g.tensor, "g": g, "s": g.sync}
+    ops, acc, bank, names, sent, chain, part = [], {}, {}, {}, [0], {}, ["set"]
     top = {"sf": 0, "sb": 0, "sh": 0, "si": 0, "su": 0}
 
     def new(buf, n):
+        u = 8 if buf in ("sf", "si") else 16
         c = top[buf]
-        top[buf] = c + (n + 15) // 16 * 16
+        top[buf] = c + (n + u - 1) // u * u
         assert top[buf] <= SCRATCH[buf][1][1], buf
         return (buf, c, c + n, 1, None)
+
+    def f(n=16):
+        return new("sf", n)
 
     def B(name, a, b, step=1, p=None):
         return (name, a, b, step, p)
@@ -114,26 +330,44 @@ def rank_program(g, core, T, topo):
         cs = slice(x[1], x[2]) if x[3] == 1 else slice(x[1], x[2], x[3])
         return T[x[0]][ps, cs]
 
-    def op(q, rd, wr, emit, busy, lat=0.0, pool=None, inc=1, after=()):
+    def op(q, rd, wr, emit, busy, lat=0.0, pool=None, inc=1, after=(), link=(), line=None, group=False):
         tt_ = []
         for x, w in [(x, False) for x in rd] + [(x, True) for x in wr]:
             if not isinstance(x, tuple):
                 continue
             if x[0] == "ind":
-                tt_ += [(x[1], w), (x[2], False)]
+                tt_ += [(x[1], w, False), (x[2], False, False)]
             else:
-                tt_.append((x, w))
-        reg = [((x[0], 0, 512, True) if x[0].startswith("ps") else (x[0], x[1], x[2], w)) for x, w in tt_]
-        need = set()
-        for b, c0, c1, w in reg:
-            for d0, d1, i, v in acc.get(b, []):
-                if (w or v) and d0 < c1 and c0 < d1:
-                    need.add(i)
+                tt_.append((x, w, w and x[3] == 1 and x[4] is None))
+        reg = [(x[0], x[1], x[2], x[3], w, all_) for x, w, all_ in tt_]
+        need, after = set(), set(after)
+        for b, c0, c1, st, w, all_ in reg:
+            for d0, d1, sd, i, v in acc.get(b, []):
+                if (w or v) and d0 < c1 and c0 < d1 and (c0 - d0) % math.gcd(st, sd) == 0:
+                    if q == "t" and ops[i]["q"] == "t" and group:
+                        after.add(i)
+                    else:
+                        need.add(i)
         i = len(ops)
+        for b in {r[0] for r in reg if r[0].startswith("ps")}:
+            eng, cur, old = bank.get(b, (q, [], []))
+            if eng != q:
+                eng, cur, old = q, [], cur
+            need.update(old)
+            if q == "t":
+                after.update(cur[-1:])
+            bank[b] = (eng, cur + [i], old)
+        if line:
+            after.update(chain.get(line, []))
+            chain[line] = [i]
         ind = any(isinstance(x, tuple) and x[0] == "ind" for x in list(rd) + list(wr))
-        ops.append(dict(q=q, w=reg[-1][:2], ind=ind, need=need, after=set(after), emit=emit, busy=busy, lat=lat, pool=pool or q, inc=inc))
-        for b, c0, c1, w in reg:
-            acc.setdefault(b, []).append((c0, c1, i, w))
+        ops.append(dict(q=q, ind=ind, need=need, after=after, link=list(link), emit=emit, busy=busy, lat=lat, pool=pool or q, inc=inc,
+                        part=part[0]))
+        for b, c0, c1, st, w, all_ in reg:
+            if all_:
+                acc[b] = [e for e in acc.get(b, []) if not (c0 <= e[0] and e[1] <= c1)]
+        for b, c0, c1, st, w, all_ in reg:
+            acc.setdefault(b, []).append((c0, c1, st, i, w))
         return i
 
     def wd(x):
@@ -151,31 +385,38 @@ def rank_program(g, core, T, topo):
             per = 0.5 if all(two(x) for x in [o] + ins) else 1.0
         return max(64, wd(o) * per) * CY
 
-    def cp(o, a):
-        op("v", [a], [o], lambda: [g.vector.tensor_copy(ap(o), ap(a))], cost(o, [a]))
+    def cp(o, a, line=None):
+        op("v", [a], [o], lambda: [g.vector.tensor_copy(ap(o), ap(a))], cost(o, [a]), line=line)
+        return o
 
-    def tt(o, a, b, f):
-        op("v", [a, b], [o], lambda: [g.vector.tensor_tensor(ap(o), ap(a), ap(b), f)], cost(o, [a, b], 1 if a[0][:2] == "ps" else 2))
+    def tt(o, a, b, fn):
+        op("v", [a, b], [o], lambda: [g.vector.tensor_tensor(ap(o), ap(a), ap(b), fn)], cost(o, [a, b], 1 if a[0][:2] == "ps" else 2))
+        return o
 
     def ts(o, a, s1, f1, s2=None, f2=None):
         if f2 is None:
             op("v", [a, s1], [o], lambda: [g.vector.tensor_scalar(ap(o), ap(a), ap(s1), None, f1)], cost(o, [a]))
         else:
             op("v", [a, s1, s2], [o], lambda: [g.vector.tensor_scalar(ap(o), ap(a), ap(s1), ap(s2), f1, f2)], cost(o, [a]))
+        return o
 
     def scan(o, d0, d1, init, f0, f1):
         op("v", [d0, d1, init], [o], lambda: [g.vector.tensor_tensor_scan(ap(o), ap(d0), ap(d1), ap(init), f0, f1)], cost(o, [d0, d1]))
+        return o
 
     def ms(o, c):
         op("v", [], [o], lambda: [g.vector.memset(ap(o), c)], cost(o, []))
+        return o
 
-    def act(o, a, f=AF.Identity, bias=0.0, scale=1.0):
-        op("a", [a, bias], [o], lambda: [g.scalar.activation(ap(o), ap(a), f, bias=ap(bias), scale=scale)], 0.05 + cost(o, [a], 1))
+    def act(o, a, fn=AF.Identity, bias=0.0, scale=1.0, line=None):
+        op("a", [a, bias], [o], lambda: [g.scalar.activation(ap(o), ap(a), fn, bias=ap(bias), scale=scale)], 0.05 + cost(o, [a], 1),
+           line=line)
+        return o
 
     def mm(items):
         op("t", [x for m in items for x in m[1:3]], [m[0] for m in items],
            lambda: [g.tensor.matmul(ap(o), ap(l), ap(r), a, z) for o, l, r, a, z in items],
-           sum(max(64, wd(m[2])) * (1 if two(m[2]) else 4) * CY for m in items))
+           sum(max(64, wd(m[2])) * (1 if two(m[2]) else 4) * CY for m in items), group=not items[0][3])
 
     def iota(o, pat, base, cm):
         if o[0] == "si":
@@ -183,636 +424,387 @@ def rank_program(g, core, T, topo):
         else:
             op("g", [], [o], lambda: [g.iota(ap(o), pat, base, cm, allow_small_or_imprecise_dtypes=True)], 0.13 + 2 * wd(o) * CY)
 
-    def pick(o, a, pat, f, base, cm):
-        op("g", [a], [o], lambda: [g.affine_select(ap(o), ap(a), pat, f, 0.0, base, cm)], 0.17 + 2 * wd(o) * CY)
+    def pick(o, a, pat, fn, base, cm):
+        op("g", [a], [o], lambda: [g.affine_select(ap(o), ap(a), pat, fn, 0.0, base, cm)], 0.17 + 2 * wd(o) * CY)
 
-    def fill(o, c, step=544):
+    def fill(o, c, step=256):
         for lo in range(0, wd(o), step):
             hi = min(wd(o), lo + step)
             iota(S(o, lo, hi), [[0, hi - lo]], c, 0)
 
-    def dma(q, o, a, us=2.1):
-        op(q, [a], [o], lambda: [Q[q].dma_start(ap(o), ap(a))], 0.1, us, pool="d", inc=16)
+    def dma(q, pairs, us=2.1, line=None, after=()):
+        op(q, [a for o, a in pairs], [o for o, a in pairs], lambda: [Q[q].dma_start(ap(o), ap(a)) for o, a in pairs],
+           0.08 * len(pairs), us, pool="d", inc=16, line=line, after=after)
 
-    msgs = {m[0]: m for m in messages()}
-    sent, sends = [0], []
-
-    def send(name):
-        src, cols, dsts = msgs[name]
-
+    def send(name, src, dst, engs, out, sem, line):
         def emit():
-            tr = []
-            for k, (buf, step) in enumerate(dsts):
-                first, dst = hop(T, topo, rank, k, step)
-                rid, pid = topo.addr(first, core)
-                e = topo.engines(core, first)[8 * k:8 * k + 8]
-                tr.append(RemoteDMATransfer(dst_ids=[DstId(rid=rid, pnc=pid)], dma_engine_mask=bits(e), remote_sem=T.sem["r" + buf],
-                                            src=T[src][:, 0:cols], dst=T[buf][:, 0:cols]))
-                sent[0] += len(e)
-            g.remote_dma_fused(tr, local_sem=T.sem.sent)
-            return []
-        i = op("g", [B(src, 0, cols)], [], emit, 0.5, after=sends[-1:], pool="-")
-        sends.append(i)
-        for buf, step in dsts:
-            op(None, [], [B(buf, 0, 512)], None, 0.0, FLY + cols * (2 if two((src,)) else 4) * 0.004, pool="r" + buf, after=[i])
+            g.remote_dma_fused([transfer(T, topo, core, dst, engs, ap(src), ap(out), sem)], local_sem=T.sem.sent)
+            sent[0] += len(engs)
+        names[name] = op("g", [src], [], emit, 0.35, pool="-", line=line)
 
-    def finish():
-        n = len(ops)
-        pre = [o["need"] | o["after"] for o in ops]
-        rank_ = [0.0] * n
-        for i in range(n - 1, -1, -1):
-            rank_[i] += ops[i]["busy"] + ops[i]["lat"] + GAP
-            for j in pre[i]:
-                rank_[j] = max(rank_[j], rank_[i])
-        post = [[] for _ in ops]
-        for i in range(n):
-            for j in pre[i]:
-                post[j].append(i)
+    def lands(buf, sem, count, us, link):
+        op(None, [], [buf], None, 0.0, us, pool=sem, inc=count, link=link)
 
-        def plan(prio, back=False):
-            start, end, slots = [0.0] * n, [0.0] * n, {q: [] for q in Q}
-            up, down = (post, pre) if back else (pre, post)
-            left = [len(p) for p in up]
-            ready = [i for i in range(n) if not left[i]]
-            while ready:
-                i = max(ready, key=lambda i: prio[i])
-                ready.remove(i)
-                o = ops[i]
-                t = max([end[j] + GAP for j in up[i]] + [0.0]) + (o["lat"] if back else 0.0)
-                if o["q"]:
-                    sl = slots[o["q"]]
-                    k = 0
-                    for a, b in sl:
-                        if b > t:
-                            if t + o["busy"] <= a:
-                                break
-                            t = b
-                        k += 1
-                    sl.insert(k, (t, t + o["busy"]))
-                start[i], end[i] = t, t + o["busy"] + (0.0 if back else o["lat"])
-                for j in down[i]:
-                    left[j] -= 1
-                    if not left[j]:
-                        ready.append(j)
-            return end, sorted(range(n), key=lambda i: (start[i] if i > 1 else -1.0, i))
-
-        def span(order, fi, fl, gap):
-            end, free = [0.0] * n, {q: 0.0 for q in Q}
-            for i in order:
-                o = ops[i]
-                t = max([end[j] + gap for j in pre[i]] + [free.get(o["q"], 0.0)])
-                b = o["busy"] * (fi if o["ind"] else 1.0)
-                if o["q"]:
-                    free[o["q"]] = t + b
-                end[i] = t + b + o["lat"] * (fl if o["q"] is None else 1.0)
-            return max(end)
-
-        if "order" not in PLAN:
-            rng = np.random.default_rng(SEED)
-            best, prio = None, list(rank_)
-            PLAN["dbg"] = (ops, pre, rank_)
-            for it in range(TRIES):
-                e = rng.normal(0, 1.0, n) * (rng.random(n) < 0.05) * (it > 0)
-                if it % 2:
-                    k = int(rng.integers(0, n))
-                    e = np.zeros(n)
-                    e[k:k + int(rng.integers(2, 40))] = rng.normal(0, 3.0)
-                p = [x + float(y) for x, y in zip(prio, e)]
-                for rep in range(2):
-                    end, order = plan(p)
-                    v = sum(span(order, *s) for s in ((1, 1, GAP), (0.75, 0.8, 0.1), (1.3, 1.4, 0.25)))
-                    if best is None or v <= best:
-                        best, prio, PLAN["order"], PLAN["us"] = v, p, order, v / 3
-                    if rep == 0:
-                        p = plan(end, True)[0]
-            rows_ = [(list(pre[i]), "vatgs".find(o["q"] or "-"), [o["busy"] * (f if o["ind"] else 1.0) for f in (1, 0.75, 1.3)],
-                      [o["lat"] * (f if o["q"] is None else 1.0) for f in (1, 0.8, 1.4)]) for i, o in enumerate(ops)]
-
-            def span3(order):
-                tot = 0.0
-                for s, gap in enumerate((GAP, 0.1, 0.25)):
-                    end, free = [0.0] * n, [0.0] * 6
-                    for i in order:
-                        p, q, b, l = rows_[i]
-                        t = free[q]
-                        for j in p:
-                            if end[j] > t:
-                                t = end[j]
-                        t += b[s]
-                        if q >= 0:
-                            free[q] = t
-                        end[i] = t + l[s] + gap
-                    tot += max(end) + 0.01 * sum(end) / n
-                return tot
-            order = PLAN["order"]
-            best = span3(order)
-            for it in range(MOVES):
-                k = int(rng.integers(2, n))
-                i = order[k]
-                lo, hi = k, k
-                while lo > 2 and order[lo - 1] not in pre[i] and k - lo < 60:
-                    lo -= 1
-                while hi < n - 1 and i not in pre[order[hi + 1]] and hi - k < 60:
-                    hi += 1
-                same = [m for m in range(lo, hi + 1) if m != k and rows_[order[m]][1] == rows_[i][1]]
-                if not same:
-                    continue
-                m = same[int(rng.integers(0, len(same)))]
-                cand = order[:k] + order[k + 1:]
-                cand.insert(m, i)
-                v = span3(cand)
-                if v <= best:
-                    best, order = v, cand
-            PLAN["order"], PLAN["us"] = order, best / 3
-        order = PLAN["order"]
-        done = {}
-        pos_ = {i: k for k, i in enumerate(order)}
-
-        def wait(q, i):
-            if i in known[q] or ops[i]["pool"] == "-":
-                return
-            sem, val, snap = done[i]
-            Q[q].wait_ge(T.sem[sem], val)
-            waited[sem] = max(waited.get(sem, 0), val)
-            known[q].add(i)
-            known[q].update(snap)
-
-        for i in order:
-            o = ops[i]
-            q, pool = o["q"], o["pool"]
-            if q is None:
-                done[i] = (pool, 8, frozenset())
-                last[pool] = [8, i]
-                continue
-            for j in sorted(o["need"], key=lambda j: -pos_[j]):
-                wait(q, j)
-            if pool == "-":
-                o["emit"]()
-                continue
-            names = ["%s%d" % (pool, k) for k in range(POOLS[pool])]
-            free = [s for s in names if s not in last or last[s][1] in known[q]]
-            if not free:
-                free = [min(names, key=lambda s: pos_[last[s][1]])]
-                wait(q, last[free[0]][1])
-            s = free[0]
-            val = last[s][0] if s in last else 0
-            for ins in o["emit"]():
-                ins.then_inc(T.sem[s], o["inc"])
-                val += o["inc"]
-            last[s] = [val, i]
-            done[i] = (s, val, frozenset(known[q]))
-        g.wait_ge(T.sem.sent, sent[0])
-        for s in sorted(last, key=lambda s: pos_[last[s][1]]):
-            if waited.get(s, 0) < last[s][0]:
-                wait("g", last[s][1])
+    def tell(k, t):
+        first = hop(T, topo, rank, k)
+        e = topo.engines(core, first)
+        send("%s%d" % (k, t), B("%ss%d" % (k, t), 0, COLS[k]), first, e if near else e[:8], B("%si%d" % (k, t), 0, COLS[k]),
+             "r%s%d" % (k, t), k)
+        lands(B("%si%d" % (k, t), 0, 32), "r%s%d" % (k, t), 8 if near else 16, FAR if near else NEAR,
+              [(1 - me, "%s%d" % (k, t)), (0, "q3"), (1, "q3")])
 
     PS = [B("ps%d" % b, 0, 512) for b in range(8)]
-    AUD = B("audb", 0, W + 8)
+    AUD = [B("aud%d" % t, 0, W + 8) for t in range(3)]
     ROW = (0, 128, 16)
+    P8 = (0, 8, 1)
 
-    def wrap(o, z, src, n, first=True, final=True):
-        return [(o, S(z, 15 - i, 143 - i), S(src, i, 16 * n, 16), first and i == 0, final and i == 15) for i in range(16)]
-
-    def spread(bank, src, n):
-        mm([(S(bank, i, 16 * n, 16), B("rs", 128 * i, 128 * i + 128), src, True, True) for i in range(16)])
-
-    dma("s", B("li", 0, C, 1, (0, 8, 1)), T.lens[:])
-    dma("a", B("spi", 0, C), T.spots[:])
-    dma("s", B("audb", 0, W // 2), T.aud[:, 0:W // 2], 4.0)
-    dma("a", B("audb", W // 2, W), T.aud[:, W // 2:W], 4.0)
-    dma("s", B("gi", 0, C), T.gua[:], 2.7)
+    loads = [(B("li", 0, C, 1, P8), T.lens[:], 2.1), (B("spi", 0, C), T.spots[:], 2.5)]
+    loads += [(B("aud0", QW * j, QW * j + QW), T.aud[:, QW * j:QW * j + QW], 3.2 + 0.9 * j) for j in range(4)]
+    loads += [(B("gi", 0, C), T.gua[:], 6.2)]
+    for k, (o, a, us) in enumerate(loads):
+        q = "sa"[k % 2]
+        op(q, [], [], (lambda q, o, a, k: lambda: Q[q].dma_start(ap(o), a).then_inc(T.sem["l%d" % k], 16))(q, o, a, k), 0.08,
+           pool="-", line="load")
+        names["l%d" % k] = len(ops) - 1
+        lands(o, "l%d" % k, 16, us, [(me, "l%d" % k)])
+    for j, c in enumerate(ports(T, topo, rank)):
+        send("q%d" % j, B("aud0", QW * j, QW * j + QW), c, topo.engines(core, c), B("aud1" if near else "aud2", QW * j, QW * j + QW),
+             "rq0" if near else "ra2", "q")
+    for j in range(4):
+        lands(B("aud1", QW * j, QW * j + QW), "rq%d" % j, 8, 9.0 if near else 10.0, [(0, "q%d" % j), (1, "q%d" % j)])
+    if not near:
+        mate = T.cores[(rank - 1) % N]
+        for j in range(4):
+            send("f%d" % j, B("aud1", QW * j, QW * j + QW), mate, topo.engines(core, mate)[8:], B("aud2", QW * j, QW * j + QW), "ra2", "q")
+    lands(B("aud2", 0, W), "ra2", 32, 8.0 if near else 13.0, [(1, "f3")] if near else [(0, "q3"), (1, "q3")])
 
     pi_, pmi = new("si", 1), new("si", 1)
-    pf, pm, pg, row0 = new("sf", 1), new("sf", 1), new("sf", 1), new("sf", 1)
-    selv, sel = new("sf", 128), new("sf", 128)
-    cmod, K = new("sf", NQ), new("sf", NQ)
-    xs, m16 = new("sf", 144), new("sf", 128)
-    s16, cio, jv0, jv = new("sf", 32), new("sf", C), new("sf", C), new("sf", C)
-    P8 = (0, 8, 1)
+    pf, pm, npm, pg, row0 = f(1), f(1), f(1), f(1), f(1)
+    selv, sel, cmod, K, xs, s16, jv = f(128), f(128), f(NQ), f(NQ), f(144), f(32), f(C)
+    spack = f(2 * C)
+    tag0 = f(C)
     iota(pi_, [[0, 1]], 0, 1)
     iota(S(selv, 0, 128, 1, P8), [[-1, 8], [0, 16]], 0, 1)
     iota(cmod, [[0, NQ // 16], [1, 16]], 0, 0)
     iota(s16, [[16, 32]], 0, 0)
     iota(xs, [[1, 144]], -15, 0)
-    iota(cio, [[1, C]], 0, 0)
-    iota(jv0, [[1, 16], [256, 16]], 0, 0)
-
-    ones, lf_, ef = new("sf", NQ), new("sf", C + 1), new("sf", C + 1)
+    lf_, ef = f(C + 1), f(C + 1)
     zb, onb = new("sb", C), new("sb", 1024)
+    MK = B("mk", 0, L + C)
+    ms(onb, 1.0)
     for q in range(4):
-        ms(B("mk0", 1088 * q, 1088 * q + 1088), 1.0)
-    ms(ones, 1.0)
+        ms(B("mk", 1088 * q, 1088 * q + 1088), 1.0)
     ms(S(lf_, 0, 1), 0.0)
     ts(pmi, pi_, 15, OP.bitwise_and)
     cp(pf, pi_)
     ms(zb, 0.0)
     cp(pm, pmi)
-    ts(S(sel, 0, 128, 1, P8), S(selv, 0, 128, 1, P8), 0.0, OP.is_equal)
-    cp(S(lf_, 1, C + 1, 1, P8), B("li", 0, C, 1, P8))
-    ts(K, cmod, pm, OP.is_equal, 2.0e7, OP.mult)
-    scan(S(ef, 0, C + 1, 1, P8), S(ones, 0, C + 1, 1, P8), S(lf_, 0, C + 1, 1, P8), 0.0, OP.mult, OP.add)
-    mm([(S(PS[1], 0, C + 1), S(sel, 0, 128, 1, P8), S(ef, 0, C + 1, 1, P8), True, True)])
-    cp(B("lu0", 0, C), B("spi", 0, C))
+    ts(npm, pm, -1.0, OP.mult)
     tt(pg, pf, pm, OP.subtract)
-    d1, d2 = new("sf", 16), new("sf", 32)
-    ts(d1, S(s16, 0, 16), pm, OP.add, float(L), OP.add)
-    d1p = new("sf", 16)
-    act(d1p, d1, bias=1.0)
-    ts(d2, s16, pm, OP.add, float(DUMP), OP.add)
-    ms(B("audb", W, W + 16), 0.0)
-    ms(B("win", L, L + C), 0.0)
-    fill(B("win", L + C, NEG), 0)
-    cp(B("lf0", 0, C), B("gi", 0, C))
-    zwb = new("sb", 144)
-    ts(zwb, xs, pg, OP.is_equal)
-    kb, ke, endw, e0, key0 = new("sf", C), new("sf", C), new("sf", 16), new("sf", 16), new("sf", 16)
-    BEG = [B("lf%d" % t, C, C + 16) for t in range(3)]
-    LEN = [B("lf%d" % t, C + 16, C + 32) for t in range(3)]
-    ZZ = [B("lf%d" % t, C + 32, C + 48) for t in range(3)]
-    G = [B("lf%d" % t, 0, C) for t in range(3)]
-    BOFF = [B("lo%d" % t, 0, 16) for t in range(3)]
-    KEND = [B("lo%d" % t, 16, 32) for t in range(3)]
-    sgz = new("sb", C)
-    act(sgz, G[0], AF.Sign, bias=-0.5)
-    scan(kb, S(K, 0, C), S(PS[1], 0, C), 0.0, OP.max, OP.min)
-    scan(ke, S(K, 0, C), S(PS[1], 1, C + 1), 0.0, OP.max, OP.min)
-    mm(wrap(S(PS[2], 0, 16), zwb, sgz, 16))
-    eqi, eqj, ei, ej = new("si", C), new("si", C), new("si", 16), new("si", 16)
-    send("lu0")
-    endw = B("lf0", C + 48, C + 64)
-    cp(BEG[0], S(kb, 15, C, 16))
-    tt(LEN[0], S(ke, 15, C, 16), S(kb, 15, C, 16), OP.subtract)
-    cp(ei, S(ke, 15, C, 16))
-    ts(e0, LEN[0], 0.5, OP.is_lt, 1.0e5, OP.mult)
-    ts(ej, ei, 4, OP.logical_shift_right)
-    tt(key0, S(kb, 15, C, 16), e0, OP.add)
-    cp(KEND[0], ej)
-    cp(B("lf0", C + 64, C + 80), ej)
-    tt(endw, key0, d1, OP.min)
-    ts(ZZ[0], S(PS[2], 0, 16), -2.5, OP.is_ge)
-    cp(BOFF[0], endw)
-    send("lf0")
-
-    Y = [B("win", 0, L + C), B("yb", 0, L + C), B("hf", 0, L + C)]
-    MK = [B("mk%d" % t, 0, L + C) for t in range(3)]
-    IB = B("ib", 0, L + C)
-    II = [IB, IB, B("yb", 0, L + C)]
-    WIN = B("win", 0, NEG + 8)
-
-    def gather(t, lo, hi, eng="a"):
-        src = IND(AUD, B("lu%d" % t, lo // 16, hi // 16))
-        (act if eng == "a" else cp)(S(Y[t], lo, hi), src)
-
-    def starts(t):
-        tmp = S(lf_, 0, C)
-        (act if t else cp)(tmp, IND(Y[t], BOFF[t]))
-        tt(IND(Y[t], BOFF[t]), tmp, G[t], OP.subtract)
-
-    def sums(t, q):
-        lo, hi = 1024 * q, 1024 * q + 1024
-        scan(S(II[t], lo, hi), S(MK[t], lo, hi), S(Y[t], lo, hi), 0.0 if q == 0 else S(II[t], lo - 1, lo), OP.mult, OP.add)
-        act(B("sg", lo, hi), S(II[t], lo, hi), AF.Sign, bias=0.5)
-        mm(wrap(S(PS[0], 64 * q, 64 * q + 64), zwb, B("sg", lo, hi), 64))
-
-    gather(0, 0, 2560)
-    for q in range(5, 8):
-        gather(0, 512 * q, 512 * q + 512, "v")
-    cp(IND(MK[0], BOFF[0]), zb)
-    starts(0)
-    fill(MK[1], 1)
-    for q in range(4):
-        sums(0, q)
-
-    cp(eqi, S(PS[1], 1, C + 1))
-    blk, tri, gt_ = new("sf", 128), new("sf", 128), new("sf", 128)
-    blkb = new("sb", 128)
-    zw = zwb
-    Fb, Rx, Z1, Z2 = new("sb", C + 2), new("sb", C + 2), new("sb", C + 2), new("sb", C + 2)
-    pick(gt_, S(ones, 0, 128), [[-16, 8], [0, 16]], OP.is_ge, 0, 1)
-    pick(blk, gt_, [[16, 8], [0, 16]], OP.is_ge, 15, -1)
-    ts(eqj, eqi, 15, OP.bitwise_and)
-    fill(onb, 1)
-    pick(tri, blk, [[1, 128]], OP.is_gt, 0, -1)
-    act(blkb, blk)
-    ts(B("lb0", 0, C), eqj, pm, OP.is_gt)
-    send("lb0")
     ts(row0, pm, 0.0, OP.is_equal)
-    ms(S(Fb, C, C + 2), 0.0)
-    ms(S(Rx, 0, 1), 0.0)
-    ms(S(Rx, C + 1, C + 2), 0.0)
-    ms(S(Z1, 0, 2), 0.0)
-    ms(S(Z2, 0, 2), 0.0)
-    rm18 = new("sf", 54)
-    iota(rm18, [[0, 3], [1, 18]], 0, 0)
-    act(rm18, rm18, AF.Sign)
+    ts(S(sel, 0, 128, 1, P8), S(selv, 0, 128, 1, P8), 0.0, OP.is_equal)
+    act(cmod, cmod, AF.Abs, bias=npm)
+    act(K, cmod, AF.Relu, bias=ms(f(1), 2.0e7), scale=-2.0e7)
+    zw = ts(new("sb", 144), xs, pg, OP.is_equal)
+    d1 = ts(f(), S(s16, 0, 16), pm, OP.add, float(L), OP.add)
+    d2 = ts(f(32), s16, pm, OP.add, float(DUMP), OP.add)
     for t in range(3):
-        fill(B("m1s%d" % t, 0, M1W), 0)
-    spack = new("sf", 2 * C)
-    k1, k2 = new("sf", C), new("sf", C)
-    AX, RW = new("sf", C + NQ + 8), new("sf", C + NQ + 8)
+        ms(B("aud%d" % t, W, W + 16), 0.0)
+    for lo in range(0, NEG, 1024):
+        hi = min(NEG, lo + 1024)
+        act(B("win", lo, hi), S(onb, 0, hi - lo), scale=0.0)
+    ms(B("win", NEG, NEG + 16), -1.0 - SH)
+    for t in range(2):
+        fill(B("y%d" % t, L, L + C), 0)
+    gt_, blk, tri, nblk = new("sb", 128), new("sb", 128), new("sb", 128), new("sb", 128)
+    pick(gt_, S(onb, 0, 128), [[-16, 8], [0, 16]], OP.is_ge, 0, 1)
+    pick(blk, gt_, [[16, 8], [0, 16]], OP.is_ge, 15, -1)
+    pick(tri, blk, [[1, 128]], OP.is_gt, 0, -1)
+    act(nblk, blk, scale=-1.0)
+    for q in range(8):
+        pick(B("rs", 256 * q, 256 * q + 256), S(onb, 0, 256), [[-1, 2], [-16, 8], [0, 16]], OP.is_equal, -2 * q, 1)
+    iota(tag0, [[2 * TAG, C]], 0, 0)
+    iota(S(spack, C, 2 * C), [[2 * TAG + NS, C]], TAG + L, 0)
+    iota(jv, [[1, 16], [256, 16]], 0, 16)
+    nblkf, ntrif = act(f(128), blk, scale=-1.0), act(f(128), tri, scale=-1.0)
+    sh, rxs, rxf = new("sb", 16), ms(new("sb", 17), 0.0), ms(f(40), 0.0)
 
-    def rows(t):
-        dma("s", B("win", EW, NEG, 1, ROW), B("sp%d" % t, 0, C))
+    def steps(m, c0, c1, n=16):
+        d = [f(n * m), f(n * m), f(n * m)]
+        for x, c in zip(d, (c0, c1)):
+            for s, v in enumerate(c):
+                if v is not None:
+                    iota(S(x, s, n * m, m), [[0, n]], int(v), 0)
+        return d, [[S(x, s, n * m, m) for s in range(m)] for x in d]
+    def wrap(o, src, n):
+        mm([(o, S(zw, 15 - i, 143 - i), S(src, i, 16 * n, 16), i == 0, i == 15) for i in range(16)])
 
-    ts(B("sp0", 0, C), B("lu0", 0, C), SH, OP.subtract)
-    rows(0)
-    act(S(spack, 0, C), cio, scale=32768.0, bias=16.0 * EW + 2048.0)
-    act(B("h0", 0, NQ), B("mk0", 0, NQ), scale=0.0)
+    def spread(bank, src, n):
+        mm([(S(bank, i, 16 * n, 16), B("rs", 128 * i, 128 * i + 128), src, True, True) for i in range(16)])
 
-    def needed(t):
-        M = new("sf", 16)
-        ts(S(Fb, 0, C), S(PS[0], 0, C), 2.5, OP.is_le)
-        scan(S(Rx, 1, C + 1), S(onb, 0, C), S(Fb, 0, C), 0.0, OP.mult, OP.add)
-        tt(S(Z2, 2, C + 2), IND(Fb, KEND[t]), B("lb%d" % t, 0, C), OP.mult)
-        act(S(Z1, 2, C + 2), IND(Rx, KEND[t]))
-        mm([(S(PS[1], 0, C + 1), blkb, S(Z2, 1, C + 2), True, False), (S(PS[1], 0, C + 1), blkb, S(Z1, 1, C + 2), False, True)])
-        scan(k1, S(K, 0, C), S(PS[1], 0, C), 0.0, OP.max, OP.min)
-        scan(k2, S(K, 0, C), S(PS[1], 1, C + 1), 0.0, OP.max, OP.min)
-        M0 = new("sf", 16)
-        tt(M0, ZZ[t], S(k1, 15, C, 16), OP.subtract)
-        tt(M, M0, S(k2, 15, C, 16), OP.add)
+    def prefix(o, tot, x, rx, below, group):
+        scan(S(rx, 1, 17), x, S(zb, 0, 16), 0.0, OP.add, OP.add)
+        mm([(o, below, x, True, False)])
+        mm([(o, group, S(rx, 0, 16), False, True)])
+        return lambda: mm([(tot, group, S(rx, 16, 17), True, True)])
+
+    cp(S(lf_, 1, C + 1, 1, P8), B("li", 0, C, 1, P8))
+    scan(S(ef, 0, C + 1, 1, P8), S(onb, 0, C + 1, 1, P8), S(lf_, 0, C + 1, 1, P8), 0.0, OP.mult, OP.add)
+    mm([(S(PS[2], 0, C + 1), S(sel, 0, 128, 1, P8), S(ef, 0, C + 1, 1, P8), True, True)])
+    kb, ke = f(C), f(C)
+    scan(kb, S(K, 0, C), S(PS[2], 0, C), 0.0, OP.max, OP.min)
+    scan(ke, S(K, 0, C), S(PS[2], 1, C + 1), 0.0, OP.max, OP.min)
+    eqi = cp(new("si", C), S(PS[2], 1, C + 1))
+    btag = tt(tag0, S(PS[2], 0, C), tag0, OP.add)
+    BEG, END = S(kb, 15, C, 16), S(ke, 15, C, 16)
+    LEN = tt(f(), END, BEG, OP.subtract)
+    BOFF = cp(new("su", 16), tt(f(), tt(f(), ts(f(), LEN, 0.5, OP.is_lt), d1, OP.mult), BEG, OP.max))
+    KEND = cp(new("su", 16), ts(new("si", 16), cp(new("si", 16), END), 4, OP.logical_shift_right))
+    lb = ts(new("sb", C), ts(eqi, eqi, 15, OP.bitwise_and), pm, OP.is_gt)
+    CUT, (cut0, cut1, cut) = steps(6, (BIG, 0, 0, None, None, 0), (None, None, None, 1, BIG, 0))
+    AT, (at0, at1, at) = steps(3, (BIG, None, None), (None, BIG, None))
+    FIN, (fin0, fin1, fin) = steps(2, (-BIG, None), (None, None), 32)
+    act(at0[1], BEG, bias=-1.0)
+    act(at1[2], d1)
+    cbig = ms(f(1), BIG)
+    ms(S(PS[4], 0, 32, 2), -BIG)
+    cp(IND(MK, BOFF), zb)
+    lu = cp(new("su", C), B("spi", 0, C))
+    G = cp(f(C), B("gi", 0, C))
+    sgz = act(new("sb", C), G, AF.Sign, bias=-0.5)
+    wrap(S(PS[7], 0, 16), sgz, 16)
+    NZ = ts(f(), S(PS[7], 0, 16), -2.5, OP.is_lt)
+    mm([(S(PS[6], 0, C), blk, sgz, True, True)])
+    zr = ts(f(C), S(PS[6], 0, C), -2.5, OP.is_ge)
+    tt(S(spack, 0, C), btag, zr, OP.add)
+    pack = [f(C), f(2 * C), f(2 * C), f(2 * C)]
+    act(S(pack[3], 0, C), zr, scale=-1.0)
+    fill(S(pack[1], C, 2 * C), 0)
+    for t in range(2):
+        act(B("ii%d" % t, L, L + C), G, scale=-1.0)
+    spf, spt = ts(f(C), B("spi", 0, C), SH, OP.subtract), f(C)
+    op("v", [spf], [spt], lambda: [g.vector.transpose(ap(spt), ap(spf))], cost(spt, [spf]))
+    dma("s", [(B("win", 512 * b, 512 * b + 512, 1, (16 * h, 128, 32)), S(spt, 32 * b + 16 * h, 32 * b + 16 * h + 16))
+              for b in range(8) for h in range(2)], 8.0, after=[names["q3"]])
+
+    Y = [B("y0", 0, L + C), B("y1", 0, L + C), B("y0", 0, L + C)]
+    II = [B("ii0", 0, L + C), B("ii1", 0, L + C), B("ii0", 0, L + C)]
+    WIN = B("win", 0, NEG + 8)
+    H0, HF = B("h0", 0, DUMP + 2 * C), B("hf", 0, DUMP + 2 * C)
+    Fb, Rx, Z1, Z2 = new("sb", C + 2), new("sb", C + 2), new("sb", C + 2), new("sb", C + 2)
+    for x in (S(Fb, C, C + 2), S(Rx, 0, 1), S(Rx, C + 1, C + 2), S(Z1, 0, 2), S(Z2, 0, 2)):
+        ms(x, 0.0)
+    fill(S(H0, 0, NQ), 0, NQ // 2)
+    tmp, k1, k2 = f(C), f(C), f(C)
+
+    def sums(t, onv):
+        part[0] = "sums%d" % t
+        for q in range(8):
+            src = IND(AUD[t], S(lu, 32 * q, 32 * q + 32))
+            (cp if q in onv else act)(S(Y[t], 512 * q, 512 * q + 512), src, line="y%d%d" % (t, q in onv))
+        act(tmp, IND(Y[t], BOFF))
+        tt(IND(Y[t], BOFF), tmp, G, OP.subtract)
+        half = 32 if t == 0 else 64
+        for q in range(4):
+            lo, hi = 1024 * q, 1024 * q + 1024
+            for l in range(lo, hi, PIECE[t]):
+                h = l + PIECE[t]
+                scan(S(II[t], l, h), S(MK, l, h), S(Y[t], l, h), 0.0 if l == 0 else S(II[t], l - 1, l), OP.mult, OP.add)
+            mid = hi if q < 3 else lo + 16 * half
+            act(B("sg", lo, mid), S(II[t], lo, mid), AF.Sign, bias=0.5)
+            if mid < hi:
+                ts(B("sg", mid, hi), S(II[t], mid, hi), 0.0, OP.is_lt)
+            wrap(S(PS[0], 64 * q, 64 * q + 64) if q < 3 else S(PS[1], 0, 64), B("sg", lo, hi), 64)
+        ts(S(Fb, 0, 192), S(PS[0], 0, 192), 2.5, OP.is_le)
+        scan(S(Rx, 1, 193), S(onb, 0, 192), S(Fb, 0, 192), 0.0, OP.mult, OP.add)
+        ts(S(Fb, 192, 192 + half), S(PS[1], 0, half), 2.5, OP.is_le)
+        if half < 64:
+            ts(S(Fb, 192 + half, 256), S(PS[1], half, 64), 6.5, OP.is_ge)
+        scan(S(Rx, 193, C + 1), S(onb, 0, 64), S(Fb, 192, C), S(Rx, 192, 193), OP.mult, OP.add)
+        tt(S(Z2, 2, C + 2), IND(Fb, KEND), lb, OP.mult)
+        act(S(Z1, 2, C + 2), IND(Rx, KEND))
+        mm([(S(PS[2], 0, C + 1), blk, S(Z2, 1, C + 2), True, False), (S(PS[2], 0, C + 1), blk, S(Z1, 1, C + 2), False, True)])
+        o = S(PS[3], 0, C)
+        mm([(o, blk, S(Z2, 2, C + 2), True, False), (o, nblk, S(Z2, 1, C + 1), False, False),
+            (o, blk, S(Z1, 2, C + 2), False, False), (o, nblk, S(Z1, 1, C + 1), False, True)])
+        scan(k1, S(K, 0, C), S(PS[2], 0, C), 0.0, OP.max, OP.min)
+        scan(k2, S(K, 0, C), S(PS[2], 1, C + 1), 0.0, OP.max, OP.min)
+        act(S(pack[t], 0, C), o)
+        M = tt(f(), tt(f(), NZ, S(k1, 15, C, 16), OP.add), S(k2, 15, C, 16), OP.subtract)
+        part[0] = "visit%d" % t
         return M
 
-    def release(t, M, a, ne, f1, lo):
-        m = B("m1s%d" % t, 0, M1W)
-        a1, n1, sh, rel, b = S(m, 56, 72), S(m, 72, 88), S(m, 89, 105), S(m, 107, 123), S(m, 125, 141)
-        uv, r16, begm, rx = new("sf", 32), new("sh", 32), new("sf", 16), new("sf", 54)
-        act(begm, BEG[t], bias=-2048.0)
-        tt(a1, M, a, OP.min)
-        if t == 0:
-            tt(sh, M, a, OP.is_gt)
-            tt(b, M, a, OP.min)
-            tt(rel, a, a1, OP.subtract)
-            tt(S(r16, 0, 16), begm, a1, OP.add)
-            uv = rel
-        else:
-            f0 = new("sf", 16)
-            tt(f0, M, a, OP.is_gt)
-            tt(S(uv, 0, 16), a, a1, OP.subtract)
-            if f1 is not None:
-                f2 = new("sf", 16)
-                tt(f2, f0, f1, OP.add)
-                f0 = f2
-            tt(S(r16, 0, 16), begm, a1, OP.add)
-            tt(n1, ne, f0, OP.min)
-            tt(S(uv, 16, 32), ne, n1, OP.subtract)
-            tt(b, a1, n1, OP.add)
-            tt(S(r16, 16, 32), lo, n1, OP.add)
-            tt(rel, S(uv, 0, 16), S(uv, 16, 32), OP.add)
-        n = 16 if t == 0 else 32
-        e = new("sf", n)
-        ts(e, S(uv, 0, n), 0.5, OP.is_lt, 1.0e5, OP.mult)
-        for lo_, hi, bank in ((0, 54, 6),) if t == 0 else ((18, 54, 6), (0, 18, 3)):
-            scan(S(rx, lo_, hi), S(rm18, lo_, hi), S(m, 88 + lo_, 88 + hi), 0.0, OP.mult, OP.add)
-            o = S(PS[bank], lo_, hi - 1)
-            mm([(o, blk, S(rx, lo_, hi - 1), True, False), (o, tri, S(m, 89 + lo_, 88 + hi), False, True)])
-            if bank == 6:
-                offu = offsets(S(PS[6], 18, 34), S(uv, 0, 16), e, n)
-            cp(S(m, lo_, hi - 1), o)
-        spread(PS[7], S(r16, 0, n), n)
-        send("m1s%d" % t)
-        return m, offu, n
+    hA, hK, relh = cmod, f(NQ), new("sh", NQ)
+    AX, RW = f(NQ + C), f(NQ + C)
 
-    def offsets(st0, u, e, n):
-        key, off, offu = new("sf", n), new("sf", n), new("su", n)
-        tt(S(key, 0, 16), st0, S(e, 0, 16), OP.add)
-        if n == 32:
-            ue = new("sf", 16)
-            tt(ue, u, S(e, 16, 32), OP.add)
-            tt(S(key, 16, 32), st0, ue, OP.add)
-        tt(off, key, S(d2, 0, n), OP.min)
-        cp(offu, off)
-        return offu
+    def slot(s):
+        return B("win", L + s, NEG, NS)
 
-    def place(src, n, e=None):
-        vi, lo, hi, l2, s1, pos = new("si", n), new("si", n), new("si", n), new("sf", n), new("sf", n), new("su", n)
-        st = [lambda: cp(vi, src), lambda: ts(lo, vi, 15, OP.bitwise_and),
-              lambda: ts(hi, vi, 4, OP.logical_shift_right, 1023, OP.bitwise_and),
-              lambda: ts(l2, lo, 256.0, OP.mult), lambda: tt(s1, l2, hi, OP.add)]
-        if e is None:
-            st.append(lambda: cp(pos, s1))
-        else:
-            s2 = new("sf", n)
-            st += [lambda: tt(s2, s1, e, OP.max), lambda: ts(pos, s2, float(NEG), OP.min)]
-        return pos, st
+    def place(src, n, ev=None):
+        vi = cp(new("si", n), src) if ev is None else tt(new("si", n), src, ev, OP.max)
+        return ts(new("su", n), ts(new("si", n), vi, TAG - 1, OP.bitwise_and), float(NEG), OP.min)
 
-    pack, hA, hK, relh = new("sf", 2 * C), new("sf", NQ), new("sf", NQ), new("sh", NQ)
-    ltb, nxb = new("sb", 2 * C), new("sf", 2 * C)
-    H0 = B("h0", 0, DUMP + 2 * C)
-
-    def lookup(t, offu, n, between):
-        act(S(pack, 0, 16 * n), S(PS[7], 0, 16 * n))
-        tt(IND(H0, offu), S(pack, 0, 16 * n), S(spack, 0, 16 * n), OP.add)
-        scan(hA, ones, S(H0, 0, NQ), -1.0, OP.add, OP.max)
+    def lookup(t, offu, n):
+        tt(IND(H0, offu), S(pack[t], 0, 16 * n), S(spack, 0, 16 * n), OP.add)
+        scan(hA, S(onb, 0, NQ), S(H0, 0, NQ), -1.0, OP.add, OP.max)
         if t < 2:
-            act(S(H0, 0, NQ), B("mk0", 0, NQ), scale=0.0)
+            fill(S(H0, 0, NQ), 0, NQ // 2)
         scan(hK, K, hA, 0.0, OP.max, OP.min)
-        pos, st = place(S(hK, 15, NQ, 16), NQ // 16)
-        for k in range(max(len(st), len(between))):
-            if k < len(st):
-                st[k]()
-            if k < len(between):
-                between[k]()
-        ts(relh, IND(WIN, pos), -SH, OP.max, row0, OP.mult)
-        mm(wrap(S(PS[7], 0, NQ // 16), zw, relh, NQ // 16))
+        pos = place(S(hK, 15, NQ, 16), NQ // 16)
+        ts(relh, IND(WIN, pos), row0, OP.mult)
+        wrap(S(PS[7], 0, NQ // 16), relh, NQ // 16)
+        ts(B("rs%d" % t, 0, NQ // 16), S(PS[7], 0, NQ // 16), SH, OP.add)
+        tell("r", t)
+        act(S(RW, NQ, NQ + C), IND(WIN, S(pos, 0, 16)))
 
-    def lookup2(t):
-        ts(B("m2s%d" % t, 0, NQ // 16), S(PS[7], 0, NQ // 16), SH, OP.add)
-        send("m2s%d" % t)
+    Ed, off = f(64), f(64)
+    a, b, aK0 = at1[0], cut1[2], S(Ed, 32, 64, 2)
 
-    def cut(t):
-        ma, mb = B("m1a%d" % (t - 1), 0, M1W), B("m1b%d" % (t - 1), 0, M1W)
-        sr, Ss, R, Pb, a1, n1, sh = S(ma, 0, 16), S(ma, 16, 17), S(ma, 34, 35), S(ma, 36, 52), S(ma, 56, 72), S(ma, 72, 88), S(ma, 89, 105)
-        c = [new("sf", 1) for _ in range(5)]
-        w = [new("sf", 16) for _ in range(17)]
-        qu = new("su", 16)
-        ts(c[0], S(mb, 16, 17), S(mb, 34, 35), OP.subtract, -float(SLOT), OP.max)
-        ts(c[4], S(mb, 16, 17), R, OP.subtract, float(C), OP.add)
-        ts(w[0], Pb, -1.0, OP.mult, float(L), OP.add)
-        act(w[1], sr, bias=-float(C + NQ))
-        ts(c[2], c[0], 0.0, OP.min, R, OP.subtract)
-        ts(w[2], sr, R, OP.is_ge, c[4], OP.mult)
-        act(w[16], n1, scale=-1.0, bias=float(t - 1))
-        tt(w[3], w[0], sr, OP.subtract)
-        ts(w[4], sr, c[2], OP.add, -0.5, OP.is_lt)
-        tt(w[5], w[1], w[2], OP.add)
-        ts(w[6], w[0], c[2], OP.add, 0.0, OP.max)
-        tt(w[7], w[4], sh, OP.mult)
-        tt(w[8], w[6], w[3], OP.max)
-        tt(w[9], w[7], n1, OP.add)
-        an = new("sf", 32)
-        a, ne = S(an, 0, 16), S(an, 16, 32)
-        tt(a, a1, w[8], OP.min)
-        tt(w[10], w[8], a, OP.subtract)
-        tt(ne, w[9], w[10], OP.min)
-        tt(w[11], ne, n1, OP.is_gt)
-        tt(w[12], w[11], w[5], OP.mult)
-        ts(qu, w[12], float(C + NQ), OP.add)
-        return dict(an=an, a=a, ne=ne, qu=qu, lo=w[16], rp=w[8], Rn=c[2], S=Ss, tot=S(ma, 52, 53), a1=a1)
-
-    def arrive(t):
-        k = t - 1
-        ma, mb = "m2a%d" % k, "m2b%d" % k
-        h = new("sh", 16 + 32 + 32)
-        ts(S(h, 0, 16), B(ma, 0, 16), SH, OP.subtract)
-        ts(S(h, 16, 44), B(mb, 0, 28), SH, OP.subtract)
-        if k:
-            ts(S(h, 48, 48 + 16 * k), B(ma, 28, 28 + 16 * k), SH, OP.subtract)
-        spread(PS[4], S(h, 0, 16), 16)
-        spread(PS[5], S(h, 16, 44), 28)
-        if k:
-            spread(PS[0] if k == 2 else S(PS[4], C, 2 * C), S(h, 48, 48 + 16 * k), 16 * k)
-
-    def arrive2(t, qu):
-        k = t - 1
-        act(S(RW, 0, C), S(PS[4], 0, C))
-        act(S(RW, C, C + NQ), S(PS[5], 0, NQ))
-        if k:
-            act(B("win", 0, C * k), PS[0] if k == 2 else S(PS[4], C, 2 * C))
-        act(B("win", C * k, C * k + C), IND(RW, qu))
-
-    M = needed(0)
-    for q in range(4):
-        pick(B("rs", 512 * q, 512 * q + 512), S(onb, 0, 512), [[-1, 4], [-16, 8], [0, 16]], OP.is_equal, -4 * q, 1)
-    for q in range(8):
-        gather(1, 512 * q, 512 * q + 512)
-    fill(B("yb", L, L + C), 0)
-    fill(B("hf", L, L + C), 0)
-    for t in (1, 2):
-        cp(B("lo%d" % t, 0, 32), B("lf%d" % t, C + 48, C + 80))
-    for q in range(8):
-        gather(2, 512 * q, 512 * q + 512)
-    fill(B("win", NEG, NEG + 8), int(-1 - SH))
-    fill(S(AX, C + NQ, C + NQ + 8), 0)
-    fill(S(RW, C + NQ, C + NQ + 8), int(W - SH))
-    m, offu, n = release(0, M, LEN[0], None, None, None)
-    lookup(0, offu, n, [])
-    act(S(spack, C, 2 * C), cio, scale=32784.0, bias=16384.0)
-
-    for t in (1, 2):
-        k = t - 1
-        cp(IND(MK[t], BOFF[t]), zb)
-        lookup2(k)
-        if t == 1:
-            fill(MK[2], 1)
-        ts(B("sp%d" % t, 0, C), B("lu%d" % t, 0, C), SH, OP.subtract)
-        rows(t)
-        starts(t)
-        act(S(II[t], L, L + C), G[t], scale=-1.0)
-        sums(t, 0)
-        u = cut(t)
-        sums(t, 1)
-        a, ne = u["a"], u["ne"]
-        bm, t1, t2, t3, t4, offp = new("sf", 16), new("sf", 16), new("sf", 16), new("sf", 16), new("sf", 16), new("su", 16)
-        tt(bm, BEG[t], d1p, OP.subtract)
-        ts(t2, a, 0.5, OP.is_gt)
-        tt(t3, a, bm, OP.add)
-        sums(t, 2)
-        act(S(AX, 0, C), IND(AUD, B("m2a%d" % k, 0, 16)), scale=-1.0)
-        act(S(AX, C, C + NQ), IND(AUD, B("m2b%d" % k, 0, 28)), scale=-1.0)
-        tt(t1, t3, t2, OP.mult)
-        arrive(t)
-        tt(t4, t1, d1, OP.add)
-        nx, lt = nxb, ltb
-        if t == 2:
-            of, e1, o1, ou = new("sf", 16), new("sf", 16), new("sf", 16), new("su", 16)
-            cp(of, B("m2a1", 28, 44))
-            ts(e1, ne, 0.5, OP.is_lt, float(W), OP.mult)
-            cp(offp, t4)
-            tt(o1, of, e1, OP.max)
-            cp(ou, o1)
-            act(S(nx, 0, C), IND(AUD, ou), scale=-1.0)
+    def release(t, x, nrel, thr1):
+        n = 16 if t == 0 else 32
+        E = f(n)
+        if t == 0:
+            ts(E, x, 0.5, OP.is_lt)
         else:
-            cp(offp, t4)
-            act(S(nx, 0, C), IND(AX, u["qu"]))
-        sums(t, 3)
-        if t == 2:
-            tt(S(nx, C, 2 * C), IND(AX, u["qu"]), S(nx, 0, C), OP.add)
-        tt(S(lt, C * k, C * t), IND(II[t], offp), S(nx, C * k, C * t), OP.is_lt)
-        f1 = None
-        if t == 2:
-            f1 = new("sf", 16)
-            s1, s2, s3, s4, offq = new("sf", 16), new("sf", 16), new("sf", 16), new("sf", 16), new("su", 16)
-            ts(s1, u["a1"], 0.5, OP.is_gt)
-            tt(s2, u["a1"], bm, OP.add)
-            tt(s3, s1, s2, OP.mult)
-            tt(s4, s3, d1, OP.add)
-            cp(offq, s4)
-            act(kb, IND(AUD, B("m2a1", 28, 44)), scale=-1.0)
-            tt(S(lt, 0, C), IND(II[t], offq), kb, OP.is_lt)
-            mm(wrap(S(PS[2], 0, 16), zwb, S(lt, 0, C), 16))
-            ts(f1, S(PS[2], 0, 16), 6.5, OP.is_ge)
-        mm(wrap(S(PS[3], 0, 16), zwb, S(lt, C * k, C * t), 16))
-        M = needed(t)
-        arrive2(t, u["qu"])
-        ts(B("m1s%d" % t, 89, 105), S(PS[3], 0, 16), 6.5, OP.is_ge)
-        if t == 2:
-            for q in range(8):
-                act(B("hf", 512 * q, 512 * q + 512), B("mk0", 512 * q, 512 * q + 512), scale=0.0)
-        eh = new("sh", C)
-        ts(eh, B("win", C * k, C * k + C), row0, OP.mult)
-        mm(wrap(S(PS[2], 0, 16), zw, eh, 16))
-        m, offu, n = release(t, M, a, ne, f1, u["lo"])
-        n1, ew = S(m, 72, 88), S(PS[2], 0, 16)
-        x = [new("sf", 16) for _ in range(6)]
-        if t == 1:
-            steps = [lambda: ts(x[0], ew, SH, OP.subtract), lambda: tt(x[1], x[0], n1, OP.mult),
-                     lambda: ts(B("m2s1", 28, 44), x[1], float(W), OP.add)]
-        else:
-            steps = [lambda: (ts(x[0], ew, SH, OP.add), tt(x[1], u["lo"], n1, OP.add)),
-                     lambda: (tt(x[2], of, x[0], OP.subtract), ts(x[3], x[1], 1.0, OP.is_equal)),
-                     lambda: (tt(x[4], x[2], x[3], OP.mult), cp(B("m2s2", 28, 44), of)),
-                     lambda: tt(x[5], x[4], x[0], OP.add), lambda: cp(B("m2s2", 44, 60), x[5])]
-        lookup(t, offu, n, steps)
+            tt(S(E, 0, 16), x, thr1, OP.is_le)
+            tt(S(E, 16, 32), x, aK0, OP.is_le)
+        tt(S(Ed, 1, 2 * n, 2), E, S(d2, 0, n), OP.mult)
+        total = prefix(S(PS[4], 1, 32, 2), S(PS[4], 40, 41), nrel, S(rxf, 0, 17), ntrif, nblkf)
+        tt(S(off, 1, 32, 2), S(PS[4], 1, 32, 2), S(Ed, 1, 32, 2), OP.max)
+        if t:
+            scan(S(off, 32, 64), S(PS[4], 0, 32), S(Ed, 32, 64), 0.0, OP.add, OP.max)
+        offu = cp(new("su", n), S(off, 1, 2 * n, 2))
+        total()
+        R = cp(B("cs%d" % t, 2, 3), S(PS[4], 40, 41))
+        lookup(t, offu, n)
+        return R
 
-    r16, begm = new("sh", 32), new("sf", 16)
-    ts(S(r16, 0, 16), BEG[0], 2048.0, OP.subtract)
-    act(jv, jv0, scale=0.0625, bias=pm)
-    lookup2(2)
-    rows(0)
-    u = cut(3)
-    cp(S(r16, 16, 32), u["lo"])
-    spread(PS[7], r16, 32)
-    nb, e, c0, c1, ev, yh, yv = new("sf", 16), new("sf", 32), new("sf", 1), new("sf", 1), kb, new("sh", 16), new("sf", 16)
-    ts(nb, u["rp"], -1.0, OP.mult, float(L), OP.add)
-    ts(e, u["an"], 0.5, OP.is_lt, 1.0e5, OP.mult)
-    offu = offsets(nb, u["a"], e, 32)
-    HF = B("hf", 0, DUMP + 2 * C)
-    act(pack, PS[7])
-    ts(c0, u["Rn"], -1.0, OP.mult, u["S"], OP.min)
-    tt(yv, u["a"], u["ne"], OP.add)
-    tt(IND(HF, offu), pack, spack, OP.add)
-    tt(c1, c0, u["tot"], OP.add)
-    ts(yh, yv, 2048.0, OP.subtract)
+    def stay(t, R):
+        total = prefix(S(PS[4], 64, 80), S(PS[4], 80, 81), b, S(rxf, 20, 37), ntrif, nblkf)
+        if t == 2:
+            total()
+        n = 17 if t == 2 else 16
+        return ts(f(n), S(PS[4], 64, 64 + n), act(f(1), R, scale=-1.0, bias=float(L)), OP.add)
+
+    def shorts(t, R, LP):
+        prefix(S(PS[5], 0, 16), S(PS[5], 16, 17), sh, rxs, tri, blk)()
+        ts(B("cs%d" % t, 1, 2), S(PS[5], 16, 17), R, OP.min, act(f(1), R, bias=-float(SLOT)), OP.max)
+        st = dict(R=R, LP=LP, S=cp(B("cs%d" % t, 0, 1), S(PS[5], 16, 17)))
+        tell("c", t)
+        sr = st["sr"] = ts(f(), S(PS[5], 0, 16), R, OP.subtract)
+        st["own"] = tt(f(), act(f(), sr, bias=act(f(1), R, bias=float(NQ))), act(f(), sr, AF.Relu, scale=-BIG), OP.min)
+        nc1 = tt(cut1[1], sr, S(LP, 0, 16), OP.subtract)
+        tight = ts(f(), tt(f(), nc1, b, OP.add), -0.5, OP.is_gt, BIG, OP.mult)
+        st["srs"] = tt(f(), tt(f(), act(f(), sh, scale=-BIG, bias=cbig), sr, OP.add), tight, OP.add)
+        return st
+
+    def given(t, st):
+        y = ts(f(), st["sr"], B("ci%d" % t, 0, 1), OP.add, float(NQ - 1), OP.min)
+        return cp(new("su", 16), tt(f(), y, st["own"], OP.max))
+
+    def arrive(t, qu):
+        h = ts(new("sh", NQ // 16), B("ri%d" % t, 0, NQ // 16), SH, OP.subtract)
+        spread(PS[6], h, NQ // 16)
+        act(S(RW, 0, NQ), S(PS[6], 0, NQ))
+        act(slot(t), IND(RW, qu))
+
+    M = sums(0, ONV[0])
+    x = tt(f(), act(f(), LEN, bias=-1.0), M, OP.add)
+    nrel = ts(f(), x, -1.0, OP.mult, 0.0, OP.min)
+    ts(sh, x, 0.0, OP.is_lt)
+    R = release(0, x, nrel, None)
+    act(a, tt(b, LEN, nrel, OP.add))
+    st, n, n0 = shorts(0, R, stay(0, R)), None, None
+    fill(S(HF, 0, L), 0)
+
+    iia, lt, lto = f(C), new("sb", C), new("sb", C)
+    for t in (1, 2):
+        z, Rb = B("ci%d" % (t - 1), 1, 2), B("ci%d" % (t - 1), 2, 3)
+        M = sums(t, ONV[t])
+        act(at0[2], a, AF.Relu, scale=-BIG, bias=cbig)
+        scan(AT[2], AT[0], AT[1], 0.0, OP.add, OP.min)
+        sofar = act(iia, IND(II[t], cp(new("su", 16), at[2])))
+        nK = tt(cut0[4] if t == 1 else f(), M, act(f(), a, scale=-1.0), OP.max)
+        if t == 2:
+            ew = ts(new("su", 16), tt(f(), e0, n, OP.mult), float(W), OP.add)
+            sofar = tt(tmp, IND(AUD[2], ew), iia, OP.add)
+            wrap(S(PS[0], 0, 16), act(lto, sofar, AF.Sign, bias=0.5), 16)
+            nK = tt(cut0[4], nK, tt(f(), S(PS[0], 0, 16), act(f(), n, scale=101.5, bias=-99.0), OP.is_le), OP.subtract)
+        aK = tt(f(), a, nK, OP.add)
+        act(aK0, aK, AF.Relu, bias=-1.0)
+        thr1 = ts(f(), aK, 1.5, OP.is_lt, BIG, OP.mult)
+        if t == 2:
+            spread(PS[0], tt(new("sb", 16), ts(f(), aK, 0.5, OP.is_ge), n, OP.mult), 16)
+            act(S(pack[2], C, 2 * C), S(PS[0], 0, C), scale=-1.0, bias=1.0)
+        ts(cut1[0], S(st["LP"], 0, 16), z, OP.add, Rb, OP.subtract)
+        ns = ts(cut0[3], st["srs"], z, OP.add, Rb, OP.is_ge)
+        scan(CUT[2], CUT[0], CUT[1], 0.0, OP.subtract, OP.min)
+        x, nrel = cut[4], cut[5]
+        qu = given(t - 1, st)
+        act(S(AX, NQ, NQ + C), IND(AUD[t], B("rs%d" % (t - 1), 0, 16)), scale=-1.0)
+        act(S(AX, 0, NQ), IND(AUD[t], B("ri%d" % (t - 1), 0, NQ // 16)), scale=-1.0)
+        tt(lt, IND(AX, qu), sofar, OP.is_gt)
+        arrive(t - 1, qu)
+        if t == 1:
+            wrap(S(PS[6], 0, 16), ts(new("sh", C), slot(0), row0, OP.mult), 16)
+            e0 = ts(f(), S(PS[6], 0, 16), SH, OP.subtract)
+        thr = tt(f(), ts(f(), x, -0.5, OP.is_gt, 100.0, OP.mult), act(f(), ns, scale=93.5, bias=-93.5), OP.add)
+        wrap(S(PS[5], 0, 16), lt, 16)
+        tt(sh, S(PS[5], 0, 16), thr, OP.is_ge)
+        R = release(t, x, nrel, thr1)
+        if t == 1:
+            pick(slot(3), slot(0), [[0, C]], OP.is_ge, 0, 0)
+        act(b, tt(f(), nrel, cut[3], OP.subtract), bias=1.0)
+        tt(a, b, a, OP.min)
+        n0, n = n, tt(f(), b, a, OP.subtract)
+        st = shorts(t, R, stay(t, R))
+
+    part[0] = "end"
+    z, Rb = B("ci2", 1, 2), B("ci2", 2, 3)
+    lo_ = tt(new("sb", 16), tt(f(), ts(f(), n, 1.0, OP.is_equal, 2.0, OP.mult), n0, OP.mult), n, OP.subtract)
+    spread(PS[3], lo_, 16)
+    act(S(pack[3], C, 2 * C), S(PS[3], 0, C), bias=2.0)
+    PR = f(32)
+    act(S(PR, 0, 16), S(st["LP"], 0, 16), scale=-1.0, bias=float(L))
+    tt(S(PR, 16, 32), S(PR, 0, 16), a, OP.add)
+    PM = act(S(FIN[0], 1, 32, 2), cut1[1], bias=float(L))
+    tt(S(FIN[0], 33, 64, 2), PM, a, OP.add)
+    tt(S(FIN[1], 1, 32, 2), act(f(), a, AF.Relu, scale=-BIG, bias=cbig), S(d2, 0, 16), OP.min)
+    D2 = tt(f(), act(f(), n, AF.Relu, scale=-BIG, bias=cbig), S(d2, 16, 32), OP.min)
+    tg = act(f(1), S(st["LP"], 16, 17), scale=-1.0, bias=act(f(1), pg, scale=16.0, bias=float(L)))
+    SR = ts(f(1), st["S"], R, OP.subtract)
+    b1 = act(f(), b, bias=1.0 - 2048.0)
+    ns = ts(f(), st["srs"], z, OP.add, Rb, OP.is_ge)
+    ts(fin1[0], PR, z, OP.subtract, Rb, OP.add)
+    tt(S(FIN[1], 33, 64, 2), ns, D2, OP.mult)
+    scan(FIN[2], FIN[0], FIN[1], 0.0, OP.min, OP.max)
+    tt(IND(HF, cp(new("su", 32), fin[1])), pack[3], spack, OP.add)
+    qu = given(2, st)
+    q3 = ts(f(1), ts(f(1), Rb, z, OP.subtract, SR, OP.min), tg, OP.add)
+    ev = ts(k1, jv, q3, OP.is_ge, float(1024 * TAG - 1), OP.mult)
+    room = act(f(), tt(f(), S(FIN[1], 0, 32, 2), PM, OP.min), scale=-1.0, bias=L - 2048.0)
+    yh = ts(new("sh", 16), tt(f(), tt(f(), b1, ns, OP.subtract), room, OP.min), -2048.0, OP.max)
     spread(PS[3], yh, 16)
-    ts(c0, c1, 0.0625, OP.mult)
-    arrive(3)
-    yr = ke
-    act(yr, S(PS[3], 0, C), bias=2048.0)
-    dma("s", T.yn[:], S(yr, 0, C, 1, ROW))
+    act(k2, S(PS[3], 0, C), bias=2048.0)
+    dma("s", [(T.yn[:], S(k2, 0, C, 1, ROW))])
+    IB, DG, OUT = II[1], Y[1], Y[0]
     for q in range(4):
         lo = 1024 * q
         scan(S(IB, lo, lo + 1024), onb, S(HF, lo, lo + 1024), -1.0 if q == 0 else S(IB, lo - 1, lo), OP.add, OP.max)
-    arrive2(3, u["qu"])
-    ts(ev, jv, c0, OP.is_ge, 8000.0, OP.mult)
-    pend = []
-    for q in range(5):
-        for j in range(4):
-            if q < 4:
-                i = 4 * q + j
-                scan(B("yb", C * i, C * i + C), S(K, 0, C), S(IB, i, L, 16), 0.0, OP.max, OP.min)
-            for f in pend[2 * j:2 * j + 2]:
-                f()
-        if q > 0:
-            lo = 1024 * (q - 1)
-            half = 1024 if q < 4 else 512
-            act(S(H0, lo, lo + half), IND(WIN, S(pos, 0, half // 16)), bias=SH)
-            if half < 1024:
-                ts(S(H0, lo + half, lo + 1024), IND(WIN, S(pos, half // 16, 64)), SH, OP.add)
-            for j in range(4):
-                i = 4 * (q - 1) + j
-                dma("s" if q < 4 or j >= 2 else "a", T.yo[i:128:16, :], S(H0, C * i, C * i + C, 1, ROW))
-        if q < 4:
-            pos, pend = place(B("yb", 1024 * q + 15, 1024 * q + 1024, 16), 64, S(ev, 64 * q, 64 * q + 64))
-
-    finish()
+    arrive(2, qu)
+    act(slot(4), IND(RW, qu))
+    for q in range(4):
+        lo = 1024 * q
+        for i in range(4 * q, 4 * q + 4):
+            scan(S(DG, C * i, C * i + C), S(K, 0, C), S(IB, i, L, 16), 0.0, OP.max, OP.min)
+        pos = place(S(DG, lo + 15, lo + 1024, 16), 64, S(ev, 64 * q, 64 * q + 64))
+        for h in range(2):
+            o, src = S(OUT, lo + 512 * h, lo + 512 * h + 512), IND(WIN, S(pos, 32 * h, 32 * h + 32))
+            onv = q == 3 and h == 1 or q == 2 and h == 1
+            if onv:
+                ts(o, src, SH, OP.add)
+            else:
+                act(o, src, bias=SH)
+            dma("a" if q == 3 and not onv else "s",
+                [(T.yo[i:128:16, :], S(OUT, C * i, C * i + C, 1, ROW)) for i in range(4 * q + 2 * h, 4 * q + 2 * h + 2)])
+    return ops, names, sent

@@ -1,7 +1,7 @@
 import math
 import numpy as np
 from concourse.bass import DstId, RemoteDMATransfer
-from concourse.mybir import AluOpType as OP, ActivationFunctionType as AF
+from concourse.mybir import AluOpType as OP, ActivationFunctionType as AF, AxisListType as AX_
 
 N, W, L, C, SLOT = 8, 3072, 4096, 256, 192
 NQ = C + SLOT
@@ -10,20 +10,22 @@ NS = 5
 NEG = L + NS * C
 DUMP = L + C
 TAG = 8192
-BIG = 1.0e5
-QW = W // 4
+BIG, LIFT = 1.0e5, 1 << 21
+QW, EW = W // 4, W // 8
 F32, BF, F16, I32, U16 = "float32", "bfloat16", "float16", "int32", "uint16"
 CY, GATH, SCAT, GAP, NEAR, FAR = 0.83e-3 * 1.1, 1.56, 3.8, 0.12, 2.5, 5.0
-PLAN, SEED, TRIES, MOVES = {}, 1, 40, 20000
-LEAD = {"set": 1.0, "sums0": 4.0, "visit1": 1.0, "visit2": 2.0}
+PLAN, SEED, TRIES, MOVES = {}, 1, 1, 100000
+LEAD = {"set": 100.0, "sums0": 100.0, "visit0": 80.0, "lift": 70.0, "sums1": 60.0, "visit1": 40.0, "sums2": 20.0}
+HEAT, SETS = 0.25, 1
+FLY = [((5.1, 6.3, 6.3, 7.4), (9.0, 10.3, 10.3, 11.6)), (6.0, 11.0)]
 PIECE = [1024, 512, 512]
-ONV = [(4, 5, 6, 7), (5, 6, 7), ()]
+ONV = [(4, 5, 6, 7), (), ()]
 
 SCRATCH = {
     "win": ("sbuf", [128, NEG + 16], F32), "h0": ("sbuf", [128, DUMP + 2 * C], F32), "hf": ("sbuf", [128, DUMP + 2 * C], F32),
     "mk": ("sbuf", [128, L + C], BF), "sg": ("sbuf", [128, L], BF), "rs": ("sbuf", [128, 2048], BF),
-    "sf": ("sbuf", [128, 12100], F32), "sb": ("sbuf", [128, 4400], BF), "sh": ("sbuf", [128, 1200], F16),
-    "si": ("sbuf", [128, 1100], I32), "su": ("sbuf", [128, 900], U16),
+    "sf": ("sbuf", [128, 11900], F32), "sb": ("sbuf", [128, 5800], BF), "sh": ("sbuf", [128, 1700], F16),
+    "si": ("sbuf", [128, 1200], I32), "su": ("sbuf", [128, 1200], U16),
     "spi": ("sbuf", [128, C], I32), "gi": ("sbuf", [128, C], I32), "li": ("sbuf", [128, C], I32),
 }
 for _t in range(3):
@@ -31,15 +33,17 @@ for _t in range(3):
     for _r in "si":
         SCRATCH["c%s%d" % (_r, _t)] = ("sbuf", [128, 4], F32)
         SCRATCH["r%s%d" % (_r, _t)] = ("sbuf", [128, 32], U16)
+SCRATCH["y0"] = ("sbuf", [128, L + C], F32)
+SCRATCH["y1"] = ("sbuf", [128, L], BF)
+SCRATCH["y2"] = ("sbuf", [128, L], BF)
 for _t in range(2):
-    SCRATCH["y%d" % _t] = ("sbuf", [128, L + C], F32)
     SCRATCH["ii%d" % _t] = ("sbuf", [128, L + C], F32)
 for _b in range(8):
     SCRATCH["ps%d" % _b] = ("psum", [128, 512], F32)
 
 POOLS = {"v": 58, "a": 30, "t": 22, "g": 12, "d": 9}
 ARR = ["q0", "q1", "q2", "q3", "a2"] + ["%s%d" % (k, t) for t in range(3) for k in "cr"]
-SEMAPHORES = ["%s%d" % (e, i) for e in POOLS for i in range(POOLS[e])] + ["r" + a for a in ARR] + ["l%d" % k for k in range(7)] + ["sent"]
+SEMAPHORES = ["%s%d" % (e, i) for e in POOLS for i in range(POOLS[e])] + ["r" + a for a in ARR] + ["l%d" % k for k in range(5)] + ["sent"]
 COLS = {"c": 3, "r": NQ // 16}
 
 
@@ -49,7 +53,8 @@ def bits(engs):
 
 def ports(T, topo, r):
     src, far = T.cores[r], T.cores[(r - 2) % N]
-    return [c for c in topo.cores_of(src) if T.rank_of(c) is None and topo.may_write(c, far)]
+    return sorted((c for c in topo.cores_of(src) if T.rank_of(c) is None and topo.may_write(c, far)),
+                  key=lambda c: topo.die(c) == topo.die(src))
 
 
 def direct(T, topo, r):
@@ -70,27 +75,22 @@ def transfer(T, topo, core, dst, engs, src, out, sem):
 def relay_program(g, core, T, topo):
     n = 0
     mine = [r for r in range(N) if core in ports(T, topo, r)]
-    for r in sorted(mine, key=lambda r: not direct(T, topo, r)):
-        j = ports(T, topo, r).index(core)
-        cs = slice(QW * j, QW * j + QW)
-        one, two = T.cores[(r - 1) % N], T.cores[(r - 2) % N]
-        off = topo.engines(core, two)
+    for r in mine:
         if direct(T, topo, r):
-            g.wait_ge(T.sem.rq0, 16)
-            tr = [transfer(T, topo, core, one, off, T.aud1[:, cs], T.aud1[:, cs], "rq%d" % j)]
-        else:
-            g.wait_ge(T.sem.ra2, 16)
-            on = [e for e in topo.engines(core, one) if e not in off]
-            tr = [transfer(T, topo, core, one, on, T.aud2[:, cs], T.aud1[:, cs], "rq%d" % j),
-                  transfer(T, topo, core, two, off, T.aud2[:, cs], T.aud2[:, cs], "ra2")]
-        g.remote_dma_fused(tr, local_sem=T.sem.sent)
-        n += 8 * len(tr)
+            j = ports(T, topo, r).index(core)
+            dst = T.cores[(r - 1) % N]
+            jobs = [("rq%d" % k, 8, T.aud1[:, EW * p:EW * p + EW], "rq%d" % (p // 2)) for k, p in enumerate((j, j + 4))]
+            jobs.append(("ra2", 16, T.aud2[:, QW * j:QW * j + QW], "ra2"))
+            for sem, count, b, there in jobs:
+                g.wait_ge(T.sem[sem], count)
+                g.remote_dma_fused([transfer(T, topo, core, dst, topo.engines(core, dst), b, b, there)], local_sem=T.sem.sent)
+                n += 8
     for t in range(3):
         for r in mine:
             for k in "cr":
                 if hop(T, topo, r, k) == core:
                     dst, b = T.cores[(r + 1) % N], T["%si%d" % (k, t)][:, 0:COLS[k]]
-                    g.wait_ge(T.sem["r%s%d" % (k, t)], 8)
+                    g.wait_ge(T.sem["r%s%d" % (k, t)], 16)
                     g.remote_dma_fused([transfer(T, topo, core, dst, topo.engines(core, dst), b, b, "r%s%d" % (k, t))], local_sem=T.sem.sent)
                     n += 8
     if n:
@@ -108,7 +108,7 @@ def schedule(both):
         p |= {both[kk][1][name] + kk * n0 for kk, name in o["link"]}
         pre.append(sorted(p))
         qs.append(5 * k + "vatgs".index(o["q"]) if o["q"] else 10)
-    hard = [[j for j in pre[i] if qs[j] != qs[i] or j - int(i >= n0) * n0 in ops[i]["need"]] for i in range(n)]
+    hard = [[j for j in pre[i] if (qs[j] != qs[i] and "alt" not in ops[j]) or j - int(i >= n0) * n0 in ops[i]["need"]] for i in range(n)]
     post = [[] for _ in ops]
     for i in range(n):
         for j in pre[i]:
@@ -155,13 +155,16 @@ def schedule(both):
                     ready.append(j)
         return end, sorted(range(n), key=lambda i: (start[i], at[i]))
 
-    sets = ((0.93, 0.93, 1.0, 1.0, 0.1), (1.2, 1.4, 1.2, 1.4, 0.16))
+    sets = ((0.93, 0.93, 1.0, 1.0, 0.135), (1.2, 1.4, 1.2, 1.4, 0.16))[:SETS]
     busy = [[o["busy"] * (s[1] if o["ind"] else s[0]) for o in ops] for s in sets]
     lat = [[o["lat"] * (s[3] if o["lat"] > FAR and not o["q"] else s[2]) + s[4] for o in ops] for s in sets]
 
-    def run(order, s):
-        end, free, bs, ls = [0.0] * n, [0.0] * 11, busy[s], lat[s]
-        for i in order:
+    def run(order, s, a=0, known=None):
+        end, free, bs, ls = list(known) if a else [0.0] * n, [0.0] * 11, busy[s], lat[s]
+        for i in order[:a]:
+            free[qs[i]] = end[i] - ls[i]
+        free[10] = 0.0
+        for i in order[a:]:
             q = qs[i]
             t = free[q]
             for j in hard[i]:
@@ -173,9 +176,11 @@ def schedule(both):
             end[i] = t + ls[i]
         return end
 
-    def span(order):
-        ends = [run(order, s) for s in range(len(sets))]
-        return sum(max(e) + 0.02 * sum(e) / n for e in ends), ends
+    soon = [i + k * n0 for k in range(2) for name, i in both[k][1].items() if name[0] in "qf"]
+
+    def span(order, a=0, known=None):
+        ends = [run(order, s, a, known[s] if a else None) for s in range(len(sets))]
+        return sum(max(e) + 0.05 * sum(e) / n + 0.05 * sum(e[i] for i in soon) for e in ends), ends
 
     def held(order, end, s):
         before, last = {}, {}
@@ -202,13 +207,30 @@ def schedule(both):
         if best is None or v < best:
             best, order, ee = v, cand, ends
         p = [x + float(y) for x, y in zip(plan(end, True)[0], rng.normal(0, 0.3, n))]
-    cur, top, keep = best, best, order
-    pairs, dice, far, slack = None, rng.random((MOVES, 2)).tolist(), rng.geometric(0.4, MOVES).tolist(), rng.exponential(1.0, MOVES).tolist()
+    def flip(i):
+        qs[i] ^= 1 if qs[i] < 5 else 3
+        for s in range(len(sets)):
+            busy[s][i] = ops[i]["alt"]["va"[qs[i] % 5]][1] * sets[s][int(ops[i]["ind"])]
+
+    cur, top, keep, keepq = best, best, order, list(qs)
+    pairs, dice, far, slack = None, rng.random((MOVES, 3)).tolist(), rng.geometric(0.4, MOVES).tolist(), rng.exponential(1.0, MOVES).tolist()
     for it in range(MOVES):
         if pairs is None:
             pairs = [x for s in range(len(sets)) for x in held(order, ee[s], s)]
         u, v = pairs[int(dice[it][0] * len(pairs))]
         a, b = order.index(u), order.index(v)
+        w = (u, v)[dice[it][1] < 0.5]
+        if dice[it][2] < 0.25 and "alt" in ops[w]:
+            flip(w)
+            val, ends = span(order, a if w == u else b, ee)
+            if val <= cur + HEAT * (1.0 - it / MOVES) * slack[it]:
+                cur, ee, pairs = val, ends, None
+                order = sorted(order, key=lambda i: ends[0][i] - lat[0][i] - busy[0][i])
+                if cur < top:
+                    top, keep, keepq = cur, order, list(qs)
+            else:
+                flip(w)
+            continue
         if dice[it][1] < 0.5:
             same = [k for k in range(max(0, a - 150), a + 1) if qs[order[k]] == qs[v]]
             a = same[max(0, len(same) - far[it])]
@@ -230,14 +252,17 @@ def schedule(both):
                 continue
             seg = [i for i in seg if i not in take] + [i for i in seg if i in take]
         cand = order[:a] + seg + order[b + 1:]
-        val, ends = span(cand)
-        if val <= cur + 0.2 * (1.0 - it / MOVES) * slack[it]:
+        val, ends = span(cand, a, ee)
+        if val <= cur + HEAT * (1.0 - it / MOVES) * slack[it]:
             cur, ee, pairs = val, ends, None
             order = sorted(cand, key=lambda i: ends[0][i] - lat[0][i] - busy[0][i])
             if cur < top:
-                top, keep = cur, order
+                top, keep, keepq = cur, order, list(qs)
+    for i in range(n):
+        if qs[i] != keepq[i]:
+            flip(i)
     PLAN["us"] = [max(e) for e in span(keep)[1]]
-    return [[i for i in keep if i < n0], [i - n0 for i in keep if i >= n0]]
+    return [[(i, "vatgs-"[qs[i] % 5]) for i in keep if i < n0], [(i - n0, "vatgs-"[qs[i] % 5]) for i in keep if i >= n0]]
 
 
 def rank_program(g, core, T, topo):
@@ -249,7 +274,10 @@ def rank_program(g, core, T, topo):
         kinds = [[r for r in range(N) if direct(T, topo, r) == d][0] for d in (True, False)]
         PLAN["order"] = schedule([record(g, T, topo, r) for r in kinds])
     ops, names, sent = record(g, T, topo, rank)
-    order = PLAN["order"][0 if direct(T, topo, rank) else 1]
+    order = [i for i, q in PLAN["order"][0 if direct(T, topo, rank) else 1]]
+    for i, q in PLAN["order"][0 if direct(T, topo, rank) else 1]:
+        if "alt" in ops[i]:
+            ops[i].update(q=q, pool=q, emit=ops[i]["alt"][q][0])
     Q = {"v": g.vector, "a": g.scalar, "t": g.tensor, "g": g, "s": g.sync}
     known, last, waited, done = {q: set() for q in Q}, {}, {}, {}
     pos_ = {i: k for k, i in enumerate(order)}
@@ -408,10 +436,31 @@ def record(g, T, topo, rank):
         op("v", [], [o], lambda: [g.vector.memset(ap(o), c)], cost(o, []))
         return o
 
-    def act(o, a, fn=AF.Identity, bias=0.0, scale=1.0, line=None):
+    def sca(o, a, fn=AF.Identity, bias=0.0, scale=1.0, line=None):
         op("a", [a, bias], [o], lambda: [g.scalar.activation(ap(o), ap(a), fn, bias=ap(bias), scale=scale)], 0.05 + cost(o, [a], 1),
            line=line)
         return o
+
+    def either(o, a, fn, bias, scale, s1, f1, s2, f2, q="a", line=None):
+        i = len(ops)
+        sca(o, a, fn, bias, scale, line)
+        ops[i]["alt"] = {"a": (ops[i]["emit"], ops[i]["busy"]),
+                         "v": (lambda: [g.vector.tensor_scalar(ap(o), ap(a), ap(s1), ap(s2), f1, f2)], cost(o, [a]))}
+        ops[i]["q"] = ops[i]["pool"] = q
+        ops[i]["emit"], ops[i]["busy"] = ops[i]["alt"][q]
+        return o
+
+    def act(o, a, fn=AF.Identity, bias=0.0, scale=1.0, q="a", line=None):
+        if fn == AF.Identity and a[0][:2] != "ps":
+            return either(o, a, fn, bias, scale, scale, OP.mult, bias, OP.add, q, line)
+        return sca(o, a, fn, bias, scale, line)
+
+    def none(o, a, at_):
+        return either(o, a, AF.Relu, cbig if at_ == 0 else 0.0, -BIG, at_ + 0.5, OP.is_lt, BIG, OP.mult)
+
+    def sign(o, a, q="a"):
+        either(o, a, AF.Sign, 0.5, 1.0, 0.0, OP.is_ge, 0.5, OP.subtract, q)
+        return len(ops) - 1
 
     def mm(items):
         op("t", [x for m in items for x in m[1:3]], [m[0] for m in items],
@@ -432,15 +481,15 @@ def record(g, T, topo, rank):
             hi = min(wd(o), lo + step)
             iota(S(o, lo, hi), [[0, hi - lo]], c, 0)
 
-    def dma(q, pairs, us=2.1, line=None, after=()):
-        op(q, [a for o, a in pairs], [o for o, a in pairs], lambda: [Q[q].dma_start(ap(o), ap(a)) for o, a in pairs],
-           0.08 * len(pairs), us, pool="d", inc=16, line=line, after=after)
+    def dma(q, pairs, us=2.1, line=None, after=(), also=()):
+        op(q, [a for o, a in pairs] + list(also), [o for o, a in pairs], lambda: [Q[q].dma_start(ap(o), ap(a)) for o, a in pairs],
+           0.1 * len(pairs), us, pool="d", inc=16, line=line, after=after)
 
-    def send(name, src, dst, engs, out, sem, line):
+    def send(name, line, *trs):
         def emit():
-            g.remote_dma_fused([transfer(T, topo, core, dst, engs, ap(src), ap(out), sem)], local_sem=T.sem.sent)
-            sent[0] += len(engs)
-        names[name] = op("g", [src], [], emit, 0.35, pool="-", line=line)
+            g.remote_dma_fused([transfer(T, topo, core, d, e, ap(a), ap(o), s) for a, d, e, o, s in trs], local_sem=T.sem.sent)
+            sent[0] += sum(len(x[2]) for x in trs)
+        names[name] = op("g", [x[0] for x in trs], [], emit, 0.35, pool="-", line=line)
 
     def lands(buf, sem, count, us, link):
         op(None, [], [buf], None, 0.0, us, pool=sem, inc=count, link=link)
@@ -448,10 +497,9 @@ def record(g, T, topo, rank):
     def tell(k, t):
         first = hop(T, topo, rank, k)
         e = topo.engines(core, first)
-        send("%s%d" % (k, t), B("%ss%d" % (k, t), 0, COLS[k]), first, e if near else e[:8], B("%si%d" % (k, t), 0, COLS[k]),
-             "r%s%d" % (k, t), k)
+        send("%s%d" % (k, t), k, (B("%ss%d" % (k, t), 0, COLS[k]), first, e, B("%si%d" % (k, t), 0, COLS[k]), "r%s%d" % (k, t)))
         lands(B("%si%d" % (k, t), 0, 32), "r%s%d" % (k, t), 8 if near else 16, FAR if near else NEAR,
-              [(1 - me, "%s%d" % (k, t)), (0, "q3"), (1, "q3")])
+              [(1 - me, "%s%d" % (k, t)), (0, "f3")])
 
     PS = [B("ps%d" % b, 0, 512) for b in range(8)]
     AUD = [B("aud%d" % t, 0, W + 8) for t in range(3)]
@@ -459,28 +507,35 @@ def record(g, T, topo, rank):
     P8 = (0, 8, 1)
 
     loads = [(B("li", 0, C, 1, P8), T.lens[:], 2.1), (B("spi", 0, C), T.spots[:], 2.5)]
-    loads += [(B("aud0", QW * j, QW * j + QW), T.aud[:, QW * j:QW * j + QW], 3.2 + 0.9 * j) for j in range(4)]
-    loads += [(B("gi", 0, C), T.gua[:], 6.2)]
+    loads += [(B("aud0", 2 * QW * j, 2 * QW * (j + 1)), T.aud[:, 2 * QW * j:2 * QW * (j + 1)], 4.3 + 1.8 * j) for j in range(2)]
+    loads += [(B("gi", 0, C), T.gua[:], 6.6)]
     for k, (o, a, us) in enumerate(loads):
-        q = "sa"[k % 2]
+        q = "sasss"[k]
         op(q, [], [], (lambda q, o, a, k: lambda: Q[q].dma_start(ap(o), a).then_inc(T.sem["l%d" % k], 16))(q, o, a, k), 0.08,
            pool="-", line="load")
         names["l%d" % k] = len(ops) - 1
         lands(o, "l%d" % k, 16, us, [(me, "l%d" % k)])
-    for j, c in enumerate(ports(T, topo, rank)):
-        send("q%d" % j, B("aud0", QW * j, QW * j + QW), c, topo.engines(core, c), B("aud1" if near else "aud2", QW * j, QW * j + QW),
-             "rq0" if near else "ra2", "q")
+    port, mate = ports(T, topo, rank), T.cores[(rank + (1 if near else -1)) % N]
+    every = topo.engines(core, mate)
+
+    def quarter(t, j):
+        return B("aud%d" % t, QW * j, QW * j + QW)
+
     for j in range(4):
-        lands(B("aud1", QW * j, QW * j + QW), "rq%d" % j, 8, 9.0 if near else 10.0, [(0, "q%d" % j), (1, "q%d" % j)])
-    if not near:
-        mate = T.cores[(rank - 1) % N]
-        for j in range(4):
-            send("f%d" % j, B("aud1", QW * j, QW * j + QW), mate, topo.engines(core, mate)[8:], B("aud2", QW * j, QW * j + QW), "ra2", "q")
-    lands(B("aud2", 0, W), "ra2", 32, 8.0 if near else 13.0, [(1, "f3")] if near else [(0, "q3"), (1, "q3")])
+        if near:
+            send("q%d" % j, "q", *[(B("aud0", EW * p, EW * p + EW), port[p % 4], every[8 * (p % 2):8 * (p % 2) + 8],
+                                    B("aud1", EW * p, EW * p + EW), "rq%d" % (p // 4)) for p in (2 * j, 2 * j + 1)])
+        else:
+            send("q%d" % j, "q", (quarter(0, j), mate, every, quarter(1, j), "rq%d" % j))
+    for j in range(4):
+        lands(quarter(1, j), "rq%d" % j, 16, FLY[0][me][j], [(1 - me, "q%d" % j)])
+    for j in range(4):
+        send("f%d" % j, "q", (quarter(1, j), port[j] if near else mate, every, quarter(2, j), "ra2"))
+    lands(B("aud2", 0, W), "ra2", 64 if near else 32, FLY[1][me], [(1 - me, "f3")])
 
     pi_, pmi = new("si", 1), new("si", 1)
     pf, pm, npm, pg, row0 = f(1), f(1), f(1), f(1), f(1)
-    selv, sel, cmod, K, xs, s16, jv = f(128), f(128), f(NQ), f(NQ), f(144), f(32), f(C)
+    selv, cmod, K, xs, s16, jv = f(128), f(NQ), f(NQ), f(144), f(32), f(C)
     spack = f(2 * C)
     tag0 = f(C)
     iota(pi_, [[0, 1]], 0, 1)
@@ -488,7 +543,7 @@ def record(g, T, topo, rank):
     iota(cmod, [[0, NQ // 16], [1, 16]], 0, 0)
     iota(s16, [[16, 32]], 0, 0)
     iota(xs, [[1, 144]], -15, 0)
-    lf_, ef = f(C + 1), f(C + 1)
+    lf_, ef = f(C + 1), new("sh", C + 1)
     zb, onb = new("sb", C), new("sb", 1024)
     MK = B("mk", 0, L + C)
     ms(onb, 1.0)
@@ -502,20 +557,26 @@ def record(g, T, topo, rank):
     ts(npm, pm, -1.0, OP.mult)
     tt(pg, pf, pm, OP.subtract)
     ts(row0, pm, 0.0, OP.is_equal)
+    sel, sel2 = new("sb", 128), new("sb", 128)
     ts(S(sel, 0, 128, 1, P8), S(selv, 0, 128, 1, P8), 0.0, OP.is_equal)
+    ts(S(sel2, 0, 128, 1, P8), S(selv, 0, 128, 1, P8), 0.0, OP.is_equal, 2048.0, OP.mult)
     act(cmod, cmod, AF.Abs, bias=npm)
     act(K, cmod, AF.Relu, bias=ms(f(1), 2.0e7), scale=-2.0e7)
     zw = ts(new("sb", 144), xs, pg, OP.is_equal)
+    zw2 = act(new("sb", 144), zw, scale=2.0)
     d1 = ts(f(), S(s16, 0, 16), pm, OP.add, float(L), OP.add)
     d2 = ts(f(32), s16, pm, OP.add, float(DUMP), OP.add)
     for t in range(3):
-        ms(B("aud%d" % t, W, W + 16), 0.0)
-    for lo in range(0, NEG, 1024):
-        hi = min(NEG, lo + 1024)
-        act(B("win", lo, hi), S(onb, 0, hi - lo), scale=0.0)
+        ms(B("aud%d" % t, W, W + 16, 2), 0.0)
+        ms(B("aud%d" % t, W + 1, W + 16, 2), float(LIFT))
+    for lo in range(0, L, 1024):
+        act(B("win", lo, lo + 1024), onb, scale=0.0)
+    for lo in range(L, NEG, 640):
+        act(B("win", lo, lo + 640), S(onb, 0, 640), scale=0.0)
+    fill(B("y0", L, L + C), 0)
+    act(B("hf", 0, 1024), onb, scale=2.0 * LIFT)
+    fill(B("hf", 1024, L), 2 * LIFT)
     ms(B("win", NEG, NEG + 16), -1.0 - SH)
-    for t in range(2):
-        fill(B("y%d" % t, L, L + C), 0)
     gt_, blk, tri, nblk = new("sb", 128), new("sb", 128), new("sb", 128), new("sb", 128)
     pick(gt_, S(onb, 0, 128), [[-16, 8], [0, 16]], OP.is_ge, 0, 1)
     pick(blk, gt_, [[16, 8], [0, 16]], OP.is_ge, 15, -1)
@@ -523,9 +584,16 @@ def record(g, T, topo, rank):
     act(nblk, blk, scale=-1.0)
     for q in range(8):
         pick(B("rs", 256 * q, 256 * q + 256), S(onb, 0, 256), [[-1, 2], [-16, 8], [0, 16]], OP.is_equal, -2 * q, 1)
-    iota(tag0, [[2 * TAG, C]], 0, 0)
-    iota(S(spack, C, 2 * C), [[2 * TAG + NS, C]], TAG + L, 0)
+    iota(tag0, [[2 * TAG, C]], TAG, 0)
+    iota(S(spack, C, 2 * C), [[2 * TAG + NS, C]], 2 * TAG + L, 0)
     iota(jv, [[1, 16], [256, 16]], 0, 16)
+    inc, jend, j0, nb, up = new("sb", C), f(), f(), f(32), f(64)
+    fill(inc, 1)
+    iota(S(inc, 0, C, 16), [[0, 16]], 241, 0)
+    iota(jend, [[256, 16]], 15 - 2 * L, 16)
+    iota(j0, [[256, 16]], -1 - 2 * L, 16)
+    fill(nb, 0)
+    fill(up, 0)
     nblkf, ntrif = act(f(128), blk, scale=-1.0), act(f(128), tri, scale=-1.0)
     sh, rxs, rxf = new("sb", 16), ms(new("sb", 17), 0.0), ms(f(40), 0.0)
 
@@ -539,6 +607,11 @@ def record(g, T, topo, rank):
     def wrap(o, src, n):
         mm([(o, S(zw, 15 - i, 143 - i), S(src, i, 16 * n, 16), i == 0, i == 15) for i in range(16)])
 
+    def count(o, src, n, by):
+        op("t", [zw, zw2, src], [o], lambda: [g.tensor.matmul(ap(o), ap(S(zw if ops[by]["q"] == "a" else zw2, 15 - i, 143 - i)),
+                                                              ap(S(src, i, 16 * n, 16)), i == 0, i == 15) for i in range(16)],
+           16 * 64 * CY)
+
     def spread(bank, src, n):
         mm([(S(bank, i, 16 * n, 16), B("rs", 128 * i, 128 * i + 128), src, True, True) for i in range(16)])
 
@@ -549,13 +622,14 @@ def record(g, T, topo, rank):
         return lambda: mm([(tot, group, S(rx, 16, 17), True, True)])
 
     cp(S(lf_, 1, C + 1, 1, P8), B("li", 0, C, 1, P8))
-    scan(S(ef, 0, C + 1, 1, P8), S(onb, 0, C + 1, 1, P8), S(lf_, 0, C + 1, 1, P8), 0.0, OP.mult, OP.add)
-    mm([(S(PS[2], 0, C + 1), S(sel, 0, 128, 1, P8), S(ef, 0, C + 1, 1, P8), True, True)])
+    scan(S(ef, 0, C + 1, 1, P8), S(onb, 0, C + 1, 1, P8), S(lf_, 0, C + 1, 1, P8), -2048.0, OP.mult, OP.add)
+    mm([(S(PS[2], 0, C + 1), S(sel2, 0, 128, 1, P8), S(onb, 0, C + 1, 1, P8), True, False)])
+    mm([(S(PS[2], 0, C + 1), S(sel, 0, 128, 1, P8), S(ef, 0, C + 1, 1, P8), False, True)])
     kb, ke = f(C), f(C)
     scan(kb, S(K, 0, C), S(PS[2], 0, C), 0.0, OP.max, OP.min)
     scan(ke, S(K, 0, C), S(PS[2], 1, C + 1), 0.0, OP.max, OP.min)
     eqi = cp(new("si", C), S(PS[2], 1, C + 1))
-    btag = tt(tag0, S(PS[2], 0, C), tag0, OP.add)
+    tt(S(spack, 0, C), S(PS[2], 0, C), tag0, OP.add)
     BEG, END = S(kb, 15, C, 16), S(ke, 15, C, 16)
     LEN = tt(f(), END, BEG, OP.subtract)
     BOFF = cp(new("su", 16), tt(f(), tt(f(), ts(f(), LEN, 0.5, OP.is_lt), d1, OP.mult), BEG, OP.max))
@@ -564,30 +638,36 @@ def record(g, T, topo, rank):
     CUT, (cut0, cut1, cut) = steps(6, (BIG, 0, 0, None, None, 0), (None, None, None, 1, BIG, 0))
     AT, (at0, at1, at) = steps(3, (BIG, None, None), (None, BIG, None))
     FIN, (fin0, fin1, fin) = steps(2, (-BIG, None), (None, None), 32)
+    TURN, (turn0, turn1, turn) = steps(2, (0, None), (None, None), 32)
     act(at0[1], BEG, bias=-1.0)
     act(at1[2], d1)
     cbig = ms(f(1), BIG)
     ms(S(PS[4], 0, 32, 2), -BIG)
     cp(IND(MK, BOFF), zb)
-    lu = cp(new("su", C), B("spi", 0, C))
     G = cp(f(C), B("gi", 0, C))
     sgz = act(new("sb", C), G, AF.Sign, bias=-0.5)
     wrap(S(PS[7], 0, 16), sgz, 16)
     NZ = ts(f(), S(PS[7], 0, 16), -2.5, OP.is_lt)
     mm([(S(PS[6], 0, C), blk, sgz, True, True)])
-    zr = ts(f(C), S(PS[6], 0, C), -2.5, OP.is_ge)
-    tt(S(spack, 0, C), btag, zr, OP.add)
+    zr = ts(new("sb", C), S(PS[6], 0, C), -2.5, OP.is_ge, row0, OP.mult)
     pack = [f(C), f(2 * C), f(2 * C), f(2 * C)]
-    act(S(pack[3], 0, C), zr, scale=-1.0)
+    fill(S(pack[3], 0, C), 0)
     fill(S(pack[1], C, 2 * C), 0)
     for t in range(2):
         act(B("ii%d" % t, L, L + C), G, scale=-1.0)
-    spf, spt = ts(f(C), B("spi", 0, C), SH, OP.subtract), f(C)
-    op("v", [spf], [spt], lambda: [g.vector.transpose(ap(spt), ap(spf))], cost(spt, [spf]))
-    dma("s", [(B("win", 512 * b, 512 * b + 512, 1, (16 * h, 128, 32)), S(spt, 32 * b + 16 * h, 32 * b + 16 * h + 16))
-              for b in range(8) for h in range(2)], 8.0, after=[names["q3"]])
+    sph, eye, spt = ts(new("sh", C), B("spi", 0, C), SH, OP.subtract), new("sb", 128), B("h0", 1024, 2048)
+    pick(eye, S(onb, 0, 128), [[-1, 128]], OP.is_equal, 0, 1)
+    P32 = (0, 32, 1)
+    for h in range(2):
+        for m in range(4):
+            mm([(S(PS[4 * h + 1], 128 * m + 16 * e, 128 * m + 16 * e + 16, 1, P32), S(sph, e, C, 8),
+                 S(eye, 64 * h + 16 * m, 64 * h + 16 * m + 16), True, True) for e in range(8)])
+        act(S(spt, 512 * h, 512 * h + 512, 1, P32), S(PS[4 * h + 1], 0, 512, 1, P32))
 
-    Y = [B("y0", 0, L + C), B("y1", 0, L + C), B("y0", 0, L + C)]
+    dma("s", [(B("win", 0, L, 1, (16 * m, 16 * m + 1, 1)), S(spt, 128 * m, 128 * m + 128, 1, P32)) for m in range(8)], 6.0,
+        after=[names["q3"]])
+    lu0 = cp(new("su", C), B("spi", 0, C))
+    Y = [B("y0", 0, L + C), B("y1", 0, L), B("y2", 0, L)]
     II = [B("ii0", 0, L + C), B("ii1", 0, L + C), B("ii0", 0, L + C)]
     WIN = B("win", 0, NEG + 8)
     H0, HF = B("h0", 0, DUMP + 2 * C), B("hf", 0, DUMP + 2 * C)
@@ -595,26 +675,48 @@ def record(g, T, topo, rank):
     for x in (S(Fb, C, C + 2), S(Rx, 0, 1), S(Rx, C + 1, C + 2), S(Z1, 0, 2), S(Z2, 0, 2)):
         ms(x, 0.0)
     fill(S(H0, 0, NQ), 0, NQ // 2)
-    tmp, k1, k2 = f(C), f(C), f(C)
+    tmp, k1, k2, lim = f(C), f(C), f(C), tag0
+    part[0] = "lift"
+    lu = new("su", C)
+    for q in range(4):
+        o = S(PS[6], 64 * q, 64 * q + 64)
+        wrap(o, S(MK, 1024 * q + 1, 1024 * q + 1025), 64)
+        cp(S(lu, 64 * q, 64 * q + 64), tt(S(k2, 64 * q, 64 * q + 64), ts(S(k1, 64 * q, 64 * q + 64), o, 8.0, OP.is_lt, W + 1.0, OP.mult),
+                                          B("spi", 64 * q, 64 * q + 64), OP.max))
+    cp(IND(S(HF, 0, L + C), BOFF), S(II[1], L, L + C))
+    LEN1 = act(f(), LEN, bias=-1.0)
+    wrap(S(PS[7], 0, 16), ts(new("sh", C), IND(WIN, ts(new("su", 16), END, 1.0, OP.subtract)), row0, OP.mult), 16)
+    last = tt(f(), ts(f(), S(PS[7], 0, 16), SH, OP.add), ts(f(), LEN, 0.5, OP.is_lt, float(W), OP.mult), OP.max)
+    sf2, lt, lto, th2 = f(2 * C), new("sb", C), new("sb", 2 * C), f(32)
+    kf = S(sf2, 0, C)
+
+    def upto(t, a, lw):
+        none(at0[2], a, 0)
+        scan(AT[2], AT[0], AT[1], 0.0, OP.add, OP.min)
+        return tt(S(sf2, 0, C), IND(AUD[t], lw), act(tmp, IND(II[t], cp(new("su", 16), at[2]))), OP.add)
 
     def sums(t, onv):
         part[0] = "sums%d" % t
         for q in range(8):
-            src = IND(AUD[t], S(lu, 32 * q, 32 * q + 32))
-            (cp if q in onv else act)(S(Y[t], 512 * q, 512 * q + 512), src, line="y%d%d" % (t, q in onv))
-        act(tmp, IND(Y[t], BOFF))
-        tt(IND(Y[t], BOFF), tmp, G, OP.subtract)
+            src = IND(AUD[t], S(lu if t else lu0, 32 * q, 32 * q + 32))
+            act(S(Y[t], 512 * q, 512 * q + 512), src, q="v" if q in onv else "a", line="y%d%d" % (t, q in onv))
+        if t == 0:
+            tt(IND(Y[t], BOFF), act(kf, IND(Y[t], BOFF)), G, OP.subtract)
         half = 32 if t == 0 else 64
         for q in range(4):
             lo, hi = 1024 * q, 1024 * q + 1024
             for l in range(lo, hi, PIECE[t]):
                 h = l + PIECE[t]
-                scan(S(II[t], l, h), S(MK, l, h), S(Y[t], l, h), 0.0 if l == 0 else S(II[t], l - 1, l), OP.mult, OP.add)
-            mid = hi if q < 3 else lo + 16 * half
-            act(B("sg", lo, mid), S(II[t], lo, mid), AF.Sign, bias=0.5)
-            if mid < hi:
+                scan(S(II[t], l, h), S(HF if t else MK, l, h), S(Y[t], l, h), S(II[t], l - 1, l) if l else float(LIFT),
+                     OP.min if t else OP.mult, OP.add)
+            o = S(PS[0], 64 * q, 64 * q + 64) if q < 3 else S(PS[1], 0, 64)
+            if q < 3 or half == 64:
+                count(o, B("sg", lo, hi), 64, sign(B("sg", lo, hi), S(II[t], lo, hi)))
+            else:
+                mid = lo + 16 * half
+                act(B("sg", lo, mid), S(II[t], lo, mid), AF.Sign, bias=0.5)
                 ts(B("sg", mid, hi), S(II[t], mid, hi), 0.0, OP.is_lt)
-            wrap(S(PS[0], 64 * q, 64 * q + 64) if q < 3 else S(PS[1], 0, 64), B("sg", lo, hi), 64)
+                wrap(o, B("sg", lo, hi), 64)
         ts(S(Fb, 0, 192), S(PS[0], 0, 192), 2.5, OP.is_le)
         scan(S(Rx, 1, 193), S(onb, 0, 192), S(Fb, 0, 192), 0.0, OP.mult, OP.add)
         ts(S(Fb, 192, 192 + half), S(PS[1], 0, half), 2.5, OP.is_le)
@@ -625,7 +727,7 @@ def record(g, T, topo, rank):
         act(S(Z1, 2, C + 2), IND(Rx, KEND))
         mm([(S(PS[2], 0, C + 1), blk, S(Z2, 1, C + 2), True, False), (S(PS[2], 0, C + 1), blk, S(Z1, 1, C + 2), False, True)])
         o = S(PS[3], 0, C)
-        mm([(o, blk, S(Z2, 2, C + 2), True, False), (o, nblk, S(Z2, 1, C + 1), False, False),
+        mm([(o, blk, zr, True, False), (o, blk, S(Z2, 2, C + 2), False, False), (o, nblk, S(Z2, 1, C + 1), False, False),
             (o, blk, S(Z1, 2, C + 2), False, False), (o, nblk, S(Z1, 1, C + 1), False, True)])
         scan(k1, S(K, 0, C), S(PS[2], 0, C), 0.0, OP.max, OP.min)
         scan(k2, S(K, 0, C), S(PS[2], 1, C + 1), 0.0, OP.max, OP.min)
@@ -651,14 +753,14 @@ def record(g, T, topo, rank):
             fill(S(H0, 0, NQ), 0, NQ // 2)
         scan(hK, K, hA, 0.0, OP.max, OP.min)
         pos = place(S(hK, 15, NQ, 16), NQ // 16)
-        ts(relh, IND(WIN, pos), row0, OP.mult)
+        ts(relh, IND(WIN, pos), -SH, OP.max, row0, OP.mult)
         wrap(S(PS[7], 0, NQ // 16), relh, NQ // 16)
         ts(B("rs%d" % t, 0, NQ // 16), S(PS[7], 0, NQ // 16), SH, OP.add)
         tell("r", t)
         act(S(RW, NQ, NQ + C), IND(WIN, S(pos, 0, 16)))
 
-    Ed, off = f(64), f(64)
-    a, b, aK0 = at1[0], cut1[2], S(Ed, 32, 64, 2)
+    Ed, off, low = f(64), f(64), f(1)
+    a, b, aK0 = f(), cut1[2], S(Ed, 32, 64, 2)
 
     def release(t, x, nrel, thr1):
         n = 16 if t == 0 else 32
@@ -669,15 +771,13 @@ def record(g, T, topo, rank):
             tt(S(E, 0, 16), x, thr1, OP.is_le)
             tt(S(E, 16, 32), x, aK0, OP.is_le)
         tt(S(Ed, 1, 2 * n, 2), E, S(d2, 0, n), OP.mult)
-        total = prefix(S(PS[4], 1, 32, 2), S(PS[4], 40, 41), nrel, S(rxf, 0, 17), ntrif, nblkf)
+        total = prefix(S(PS[4], 1, 32, 2), S(PS[5], 40, 41), nrel, S(rxf, 0, 17), ntrif, nblkf)
         tt(S(off, 1, 32, 2), S(PS[4], 1, 32, 2), S(Ed, 1, 32, 2), OP.max)
         if t:
             scan(S(off, 32, 64), S(PS[4], 0, 32), S(Ed, 32, 64), 0.0, OP.add, OP.max)
         offu = cp(new("su", n), S(off, 1, 2 * n, 2))
-        total()
-        R = cp(B("cs%d" % t, 2, 3), S(PS[4], 40, 41))
         lookup(t, offu, n)
-        return R
+        return total
 
     def stay(t, R):
         total = prefix(S(PS[4], 64, 80), S(PS[4], 80, 81), b, S(rxf, 20, 37), ntrif, nblkf)
@@ -686,13 +786,17 @@ def record(g, T, topo, rank):
         n = 17 if t == 2 else 16
         return ts(f(n), S(PS[4], 64, 64 + n), act(f(1), R, scale=-1.0, bias=float(L)), OP.add)
 
-    def shorts(t, R, LP):
+    def shorts(t, total):
+        total()
         prefix(S(PS[5], 0, 16), S(PS[5], 16, 17), sh, rxs, tri, blk)()
-        ts(B("cs%d" % t, 1, 2), S(PS[5], 16, 17), R, OP.min, act(f(1), R, bias=-float(SLOT)), OP.max)
-        st = dict(R=R, LP=LP, S=cp(B("cs%d" % t, 0, 1), S(PS[5], 16, 17)))
+        R = cp(B("cs%d" % t, 2, 3), S(PS[5], 40, 41))
+        ts(low, S(PS[5], 40, 41), float(SLOT), OP.subtract)
+        ts(B("cs%d" % t, 1, 2), S(PS[5], 16, 17), R, OP.min, low, OP.max)
+        st = dict(R=R, S=cp(B("cs%d" % t, 0, 1), S(PS[5], 16, 17)))
         tell("c", t)
+        LP = st["LP"] = stay(t, R)
         sr = st["sr"] = ts(f(), S(PS[5], 0, 16), R, OP.subtract)
-        st["own"] = tt(f(), act(f(), sr, bias=act(f(1), R, bias=float(NQ))), act(f(), sr, AF.Relu, scale=-BIG), OP.min)
+        st["own"] = tt(f(), act(f(), sr, bias=act(f(1), R, bias=float(NQ))), none(f(), sr, -1), OP.min)
         nc1 = tt(cut1[1], sr, S(LP, 0, 16), OP.subtract)
         tight = ts(f(), tt(f(), nc1, b, OP.add), -0.5, OP.is_gt, BIG, OP.mult)
         st["srs"] = tt(f(), tt(f(), act(f(), sh, scale=-BIG, bias=cbig), sr, OP.add), tight, OP.add)
@@ -709,33 +813,37 @@ def record(g, T, topo, rank):
         act(slot(t), IND(RW, qu))
 
     M = sums(0, ONV[0])
-    x = tt(f(), act(f(), LEN, bias=-1.0), M, OP.add)
+    x = tt(f(), LEN1, M, OP.add)
     nrel = ts(f(), x, -1.0, OP.mult, 0.0, OP.min)
     ts(sh, x, 0.0, OP.is_lt)
     R = release(0, x, nrel, None)
     act(a, tt(b, LEN, nrel, OP.add))
-    st, n, n0 = shorts(0, R, stay(0, R)), None, None
-    fill(S(HF, 0, L), 0)
+    st, n, n0 = shorts(0, R), None, None
 
-    iia, lt, lto = f(C), new("sb", C), new("sb", C)
+    act(S(th2, 0, 16), LEN, scale=0.0, bias=2.5)
     for t in (1, 2):
         z, Rb = B("ci%d" % (t - 1), 1, 2), B("ci%d" % (t - 1), 2, 3)
         M = sums(t, ONV[t])
-        act(at0[2], a, AF.Relu, scale=-BIG, bias=cbig)
-        scan(AT[2], AT[0], AT[1], 0.0, OP.add, OP.min)
-        sofar = act(iia, IND(II[t], cp(new("su", 16), at[2])))
-        nK = tt(cut0[4] if t == 1 else f(), M, act(f(), a, scale=-1.0), OP.max)
-        if t == 2:
+        lw = cp(new("su", 16), tt(f(), ts(f(), tt(f(), a, LEN, OP.subtract), -0.5, OP.is_lt, float(W), OP.mult), last, OP.max))
+        sofar = upto(t, tt(at1[0], a, LEN1, OP.min), lw)
+        nK = tt(f(), M, act(f(), a, scale=-1.0, bias=1.0), OP.max)
+        if t == 1:
+            count(S(PS[0], 0, 16), S(lto, 0, C), 16, sign(S(lto, 0, C), sofar))
+            more = ts(f(), S(PS[0], 0, 16), 2.5, OP.is_le)
+        else:
             ew = ts(new("su", 16), tt(f(), e0, n, OP.mult), float(W), OP.add)
-            sofar = tt(tmp, IND(AUD[2], ew), iia, OP.add)
-            wrap(S(PS[0], 0, 16), act(lto, sofar, AF.Sign, bias=0.5), 16)
-            nK = tt(cut0[4], nK, tt(f(), S(PS[0], 0, 16), act(f(), n, scale=101.5, bias=-99.0), OP.is_le), OP.subtract)
+            sofar = tt(S(sf2, C, 2 * C), IND(AUD[2], ew), sofar, OP.add)
+            wrap(S(PS[0], 0, 32), act(lto, sf2, AF.Sign, bias=0.5), 32)
+            mm([(S(PS[0], C, 2 * C), blk, S(lto, 0, C), True, True)])
+            act(S(th2, 16, 32), n, scale=101.5, bias=-99.0)
+            both = tt(f(32), S(PS[0], 0, 32), th2, OP.is_le)
+            more = tt(f(), S(both, 0, 16), S(both, 16, 32), OP.add)
+            tt(S(pack[2], C, 2 * C), S(PS[0], C, 2 * C), lim, OP.is_le)
+            fill(S(HF, 0, L), 0)
+        nK = tt(cut0[4], nK, more, OP.subtract)
         aK = tt(f(), a, nK, OP.add)
-        act(aK0, aK, AF.Relu, bias=-1.0)
+        either(aK0, aK, AF.Relu, -1.0, 1.0, -1.0, OP.add, 0.0, OP.max)
         thr1 = ts(f(), aK, 1.5, OP.is_lt, BIG, OP.mult)
-        if t == 2:
-            spread(PS[0], tt(new("sb", 16), ts(f(), aK, 0.5, OP.is_ge), n, OP.mult), 16)
-            act(S(pack[2], C, 2 * C), S(PS[0], 0, C), scale=-1.0, bias=1.0)
         ts(cut1[0], S(st["LP"], 0, 16), z, OP.add, Rb, OP.subtract)
         ns = ts(cut0[3], st["srs"], z, OP.add, Rb, OP.is_ge)
         scan(CUT[2], CUT[0], CUT[1], 0.0, OP.subtract, OP.min)
@@ -746,7 +854,7 @@ def record(g, T, topo, rank):
         tt(lt, IND(AX, qu), sofar, OP.is_gt)
         arrive(t - 1, qu)
         if t == 1:
-            wrap(S(PS[6], 0, 16), ts(new("sh", C), slot(0), row0, OP.mult), 16)
+            wrap(S(PS[6], 0, 16), ts(new("sh", C), slot(0), -SH, OP.max, row0, OP.mult), 16)
             e0 = ts(f(), S(PS[6], 0, 16), SH, OP.subtract)
         thr = tt(f(), ts(f(), x, -0.5, OP.is_gt, 100.0, OP.mult), act(f(), ns, scale=93.5, bias=-93.5), OP.add)
         wrap(S(PS[5], 0, 16), lt, 16)
@@ -757,7 +865,10 @@ def record(g, T, topo, rank):
         act(b, tt(f(), nrel, cut[3], OP.subtract), bias=1.0)
         tt(a, b, a, OP.min)
         n0, n = n, tt(f(), b, a, OP.subtract)
-        st = shorts(t, R, stay(t, R))
+        if t == 1:
+            spread(PS[6], act(new("sb", 16), n), 16)
+            act(lim, S(PS[6], 0, C), scale=-96.5, bias=99.0)
+        st = shorts(t, R)
 
     part[0] = "end"
     z, Rb = B("ci2", 1, 2), B("ci2", 2, 3)
@@ -769,16 +880,21 @@ def record(g, T, topo, rank):
     tt(S(PR, 16, 32), S(PR, 0, 16), a, OP.add)
     PM = act(S(FIN[0], 1, 32, 2), cut1[1], bias=float(L))
     tt(S(FIN[0], 33, 64, 2), PM, a, OP.add)
-    tt(S(FIN[1], 1, 32, 2), act(f(), a, AF.Relu, scale=-BIG, bias=cbig), S(d2, 0, 16), OP.min)
-    D2 = tt(f(), act(f(), n, AF.Relu, scale=-BIG, bias=cbig), S(d2, 16, 32), OP.min)
+    tt(S(FIN[1], 1, 32, 2), none(f(), a, 0), S(d2, 0, 16), OP.min)
+    D2 = tt(f(), none(f(), n, 0), S(d2, 16, 32), OP.min)
     tg = act(f(1), S(st["LP"], 16, 17), scale=-1.0, bias=act(f(1), pg, scale=16.0, bias=float(L)))
-    SR = ts(f(1), st["S"], R, OP.subtract)
+    SR = ts(f(1), st["S"], st["R"], OP.subtract)
     b1 = act(f(), b, bias=1.0 - 2048.0)
     ns = ts(f(), st["srs"], z, OP.add, Rb, OP.is_ge)
     ts(fin1[0], PR, z, OP.subtract, Rb, OP.add)
     tt(S(FIN[1], 33, 64, 2), ns, D2, OP.mult)
     scan(FIN[2], FIN[0], FIN[1], 0.0, OP.min, OP.max)
-    tt(IND(HF, cp(new("su", 32), fin[1])), pack[3], spack, OP.add)
+    vi = cp(new("si", 32), fin[1])
+    ts(turn0[1], fin[1], L - 0.5, OP.is_lt, 240.0, OP.mult)
+    tt(fin[0], ts(new("si", 32), vi, 4, OP.logical_shift_right, 15, OP.bitwise_and), ts(new("si", 32), vi, 8, OP.logical_shift_right),
+       OP.subtract)
+    scan(TURN[2], TURN[0], FIN[2], 0.0, OP.mult, OP.add)
+    tt(IND(HF, cp(new("su", 32), turn[1])), pack[3], spack, OP.add)
     qu = given(2, st)
     q3 = ts(f(1), ts(f(1), Rb, z, OP.subtract, SR, OP.min), tg, OP.add)
     ev = ts(k1, jv, q3, OP.is_ge, float(1024 * TAG - 1), OP.mult)
@@ -787,24 +903,33 @@ def record(g, T, topo, rank):
     spread(PS[3], yh, 16)
     act(k2, S(PS[3], 0, C), bias=2048.0)
     dma("s", [(T.yn[:], S(k2, 0, C, 1, ROW))])
-    IB, DG, OUT = II[1], Y[1], Y[0]
-    for q in range(4):
-        lo = 1024 * q
-        scan(S(IB, lo, lo + 1024), onb, S(HF, lo, lo + 1024), -1.0 if q == 0 else S(IB, lo - 1, lo), OP.add, OP.max)
+    HB, run, DG, OUT = tmp, S(sf2, 0, C), G, II[1]
+    dma("s", [(HB, S(HF, 0, L, 1, ROW))], 2.8)
+    scan(run, inc, HB, 0.0, OP.add, OP.max)
+
+    def turn_(o, x):
+        op("v", [x], [o], lambda: [g.vector.transpose(ap(o), ap(x))], cost(o, [x]))
+        return o
+
+    tt(S(nb, 0, 16), S(run, 15, C, 16), jend, OP.subtract)
+    nt = turn_(f(32), nb)
+    for h in (0, 16):
+        scan(S(up, h + 1, h + 16), S(nt, h, h + 15), S(zb, 0, 15), 0.0, OP.max, OP.max)
+        top_ = f(1)
+        op("v", [S(nt, h, h + 16)], [top_], (lambda o, x: lambda: [g.vector.tensor_reduce(ap(o), ap(x), AX_.X, OP.max)])(top_, S(nt, h, h + 16)),
+           64 * CY)
+        ts(S(up, 32 + h, 48 + h), S(zb, 0, 16), top_, OP.max)
+    back = turn_(f(64), up)
+    first = tt(f(), tt(f(), S(back, 0, 16), S(back, 31, 47), OP.max), j0, OP.add)
+    for k in range(16):
+        scan(S(DG, k, C, 16), S(onb, 0, 16), S(HB, 16 * k, 16 * k + 16), S(first, k, k + 1), OP.add, OP.max)
     arrive(2, qu)
-    act(slot(4), IND(RW, qu))
+    act(slot(4), IND(RW, qu), q="v")
     for q in range(4):
         lo = 1024 * q
-        for i in range(4 * q, 4 * q + 4):
-            scan(S(DG, C * i, C * i + C), S(K, 0, C), S(IB, i, L, 16), 0.0, OP.max, OP.min)
-        pos = place(S(DG, lo + 15, lo + 1024, 16), 64, S(ev, 64 * q, 64 * q + 64))
+        pos = place(S(DG, 64 * q, 64 * q + 64), 64, S(ev, 64 * q, 64 * q + 64))
         for h in range(2):
             o, src = S(OUT, lo + 512 * h, lo + 512 * h + 512), IND(WIN, S(pos, 32 * h, 32 * h + 32))
-            onv = q == 3 and h == 1 or q == 2 and h == 1
-            if onv:
-                ts(o, src, SH, OP.add)
-            else:
-                act(o, src, bias=SH)
-            dma("a" if q == 3 and not onv else "s",
-                [(T.yo[i:128:16, :], S(OUT, C * i, C * i + C, 1, ROW)) for i in range(4 * q + 2 * h, 4 * q + 2 * h + 2)])
+            act(o, src, bias=SH, q="av"[h])
+            dma("s", [(T.yo[i:128:16, :], S(OUT, C * i, C * i + C, 1, ROW)) for i in range(4 * q + 2 * h, 4 * q + 2 * h + 2)])
     return ops, names, sent

import math
import numpy as np
from concourse.bass import DstId, RemoteDMATransfer
from concourse.mybir import AluOpType as OP, ActivationFunctionType as AF, AxisListType as AX_

N, W, L, C, SLOT = 8, 3072, 4096, 256, 192
NQ = C + SLOT
SH = 1536.0
NS = 5
NEG = L + NS * C
DUMP = L + C
TAG = 8192
BIG, LIFT = 1.0e5, 1 << 21
QW, EW = W // 4, W // 8
F32, BF, F16, I32, U16 = "float32", "bfloat16", "float16", "int32", "uint16"
CY, GATH, SCAT, GAP, NEAR, FAR = 0.83e-3 * 1.1, 1.56, 3.8, 0.12, 2.5, 5.0
PLAN, SEED, TRIES, MOVES = {}, 1, 1, 100000
LEAD = {"set": 100.0, "sums0": 100.0, "visit0": 80.0, "lift": 70.0, "sums1": 60.0, "visit1": 40.0, "sums2": 20.0}
HEAT, SETS = 0.25, 1
FLY = [((5.1, 6.3, 6.3, 7.4), (9.0, 10.3, 10.3, 11.6)), (6.0, 11.0)]
PIECE = [1024, 512, 512]
ONV = [(4, 5, 6, 7), (), ()]

SCRATCH = {
    "win": ("sbuf", [128, NEG + 16], F32), "h0": ("sbuf", [128, DUMP + 2 * C], F32), "hf": ("sbuf", [128, DUMP + 2 * C], F32),
    "mk": ("sbuf", [128, L + C], BF), "sg": ("sbuf", [128, L], BF), "rs": ("sbuf", [128, 2048], BF),
    "sf": ("sbuf", [128, 11900], F32), "sb": ("sbuf", [128, 5800], BF), "sh": ("sbuf", [128, 1700], F16),
    "si": ("sbuf", [128, 1200], I32), "su": ("sbuf", [128, 1200], U16),
    "spi": ("sbuf", [128, C], I32), "gi": ("sbuf", [128, C], I32), "li": ("sbuf", [128, C], I32),
}
for _t in range(3):
    SCRATCH["aud%d" % _t] = ("sbuf", [128, W + 16], BF)
    for _r in "si":
        SCRATCH["c%s%d" % (_r, _t)] = ("sbuf", [128, 4], F32)
        SCRATCH["r%s%d" % (_r, _t)] = ("sbuf", [128, 32], U16)
SCRATCH["y0"] = ("sbuf", [128, L + C], F32)
SCRATCH["y1"] = ("sbuf", [128, L], BF)
SCRATCH["y2"] = ("sbuf", [128, L], BF)
for _t in range(2):
    SCRATCH["ii%d" % _t] = ("sbuf", [128, L + C], F32)
for _b in range(8):
    SCRATCH["ps%d" % _b] = ("psum", [128, 512], F32)

POOLS = {"v": 58, "a": 30, "t": 22, "g": 12, "d": 9}
ARR = ["q0", "q1", "q2", "q3", "a2"] + ["%s%d" % (k, t) for t in range(3) for k in "cr"]
SEMAPHORES = ["%s%d" % (e, i) for e in POOLS for i in range(POOLS[e])] + ["r" + a for a in ARR] + ["l%d" % k for k in range(5)] + ["sent"]
COLS = {"c": 3, "r": NQ // 16}


def bits(engs):
    return sum(1 << e for e in engs)


def ports(T, topo, r):
    src, far = T.cores[r], T.cores[(r - 2) % N]
    return sorted((c for c in topo.cores_of(src) if T.rank_of(c) is None and topo.may_write(c, far)),
                  key=lambda c: topo.die(c) == topo.die(src))


def direct(T, topo, r):
    return topo.may_write(T.cores[r], T.cores[(r + 1) % N])


def hop(T, topo, r, kind):
    if direct(T, topo, r):
        return T.cores[(r + 1) % N]
    return [c for c in ports(T, topo, r) if topo.die(c) == topo.die(T.cores[r])]["cr".index(kind)]


def transfer(T, topo, core, dst, engs, src, out, sem):
    rid, pid = topo.addr(dst, core)
    return RemoteDMATransfer(dst_ids=[DstId(rid=rid, pnc=pid)], dma_engine_mask=bits(engs), remote_sem=T.sem[sem], src=src, dst=out)


def relay_program(g, core, T, topo):
    n = 0
    mine = [r for r in range(N) if core in ports(T, topo, r)]
    for r in mine:
        if direct(T, topo, r):
            j = ports(T, topo, r).index(core)
            dst = T.cores[(r - 1) % N]
            jobs = [("rq%d" % k, 8, T.aud1[:, EW * p:EW * p + EW], "rq%d" % (p // 2)) for k, p in enumerate((j, j + 4))]
            jobs.append(("ra2", 16, T.aud2[:, QW * j:QW * j + QW], "ra2"))
            for sem, count, b, there in jobs:
                g.wait_ge(T.sem[sem], count)
                g.remote_dma_fused([transfer(T, topo, core, dst, topo.engines(core, dst), b, b, there)], local_sem=T.sem.sent)
                n += 8
    for t in range(3):
        for r in mine:
            for k in "cr":
                if hop(T, topo, r, k) == core:
                    dst, b = T.cores[(r + 1) % N], T["%si%d" % (k, t)][:, 0:COLS[k]]
                    g.wait_ge(T.sem["r%s%d" % (k, t)], 16)
                    g.remote_dma_fused([transfer(T, topo, core, dst, topo.engines(core, dst), b, b, "r%s%d" % (k, t))], local_sem=T.sem.sent)
                    n += 8
    if n:
        g.wait_ge(T.sem.sent, n)


def schedule(both):
    n0 = len(both[0][0])
    ops = both[0][0] + both[1][0]
    n = len(ops)
    pre, qs = [], []
    for i, o in enumerate(ops):
        k = int(i >= n0)
        p = {j + k * n0 for j in o["need"] | o["after"]}
        p |= {both[kk][1][name] + kk * n0 for kk, name in o["link"]}
        pre.append(sorted(p))
        qs.append(5 * k + "vatgs".index(o["q"]) if o["q"] else 10)
    hard = [[j for j in pre[i] if (qs[j] != qs[i] and "alt" not in ops[j]) or j - int(i >= n0) * n0 in ops[i]["need"]] for i in range(n)]
    post = [[] for _ in ops]
    for i in range(n):
        for j in pre[i]:
            post[j].append(i)
    left = [len(p) for p in pre]
    topo_ = [i for i in range(n) if not left[i]]
    for i in topo_:
        for j in post[i]:
            left[j] -= 1
            if not left[j]:
                topo_.append(j)
    at = {i: k for k, i in enumerate(topo_)}
    rank_ = [0.0] * n
    for i in reversed(topo_):
        rank_[i] += ops[i]["busy"] + ops[i]["lat"] + GAP
        for j in pre[i]:
            rank_[j] = max(rank_[j], rank_[i])

    def plan(prio, back=False):
        start, end, slots = [0.0] * n, [0.0] * n, [[] for _ in range(10)]
        up, down = (post, pre) if back else (pre, post)
        left = [len(p) for p in up]
        ready = [i for i in range(n) if not left[i]]
        while ready:
            i = max(ready, key=lambda i: prio[i])
            ready.remove(i)
            o = ops[i]
            t = max([end[j] + (GAP if (i in hard[j] if back else j in hard[i]) else 0.0) for j in up[i]] + [0.0])
            t += o["lat"] if back else 0.0
            if qs[i] < 10:
                sl = slots[qs[i]]
                k = 0
                for a, b in sl:
                    if b > t:
                        if t + o["busy"] <= a:
                            break
                        t = b
                    k += 1
                sl.insert(k, (t, t + o["busy"]))
            start[i], end[i] = t, t + o["busy"] + (0.0 if back else o["lat"])
            for j in down[i]:
                left[j] -= 1
                if not left[j]:
                    ready.append(j)
        return end, sorted(range(n), key=lambda i: (start[i], at[i]))

    sets = ((0.93, 0.93, 1.0, 1.0, 0.135), (1.2, 1.4, 1.2, 1.4, 0.16))[:SETS]
    busy = [[o["busy"] * (s[1] if o["ind"] else s[0]) for o in ops] for s in sets]
    lat = [[o["lat"] * (s[3] if o["lat"] > FAR and not o["q"] else s[2]) + s[4] for o in ops] for s in sets]

    def run(order, s, a=0, known=None):
        end, free, bs, ls = list(known) if a else [0.0] * n, [0.0] * 11, busy[s], lat[s]
        for i in order[:a]:
            free[qs[i]] = end[i] - ls[i]
        free[10] = 0.0
        for i in order[a:]:
            q = qs[i]
            t = free[q]
            for j in hard[i]:
                if end[j] > t:
                    t = end[j]
            t += bs[i]
            if q < 10:
                free[q] = t
            end[i] = t + ls[i]
        return end

    soon = [i + k * n0 for k in range(2) for name, i in both[k][1].items() if name[0] in "qf"]

    def span(order, a=0, known=None):
        ends = [run(order, s, a, known[s] if a else None) for s in range(len(sets))]
        return sum(max(e) + 0.05 * sum(e) / n + 0.05 * sum(e[i] for i in soon) for e in ends), ends

    def held(order, end, s):
        before, last = {}, {}
        for i in order:
            before[i] = last.get(qs[i])
            last[qs[i]] = i
        i, out = max(range(n), key=lambda i: end[i]), []
        while True:
            t = end[i] - lat[s][i] - busy[s][i]
            p = [j for j in hard[i] if end[j] >= t - 1e-9]
            if p:
                i = p[0]
            elif qs[i] < 10 and before[i] is not None and t > 1e-9:
                out.append((before[i], i))
                i = before[i]
            else:
                return out

    rng = np.random.default_rng(SEED)
    best, p = None, [rank_[i] + LEAD.get(ops[i]["part"], 0.0) for i in range(n)]
    for it in range(TRIES):
        end, cand = plan(p)
        v, ends = span(cand)
        if best is None or v < best:
            best, order, ee = v, cand, ends
        p = [x + float(y) for x, y in zip(plan(end, True)[0], rng.normal(0, 0.3, n))]
    def flip(i):
        qs[i] ^= 1 if qs[i] < 5 else 3
        for s in range(len(sets)):
            busy[s][i] = ops[i]["alt"]["va"[qs[i] % 5]][1] * sets[s][int(ops[i]["ind"])]

    cur, top, keep, keepq = best, best, order, list(qs)
    pairs, dice, far, slack = None, rng.random((MOVES, 3)).tolist(), rng.geometric(0.4, MOVES).tolist(), rng.exponential(1.0, MOVES).tolist()
    for it in range(MOVES):
        if pairs is None:
            pairs = [x for s in range(len(sets)) for x in held(order, ee[s], s)]
        u, v = pairs[int(dice[it][0] * len(pairs))]
        a, b = order.index(u), order.index(v)
        w = (u, v)[dice[it][1] < 0.5]
        if dice[it][2] < 0.25 and "alt" in ops[w]:
            flip(w)
            val, ends = span(order, a if w == u else b, ee)
            if val <= cur + HEAT * (1.0 - it / MOVES) * slack[it]:
                cur, ee, pairs = val, ends, None
                order = sorted(order, key=lambda i: ends[0][i] - lat[0][i] - busy[0][i])
                if cur < top:
                    top, keep, keepq = cur, order, list(qs)
            else:
                flip(w)
            continue
        if dice[it][1] < 0.5:
            same = [k for k in range(max(0, a - 150), a + 1) if qs[order[k]] == qs[v]]
            a = same[max(0, len(same) - far[it])]
            seg, take = order[a:b + 1], {v}
            for i in reversed(seg):
                if i in take:
                    take.update(pre[i])
            if seg[0] in take:
                continue
            seg = [i for i in seg if i in take] + [i for i in seg if i not in take]
        else:
            same = [k for k in range(b, min(n, b + 150)) if qs[order[k]] == qs[v]]
            b = same[min(len(same), far[it]) - 1]
            seg, take = order[a:b + 1], {u}
            for i in seg:
                if i in take:
                    take.update(post[i])
            if seg[-1] in take:
                continue
            seg = [i for i in seg if i not in take] + [i for i in seg if i in take]
        cand = order[:a] + seg + order[b + 1:]
        val, ends = span(cand, a, ee)
        if val <= cur + HEAT * (1.0 - it / MOVES) * slack[it]:
            cur, ee, pairs = val, ends, None
            order = sorted(cand, key=lambda i: ends[0][i] - lat[0][i] - busy[0][i])
            if cur < top:
                top, keep, keepq = cur, order, list(qs)
    for i in range(n):
        if qs[i] != keepq[i]:
            flip(i)
    PLAN["us"] = [max(e) for e in span(keep)[1]]
    return [[(i, "vatgs-"[qs[i] % 5]) for i in keep if i < n0], [(i - n0, "vatgs-"[qs[i] % 5]) for i in keep if i >= n0]]


def rank_program(g, core, T, topo):
    rank = T.rank_of(core)
    if rank is None:
        relay_program(g, core, T, topo)
        return
    if "order" not in PLAN:
        kinds = [[r for r in range(N) if direct(T, topo, r) == d][0] for d in (True, False)]
        PLAN["order"] = schedule([record(g, T, topo, r) for r in kinds])
    ops, names, sent = record(g, T, topo, rank)
    order = [i for i, q in PLAN["order"][0 if direct(T, topo, rank) else 1]]
    for i, q in PLAN["order"][0 if direct(T, topo, rank) else 1]:
        if "alt" in ops[i]:
            ops[i].update(q=q, pool=q, emit=ops[i]["alt"][q][0])
    Q = {"v": g.vector, "a": g.scalar, "t": g.tensor, "g": g, "s": g.sync}
    known, last, waited, done = {q: set() for q in Q}, {}, {}, {}
    pos_ = {i: k for k, i in enumerate(order)}

    def wait(q, i):
        if i in known[q] or ops[i]["pool"] == "-":
            return
        sem, val, snap = done[i]
        Q[q].wait_ge(T.sem[sem], val)
        waited[sem] = max(waited.get(sem, 0), val)
        known[q].add(i)
        known[q].update(snap)

    for i in order:
        o = ops[i]
        q, pool = o["q"], o["pool"]
        if q is None:
            done[i] = (pool, o["inc"], frozenset())
            last[pool] = [o["inc"], i]
            continue
        for j in sorted(o["need"], key=lambda j: -pos_[j]):
            wait(q, j)
        if pool == "-":
            o["emit"]()
            continue
        pn = ["%s%d" % (pool, k) for k in range(POOLS[pool])]
        free = [s for s in pn if s not in last or last[s][1] in known[q]]
        if not free:
            free = [min(pn, key=lambda s: pos_[last[s][1]])]
            wait(q, last[free[0]][1])
        s = free[0]
        val = last[s][0] if s in last else 0
        for ins in o["emit"]():
            ins.then_inc(T.sem[s], o["inc"])
            val += o["inc"]
        last[s] = [val, i]
        done[i] = (s, val, frozenset(known[q]))
    g.wait_ge(T.sem.sent, sent[0])
    for s in sorted(last, key=lambda s: pos_[last[s][1]]):
        if waited.get(s, 0) < last[s][0]:
            wait("g", last[s][1])


def record(g, T, topo, rank):
    core = T.cores[rank]
    near = direct(T, topo, rank)
    me = 0 if near else 1
    Q = {"v": g.vector, "a": g.scalar, "t": g.tensor, "g": g, "s": g.sync}
    ops, acc, bank, names, sent, chain, part = [], {}, {}, {}, [0], {}, ["set"]
    top = {"sf": 0, "sb": 0, "sh": 0, "si": 0, "su": 0}

    def new(buf, n):
        u = 8 if buf in ("sf", "si") else 16
        c = top[buf]
        top[buf] = c + (n + u - 1) // u * u
        assert top[buf] <= SCRATCH[buf][1][1], buf
        return (buf, c, c + n, 1, None)

    def f(n=16):
        return new("sf", n)

    def B(name, a, b, step=1, p=None):
        return (name, a, b, step, p)

    def S(x, a, b, step=1, p=None):
        return (x[0], x[1] + a, x[1] + b, step, p)

    def IND(w, off):
        return ("ind", w, off)

    def ap(x):
        if not isinstance(x, tuple):
            return x
        if x[0] == "ind":
            return ap(x[1]).indirect(ap(x[2]))
        p = x[4] or (0, 128, 1)
        ps = slice(p[0], p[1]) if p[2] == 1 else slice(p[0], p[1], p[2])
        cs = slice(x[1], x[2]) if x[3] == 1 else slice(x[1], x[2], x[3])
        return T[x[0]][ps, cs]

    def op(q, rd, wr, emit, busy, lat=0.0, pool=None, inc=1, after=(), link=(), line=None, group=False):
        tt_ = []
        for x, w in [(x, False) for x in rd] + [(x, True) for x in wr]:
            if not isinstance(x, tuple):
                continue
            if x[0] == "ind":
                tt_ += [(x[1], w, False), (x[2], False, False)]
            else:
                tt_.append((x, w, w and x[3] == 1 and x[4] is None))
        reg = [(x[0], x[1], x[2], x[3], w, all_) for x, w, all_ in tt_]
        need, after = set(), set(after)
        for b, c0, c1, st, w, all_ in reg:
            for d0, d1, sd, i, v in acc.get(b, []):
                if (w or v) and d0 < c1 and c0 < d1 and (c0 - d0) % math.gcd(st, sd) == 0:
                    if q == "t" and ops[i]["q"] == "t" and group:
                        after.add(i)
                    else:
                        need.add(i)
        i = len(ops)
        for b in {r[0] for r in reg if r[0].startswith("ps")}:
            eng, cur, old = bank.get(b, (q, [], []))
            if eng != q:
                eng, cur, old = q, [], cur
            need.update(old)
            if q == "t":
                after.update(cur[-1:])
            bank[b] = (eng, cur + [i], old)
        if line:
            after.update(chain.get(line, []))
            chain[line] = [i]
        ind = any(isinstance(x, tuple) and x[0] == "ind" for x in list(rd) + list(wr))
        ops.append(dict(q=q, ind=ind, need=need, after=after, link=list(link), emit=emit, busy=busy, lat=lat, pool=pool or q, inc=inc,
                        part=part[0]))
        for b, c0, c1, st, w, all_ in reg:
            if all_:
                acc[b] = [e for e in acc.get(b, []) if not (c0 <= e[0] and e[1] <= c1)]
        for b, c0, c1, st, w, all_ in reg:
            acc.setdefault(b, []).append((c0, c1, st, i, w))
        return i

    def wd(x):
        return 16 * wd(x[2]) if x[0] == "ind" else (x[2] - x[1] + x[3] - 1) // x[3]

    def two(x):
        return SCRATCH[x[0]][2] in (BF, F16, U16)

    def cost(o, ins, per=None):
        if o[0] == "ind":
            return 0.05 + wd(o) * SCAT * CY
        if ins and ins[0][0] == "ind":
            return 0.05 + wd(o) * GATH * CY
        if per is None:
            per = 0.5 if all(two(x) for x in [o] + ins) else 1.0
        return max(64, wd(o) * per) * CY

    def cp(o, a, line=None):
        op("v", [a], [o], lambda: [g.vector.tensor_copy(ap(o), ap(a))], cost(o, [a]), line=line)
        return o

    def tt(o, a, b, fn):
        op("v", [a, b], [o], lambda: [g.vector.tensor_tensor(ap(o), ap(a), ap(b), fn)], cost(o, [a, b], 1 if a[0][:2] == "ps" else 2))
        return o

    def ts(o, a, s1, f1, s2=None, f2=None):
        if f2 is None:
            op("v", [a, s1], [o], lambda: [g.vector.tensor_scalar(ap(o), ap(a), ap(s1), None, f1)], cost(o, [a]))
        else:
            op("v", [a, s1, s2], [o], lambda: [g.vector.tensor_scalar(ap(o), ap(a), ap(s1), ap(s2), f1, f2)], cost(o, [a]))
        return o

    def scan(o, d0, d1, init, f0, f1):
        op("v", [d0, d1, init], [o], lambda: [g.vector.tensor_tensor_scan(ap(o), ap(d0), ap(d1), ap(init), f0, f1)], cost(o, [d0, d1]))
        return o

    def ms(o, c):
        op("v", [], [o], lambda: [g.vector.memset(ap(o), c)], cost(o, []))
        return o

    def sca(o, a, fn=AF.Identity, bias=0.0, scale=1.0, line=None):
        op("a", [a, bias], [o], lambda: [g.scalar.activation(ap(o), ap(a), fn, bias=ap(bias), scale=scale)], 0.05 + cost(o, [a], 1),
           line=line)
        return o

    def either(o, a, fn, bias, scale, s1, f1, s2, f2, q="a", line=None):
        i = len(ops)
        sca(o, a, fn, bias, scale, line)
        ops[i]["alt"] = {"a": (ops[i]["emit"], ops[i]["busy"]),
                         "v": (lambda: [g.vector.tensor_scalar(ap(o), ap(a), ap(s1), ap(s2), f1, f2)], cost(o, [a]))}
        ops[i]["q"] = ops[i]["pool"] = q
        ops[i]["emit"], ops[i]["busy"] = ops[i]["alt"][q]
        return o

    def act(o, a, fn=AF.Identity, bias=0.0, scale=1.0, q="a", line=None):
        if fn == AF.Identity and a[0][:2] != "ps":
            return either(o, a, fn, bias, scale, scale, OP.mult, bias, OP.add, q, line)
        return sca(o, a, fn, bias, scale, line)

    def none(o, a, at_):
        return either(o, a, AF.Relu, cbig if at_ == 0 else 0.0, -BIG, at_ + 0.5, OP.is_lt, BIG, OP.mult)

    def sign(o, a, q="a"):
        either(o, a, AF.Sign, 0.5, 1.0, 0.0, OP.is_ge, 0.5, OP.subtract, q)
        return len(ops) - 1

    def mm(items):
        op("t", [x for m in items for x in m[1:3]], [m[0] for m in items],
           lambda: [g.tensor.matmul(ap(o), ap(l), ap(r), a, z) for o, l, r, a, z in items],
           sum(max(64, wd(m[2])) * (1 if two(m[2]) else 4) * CY for m in items), group=not items[0][3])

    def iota(o, pat, base, cm):
        if o[0] == "si":
            op("g", [], [o], lambda: [g.iota(ap(o), pat, base, cm)], 0.13 + 2 * wd(o) * CY)
        else:
            op("g", [], [o], lambda: [g.iota(ap(o), pat, base, cm, allow_small_or_imprecise_dtypes=True)], 0.13 + 2 * wd(o) * CY)

    def pick(o, a, pat, fn, base, cm):
        op("g", [a], [o], lambda: [g.affine_select(ap(o), ap(a), pat, fn, 0.0, base, cm)], 0.17 + 2 * wd(o) * CY)

    def fill(o, c, step=256):
        for lo in range(0, wd(o), step):
            hi = min(wd(o), lo + step)
            iota(S(o, lo, hi), [[0, hi - lo]], c, 0)

    def dma(q, pairs, us=2.1, line=None, after=(), also=()):
        op(q, [a for o, a in pairs] + list(also), [o for o, a in pairs], lambda: [Q[q].dma_start(ap(o), ap(a)) for o, a in pairs],
           0.1 * len(pairs), us, pool="d", inc=16, line=line, after=after)

    def send(name, line, *trs):
        def emit():
            g.remote_dma_fused([transfer(T, topo, core, d, e, ap(a), ap(o), s) for a, d, e, o, s in trs], local_sem=T.sem.sent)
            sent[0] += sum(len(x[2]) for x in trs)
        names[name] = op("g", [x[0] for x in trs], [], emit, 0.35, pool="-", line=line)

    def lands(buf, sem, count, us, link):
        op(None, [], [buf], None, 0.0, us, pool=sem, inc=count, link=link)

    def tell(k, t):
        first = hop(T, topo, rank, k)
        e = topo.engines(core, first)
        send("%s%d" % (k, t), k, (B("%ss%d" % (k, t), 0, COLS[k]), first, e, B("%si%d" % (k, t), 0, COLS[k]), "r%s%d" % (k, t)))
        lands(B("%si%d" % (k, t), 0, 32), "r%s%d" % (k, t), 8 if near else 16, FAR if near else NEAR,
              [(1 - me, "%s%d" % (k, t)), (0, "f3")])

    PS = [B("ps%d" % b, 0, 512) for b in range(8)]
    AUD = [B("aud%d" % t, 0, W + 8) for t in range(3)]
    ROW = (0, 128, 16)
    P8 = (0, 8, 1)

    loads = [(B("li", 0, C, 1, P8), T.lens[:], 2.1), (B("spi", 0, C), T.spots[:], 2.5)]
    loads += [(B("aud0", 2 * QW * j, 2 * QW * (j + 1)), T.aud[:, 2 * QW * j:2 * QW * (j + 1)], 4.3 + 1.8 * j) for j in range(2)]
    loads += [(B("gi", 0, C), T.gua[:], 6.6)]
    for k, (o, a, us) in enumerate(loads):
        q = "sasss"[k]
        op(q, [], [], (lambda q, o, a, k: lambda: Q[q].dma_start(ap(o), a).then_inc(T.sem["l%d" % k], 16))(q, o, a, k), 0.08,
           pool="-", line="load")
        names["l%d" % k] = len(ops) - 1
        lands(o, "l%d" % k, 16, us, [(me, "l%d" % k)])
    port, mate = ports(T, topo, rank), T.cores[(rank + (1 if near else -1)) % N]
    every = topo.engines(core, mate)

    def quarter(t, j):
        return B("aud%d" % t, QW * j, QW * j + QW)

    for j in range(4):
        if near:
            send("q%d" % j, "q", *[(B("aud0", EW * p, EW * p + EW), port[p % 4], every[8 * (p % 2):8 * (p % 2) + 8],
                                    B("aud1", EW * p, EW * p + EW), "rq%d" % (p // 4)) for p in (2 * j, 2 * j + 1)])
        else:
            send("q%d" % j, "q", (quarter(0, j), mate, every, quarter(1, j), "rq%d" % j))
    for j in range(4):
        lands(quarter(1, j), "rq%d" % j, 16, FLY[0][me][j], [(1 - me, "q%d" % j)])
    for j in range(4):
        send("f%d" % j, "q", (quarter(1, j), port[j] if near else mate, every, quarter(2, j), "ra2"))
    lands(B("aud2", 0, W), "ra2", 64 if near else 32, FLY[1][me], [(1 - me, "f3")])

    pi_, pmi = new("si", 1), new("si", 1)
    pf, pm, npm, pg, row0 = f(1), f(1), f(1), f(1), f(1)
    selv, cmod, K, xs, s16, jv = f(128), f(NQ), f(NQ), f(144), f(32), f(C)
    spack = f(2 * C)
    tag0 = f(C)
    iota(pi_, [[0, 1]], 0, 1)
    iota(S(selv, 0, 128, 1, P8), [[-1, 8], [0, 16]], 0, 1)
    iota(cmod, [[0, NQ // 16], [1, 16]], 0, 0)
    iota(s16, [[16, 32]], 0, 0)
    iota(xs, [[1, 144]], -15, 0)
    lf_, ef = f(C + 1), new("sh", C + 1)
    zb, onb = new("sb", C), new("sb", 1024)
    MK = B("mk", 0, L + C)
    ms(onb, 1.0)
    for q in range(4):
        ms(B("mk", 1088 * q, 1088 * q + 1088), 1.0)
    ms(S(lf_, 0, 1), 0.0)
    ts(pmi, pi_, 15, OP.bitwise_and)
    cp(pf, pi_)
    ms(zb, 0.0)
    cp(pm, pmi)
    ts(npm, pm, -1.0, OP.mult)
    tt(pg, pf, pm, OP.subtract)
    ts(row0, pm, 0.0, OP.is_equal)
    sel, sel2 = new("sb", 128), new("sb", 128)
    ts(S(sel, 0, 128, 1, P8), S(selv, 0, 128, 1, P8), 0.0, OP.is_equal)
    ts(S(sel2, 0, 128, 1, P8), S(selv, 0, 128, 1, P8), 0.0, OP.is_equal, 2048.0, OP.mult)
    act(cmod, cmod, AF.Abs, bias=npm)
    act(K, cmod, AF.Relu, bias=ms(f(1), 2.0e7), scale=-2.0e7)
    zw = ts(new("sb", 144), xs, pg, OP.is_equal)
    zw2 = act(new("sb", 144), zw, scale=2.0)
    d1 = ts(f(), S(s16, 0, 16), pm, OP.add, float(L), OP.add)
    d2 = ts(f(32), s16, pm, OP.add, float(DUMP), OP.add)
    for t in range(3):
        ms(B("aud%d" % t, W, W + 16, 2), 0.0)
        ms(B("aud%d" % t, W + 1, W + 16, 2), float(LIFT))
    for lo in range(0, L, 1024):
        act(B("win", lo, lo + 1024), onb, scale=0.0)
    for lo in range(L, NEG, 640):
        act(B("win", lo, lo + 640), S(onb, 0, 640), scale=0.0)
    fill(B("y0", L, L + C), 0)
    act(B("hf", 0, 1024), onb, scale=2.0 * LIFT)
    fill(B("hf", 1024, L), 2 * LIFT)
    ms(B("win", NEG, NEG + 16), -1.0 - SH)
    gt_, blk, tri, nblk = new("sb", 128), new("sb", 128), new("sb", 128), new("sb", 128)
    pick(gt_, S(onb, 0, 128), [[-16, 8], [0, 16]], OP.is_ge, 0, 1)
    pick(blk, gt_, [[16, 8], [0, 16]], OP.is_ge, 15, -1)
    pick(tri, blk, [[1, 128]], OP.is_gt, 0, -1)
    act(nblk, blk, scale=-1.0)
    for q in range(8):
        pick(B("rs", 256 * q, 256 * q + 256), S(onb, 0, 256), [[-1, 2], [-16, 8], [0, 16]], OP.is_equal, -2 * q, 1)
    iota(tag0, [[2 * TAG, C]], TAG, 0)
    iota(S(spack, C, 2 * C), [[2 * TAG + NS, C]], 2 * TAG + L, 0)
    iota(jv, [[1, 16], [256, 16]], 0, 16)
    inc, jend, j0, nb, up = new("sb", C), f(), f(), f(32), f(64)
    fill(inc, 1)
    iota(S(inc, 0, C, 16), [[0, 16]], 241, 0)
    iota(jend, [[256, 16]], 15 - 2 * L, 16)
    iota(j0, [[256, 16]], -1 - 2 * L, 16)
    fill(nb, 0)
    fill(up, 0)
    nblkf, ntrif = act(f(128), blk, scale=-1.0), act(f(128), tri, scale=-1.0)
    sh, rxs, rxf = new("sb", 16), ms(new("sb", 17), 0.0), ms(f(40), 0.0)

    def steps(m, c0, c1, n=16):
        d = [f(n * m), f(n * m), f(n * m)]
        for x, c in zip(d, (c0, c1)):
            for s, v in enumerate(c):
                if v is not None:
                    iota(S(x, s, n * m, m), [[0, n]], int(v), 0)
        return d, [[S(x, s, n * m, m) for s in range(m)] for x in d]
    def wrap(o, src, n):
        mm([(o, S(zw, 15 - i, 143 - i), S(src, i, 16 * n, 16), i == 0, i == 15) for i in range(16)])

    def count(o, src, n, by):
        op("t", [zw, zw2, src], [o], lambda: [g.tensor.matmul(ap(o), ap(S(zw if ops[by]["q"] == "a" else zw2, 15 - i, 143 - i)),
                                                              ap(S(src, i, 16 * n, 16)), i == 0, i == 15) for i in range(16)],
           16 * 64 * CY)

    def spread(bank, src, n):
        mm([(S(bank, i, 16 * n, 16), B("rs", 128 * i, 128 * i + 128), src, True, True) for i in range(16)])

    def prefix(o, tot, x, rx, below, group):
        scan(S(rx, 1, 17), x, S(zb, 0, 16), 0.0, OP.add, OP.add)
        mm([(o, below, x, True, False)])
        mm([(o, group, S(rx, 0, 16), False, True)])
        return lambda: mm([(tot, group, S(rx, 16, 17), True, True)])

    cp(S(lf_, 1, C + 1, 1, P8), B("li", 0, C, 1, P8))
    scan(S(ef, 0, C + 1, 1, P8), S(onb, 0, C + 1, 1, P8), S(lf_, 0, C + 1, 1, P8), -2048.0, OP.mult, OP.add)
    mm([(S(PS[2], 0, C + 1), S(sel2, 0, 128, 1, P8), S(onb, 0, C + 1, 1, P8), True, False)])
    mm([(S(PS[2], 0, C + 1), S(sel, 0, 128, 1, P8), S(ef, 0, C + 1, 1, P8), False, True)])
    kb, ke = f(C), f(C)
    scan(kb, S(K, 0, C), S(PS[2], 0, C), 0.0, OP.max, OP.min)
    scan(ke, S(K, 0, C), S(PS[2], 1, C + 1), 0.0, OP.max, OP.min)
    eqi = cp(new("si", C), S(PS[2], 1, C + 1))
    tt(S(spack, 0, C), S(PS[2], 0, C), tag0, OP.add)
    BEG, END = S(kb, 15, C, 16), S(ke, 15, C, 16)
    LEN = tt(f(), END, BEG, OP.subtract)
    BOFF = cp(new("su", 16), tt(f(), tt(f(), ts(f(), LEN, 0.5, OP.is_lt), d1, OP.mult), BEG, OP.max))
    KEND = cp(new("su", 16), ts(new("si", 16), cp(new("si", 16), END), 4, OP.logical_shift_right))
    lb = ts(new("sb", C), ts(eqi, eqi, 15, OP.bitwise_and), pm, OP.is_gt)
    CUT, (cut0, cut1, cut) = steps(6, (BIG, 0, 0, None, None, 0), (None, None, None, 1, BIG, 0))
    AT, (at0, at1, at) = steps(3, (BIG, None, None), (None, BIG, None))
    FIN, (fin0, fin1, fin) = steps(2, (-BIG, None), (None, None), 32)
    TURN, (turn0, turn1, turn) = steps(2, (0, None), (None, None), 32)
    act(at0[1], BEG, bias=-1.0)
    act(at1[2], d1)
    cbig = ms(f(1), BIG)
    ms(S(PS[4], 0, 32, 2), -BIG)
    cp(IND(MK, BOFF), zb)
    G = cp(f(C), B("gi", 0, C))
    sgz = act(new("sb", C), G, AF.Sign, bias=-0.5)
    wrap(S(PS[7], 0, 16), sgz, 16)
    NZ = ts(f(), S(PS[7], 0, 16), -2.5, OP.is_lt)
    mm([(S(PS[6], 0, C), blk, sgz, True, True)])
    zr = ts(new("sb", C), S(PS[6], 0, C), -2.5, OP.is_ge, row0, OP.mult)
    pack = [f(C), f(2 * C), f(2 * C), f(2 * C)]
    fill(S(pack[3], 0, C), 0)
    fill(S(pack[1], C, 2 * C), 0)
    for t in range(2):
        act(B("ii%d" % t, L, L + C), G, scale=-1.0)
    sph, eye, spt = ts(new("sh", C), B("spi", 0, C), SH, OP.subtract), new("sb", 128), B("h0", 1024, 2048)
    pick(eye, S(onb, 0, 128), [[-1, 128]], OP.is_equal, 0, 1)
    P32 = (0, 32, 1)
    for h in range(2):
        for m in range(4):
            mm([(S(PS[4 * h + 1], 128 * m + 16 * e, 128 * m + 16 * e + 16, 1, P32), S(sph, e, C, 8),
                 S(eye, 64 * h + 16 * m, 64 * h + 16 * m + 16), True, True) for e in range(8)])
        act(S(spt, 512 * h, 512 * h + 512, 1, P32), S(PS[4 * h + 1], 0, 512, 1, P32))

    dma("s", [(B("win", 0, L, 1, (16 * m, 16 * m + 1, 1)), S(spt, 128 * m, 128 * m + 128, 1, P32)) for m in range(8)], 6.0,
        after=[names["q3"]])
    lu0 = cp(new("su", C), B("spi", 0, C))
    Y = [B("y0", 0, L + C), B("y1", 0, L), B("y2", 0, L)]
    II = [B("ii0", 0, L + C), B("ii1", 0, L + C), B("ii0", 0, L + C)]
    WIN = B("win", 0, NEG + 8)
    H0, HF = B("h0", 0, DUMP + 2 * C), B("hf", 0, DUMP + 2 * C)
    Fb, Rx, Z1, Z2 = new("sb", C + 2), new("sb", C + 2), new("sb", C + 2), new("sb", C + 2)
    for x in (S(Fb, C, C + 2), S(Rx, 0, 1), S(Rx, C + 1, C + 2), S(Z1, 0, 2), S(Z2, 0, 2)):
        ms(x, 0.0)
    fill(S(H0, 0, NQ), 0, NQ // 2)
    tmp, k1, k2, lim = f(C), f(C), f(C), tag0
    part[0] = "lift"
    lu = new("su", C)
    for q in range(4):
        o = S(PS[6], 64 * q, 64 * q + 64)
        wrap(o, S(MK, 1024 * q + 1, 1024 * q + 1025), 64)
        cp(S(lu, 64 * q, 64 * q + 64), tt(S(k2, 64 * q, 64 * q + 64), ts(S(k1, 64 * q, 64 * q + 64), o, 8.0, OP.is_lt, W + 1.0, OP.mult),
                                          B("spi", 64 * q, 64 * q + 64), OP.max))
    cp(IND(S(HF, 0, L + C), BOFF), S(II[1], L, L + C))
    LEN1 = act(f(), LEN, bias=-1.0)
    wrap(S(PS[7], 0, 16), ts(new("sh", C), IND(WIN, ts(new("su", 16), END, 1.0, OP.subtract)), row0, OP.mult), 16)
    last = tt(f(), ts(f(), S(PS[7], 0, 16), SH, OP.add), ts(f(), LEN, 0.5, OP.is_lt, float(W), OP.mult), OP.max)
    sf2, lt, lto, th2 = f(2 * C), new("sb", C), new("sb", 2 * C), f(32)
    kf = S(sf2, 0, C)

    def upto(t, a, lw):
        none(at0[2], a, 0)
        scan(AT[2], AT[0], AT[1], 0.0, OP.add, OP.min)
        return tt(S(sf2, 0, C), IND(AUD[t], lw), act(tmp, IND(II[t], cp(new("su", 16), at[2]))), OP.add)

    def sums(t, onv):
        part[0] = "sums%d" % t
        for q in range(8):
            src = IND(AUD[t], S(lu if t else lu0, 32 * q, 32 * q + 32))
            act(S(Y[t], 512 * q, 512 * q + 512), src, q="v" if q in onv else "a", line="y%d%d" % (t, q in onv))
        if t == 0:
            tt(IND(Y[t], BOFF), act(kf, IND(Y[t], BOFF)), G, OP.subtract)
        half = 32 if t == 0 else 64
        for q in range(4):
            lo, hi = 1024 * q, 1024 * q + 1024
            for l in range(lo, hi, PIECE[t]):
                h = l + PIECE[t]
                scan(S(II[t], l, h), S(HF if t else MK, l, h), S(Y[t], l, h), S(II[t], l - 1, l) if l else float(LIFT),
                     OP.min if t else OP.mult, OP.add)
            o = S(PS[0], 64 * q, 64 * q + 64) if q < 3 else S(PS[1], 0, 64)
            if q < 3 or half == 64:
                count(o, B("sg", lo, hi), 64, sign(B("sg", lo, hi), S(II[t], lo, hi)))
            else:
                mid = lo + 16 * half
                act(B("sg", lo, mid), S(II[t], lo, mid), AF.Sign, bias=0.5)
                ts(B("sg", mid, hi), S(II[t], mid, hi), 0.0, OP.is_lt)
                wrap(o, B("sg", lo, hi), 64)
        ts(S(Fb, 0, 192), S(PS[0], 0, 192), 2.5, OP.is_le)
        scan(S(Rx, 1, 193), S(onb, 0, 192), S(Fb, 0, 192), 0.0, OP.mult, OP.add)
        ts(S(Fb, 192, 192 + half), S(PS[1], 0, half), 2.5, OP.is_le)
        if half < 64:
            ts(S(Fb, 192 + half, 256), S(PS[1], half, 64), 6.5, OP.is_ge)
        scan(S(Rx, 193, C + 1), S(onb, 0, 64), S(Fb, 192, C), S(Rx, 192, 193), OP.mult, OP.add)
        tt(S(Z2, 2, C + 2), IND(Fb, KEND), lb, OP.mult)
        act(S(Z1, 2, C + 2), IND(Rx, KEND))
        mm([(S(PS[2], 0, C + 1), blk, S(Z2, 1, C + 2), True, False), (S(PS[2], 0, C + 1), blk, S(Z1, 1, C + 2), False, True)])
        o = S(PS[3], 0, C)
        mm([(o, blk, zr, True, False), (o, blk, S(Z2, 2, C + 2), False, False), (o, nblk, S(Z2, 1, C + 1), False, False),
            (o, blk, S(Z1, 2, C + 2), False, False), (o, nblk, S(Z1, 1, C + 1), False, True)])
        scan(k1, S(K, 0, C), S(PS[2], 0, C), 0.0, OP.max, OP.min)
        scan(k2, S(K, 0, C), S(PS[2], 1, C + 1), 0.0, OP.max, OP.min)
        act(S(pack[t], 0, C), o)
        M = tt(f(), tt(f(), NZ, S(k1, 15, C, 16), OP.add), S(k2, 15, C, 16), OP.subtract)
        part[0] = "visit%d" % t
        return M

    hA, hK, relh = cmod, f(NQ), new("sh", NQ)
    AX, RW = f(NQ + C), f(NQ + C)

    def slot(s):
        return B("win", L + s, NEG, NS)

    def place(src, n, ev=None):
        vi = cp(new("si", n), src) if ev is None else tt(new("si", n), src, ev, OP.max)
        return ts(new("su", n), ts(new("si", n), vi, TAG - 1, OP.bitwise_and), float(NEG), OP.min)

    def lookup(t, offu, n):
        tt(IND(H0, offu), S(pack[t], 0, 16 * n), S(spack, 0, 16 * n), OP.add)
        scan(hA, S(onb, 0, NQ), S(H0, 0, NQ), -1.0, OP.add, OP.max)
        if t < 2:
            fill(S(H0, 0, NQ), 0, NQ // 2)
        scan(hK, K, hA, 0.0, OP.max, OP.min)
        pos = place(S(hK, 15, NQ, 16), NQ // 16)
        ts(relh, IND(WIN, pos), -SH, OP.max, row0, OP.mult)
        wrap(S(PS[7], 0, NQ // 16), relh, NQ // 16)
        ts(B("rs%d" % t, 0, NQ // 16), S(PS[7], 0, NQ // 16), SH, OP.add)
        tell("r", t)
        act(S(RW, NQ, NQ + C), IND(WIN, S(pos, 0, 16)))

    Ed, off, low = f(64), f(64), f(1)
    a, b, aK0 = f(), cut1[2], S(Ed, 32, 64, 2)

    def release(t, x, nrel, thr1):
        n = 16 if t == 0 else 32
        E = f(n)
        if t == 0:
            ts(E, x, 0.5, OP.is_lt)
        else:
            tt(S(E, 0, 16), x, thr1, OP.is_le)
            tt(S(E, 16, 32), x, aK0, OP.is_le)
        tt(S(Ed, 1, 2 * n, 2), E, S(d2, 0, n), OP.mult)
        total = prefix(S(PS[4], 1, 32, 2), S(PS[5], 40, 41), nrel, S(rxf, 0, 17), ntrif, nblkf)
        tt(S(off, 1, 32, 2), S(PS[4], 1, 32, 2), S(Ed, 1, 32, 2), OP.max)
        if t:
            scan(S(off, 32, 64), S(PS[4], 0, 32), S(Ed, 32, 64), 0.0, OP.add, OP.max)
        offu = cp(new("su", n), S(off, 1, 2 * n, 2))
        lookup(t, offu, n)
        return total

    def stay(t, R):
        total = prefix(S(PS[4], 64, 80), S(PS[4], 80, 81), b, S(rxf, 20, 37), ntrif, nblkf)
        if t == 2:
            total()
        n = 17 if t == 2 else 16
        return ts(f(n), S(PS[4], 64, 64 + n), act(f(1), R, scale=-1.0, bias=float(L)), OP.add)

    def shorts(t, total):
        total()
        prefix(S(PS[5], 0, 16), S(PS[5], 16, 17), sh, rxs, tri, blk)()
        R = cp(B("cs%d" % t, 2, 3), S(PS[5], 40, 41))
        ts(low, S(PS[5], 40, 41), float(SLOT), OP.subtract)
        ts(B("cs%d" % t, 1, 2), S(PS[5], 16, 17), R, OP.min, low, OP.max)
        st = dict(R=R, S=cp(B("cs%d" % t, 0, 1), S(PS[5], 16, 17)))
        tell("c", t)
        LP = st["LP"] = stay(t, R)
        sr = st["sr"] = ts(f(), S(PS[5], 0, 16), R, OP.subtract)
        st["own"] = tt(f(), act(f(), sr, bias=act(f(1), R, bias=float(NQ))), none(f(), sr, -1), OP.min)
        nc1 = tt(cut1[1], sr, S(LP, 0, 16), OP.subtract)
        tight = ts(f(), tt(f(), nc1, b, OP.add), -0.5, OP.is_gt, BIG, OP.mult)
        st["srs"] = tt(f(), tt(f(), act(f(), sh, scale=-BIG, bias=cbig), sr, OP.add), tight, OP.add)
        return st

    def given(t, st):
        y = ts(f(), st["sr"], B("ci%d" % t, 0, 1), OP.add, float(NQ - 1), OP.min)
        return cp(new("su", 16), tt(f(), y, st["own"], OP.max))

    def arrive(t, qu):
        h = ts(new("sh", NQ // 16), B("ri%d" % t, 0, NQ // 16), SH, OP.subtract)
        spread(PS[6], h, NQ // 16)
        act(S(RW, 0, NQ), S(PS[6], 0, NQ))
        act(slot(t), IND(RW, qu))

    M = sums(0, ONV[0])
    x = tt(f(), LEN1, M, OP.add)
    nrel = ts(f(), x, -1.0, OP.mult, 0.0, OP.min)
    ts(sh, x, 0.0, OP.is_lt)
    R = release(0, x, nrel, None)
    act(a, tt(b, LEN, nrel, OP.add))
    st, n, n0 = shorts(0, R), None, None

    act(S(th2, 0, 16), LEN, scale=0.0, bias=2.5)
    for t in (1, 2):
        z, Rb = B("ci%d" % (t - 1), 1, 2), B("ci%d" % (t - 1), 2, 3)
        M = sums(t, ONV[t])
        lw = cp(new("su", 16), tt(f(), ts(f(), tt(f(), a, LEN, OP.subtract), -0.5, OP.is_lt, float(W), OP.mult), last, OP.max))
        sofar = upto(t, tt(at1[0], a, LEN1, OP.min), lw)
        nK = tt(f(), M, act(f(), a, scale=-1.0, bias=1.0), OP.max)
        if t == 1:
            count(S(PS[0], 0, 16), S(lto, 0, C), 16, sign(S(lto, 0, C), sofar))
            more = ts(f(), S(PS[0], 0, 16), 2.5, OP.is_le)
        else:
            ew = ts(new("su", 16), tt(f(), e0, n, OP.mult), float(W), OP.add)
            sofar = tt(S(sf2, C, 2 * C), IND(AUD[2], ew), sofar, OP.add)
            wrap(S(PS[0], 0, 32), act(lto, sf2, AF.Sign, bias=0.5), 32)
            mm([(S(PS[0], C, 2 * C), blk, S(lto, 0, C), True, True)])
            act(S(th2, 16, 32), n, scale=101.5, bias=-99.0)
            both = tt(f(32), S(PS[0], 0, 32), th2, OP.is_le)
            more = tt(f(), S(both, 0, 16), S(both, 16, 32), OP.add)
            tt(S(pack[2], C, 2 * C), S(PS[0], C, 2 * C), lim, OP.is_le)
            fill(S(HF, 0, L), 0)
        nK = tt(cut0[4], nK, more, OP.subtract)
        aK = tt(f(), a, nK, OP.add)
        either(aK0, aK, AF.Relu, -1.0, 1.0, -1.0, OP.add, 0.0, OP.max)
        thr1 = ts(f(), aK, 1.5, OP.is_lt, BIG, OP.mult)
        ts(cut1[0], S(st["LP"], 0, 16), z, OP.add, Rb, OP.subtract)
        ns = ts(cut0[3], st["srs"], z, OP.add, Rb, OP.is_ge)
        scan(CUT[2], CUT[0], CUT[1], 0.0, OP.subtract, OP.min)
        x, nrel = cut[4], cut[5]
        qu = given(t - 1, st)
        act(S(AX, NQ, NQ + C), IND(AUD[t], B("rs%d" % (t - 1), 0, 16)), scale=-1.0)
        act(S(AX, 0, NQ), IND(AUD[t], B("ri%d" % (t - 1), 0, NQ // 16)), scale=-1.0)
        tt(lt, IND(AX, qu), sofar, OP.is_gt)
        arrive(t - 1, qu)
        if t == 1:
            wrap(S(PS[6], 0, 16), ts(new("sh", C), slot(0), -SH, OP.max, row0, OP.mult), 16)
            e0 = ts(f(), S(PS[6], 0, 16), SH, OP.subtract)
        thr = tt(f(), ts(f(), x, -0.5, OP.is_gt, 100.0, OP.mult), act(f(), ns, scale=93.5, bias=-93.5), OP.add)
        wrap(S(PS[5], 0, 16), lt, 16)
        tt(sh, S(PS[5], 0, 16), thr, OP.is_ge)
        R = release(t, x, nrel, thr1)
        if t == 1:
            pick(slot(3), slot(0), [[0, C]], OP.is_ge, 0, 0)
        act(b, tt(f(), nrel, cut[3], OP.subtract), bias=1.0)
        tt(a, b, a, OP.min)
        n0, n = n, tt(f(), b, a, OP.subtract)
        if t == 1:
            spread(PS[6], act(new("sb", 16), n), 16)
            act(lim, S(PS[6], 0, C), scale=-96.5, bias=99.0)
        st = shorts(t, R)

    part[0] = "end"
    z, Rb = B("ci2", 1, 2), B("ci2", 2, 3)
    lo_ = tt(new("sb", 16), tt(f(), ts(f(), n, 1.0, OP.is_equal, 2.0, OP.mult), n0, OP.mult), n, OP.subtract)
    spread(PS[3], lo_, 16)
    act(S(pack[3], C, 2 * C), S(PS[3], 0, C), bias=2.0)
    PR = f(32)
    act(S(PR, 0, 16), S(st["LP"], 0, 16), scale=-1.0, bias=float(L))
    tt(S(PR, 16, 32), S(PR, 0, 16), a, OP.add)
    PM = act(S(FIN[0], 1, 32, 2), cut1[1], bias=float(L))
    tt(S(FIN[0], 33, 64, 2), PM, a, OP.add)
    tt(S(FIN[1], 1, 32, 2), none(f(), a, 0), S(d2, 0, 16), OP.min)
    D2 = tt(f(), none(f(), n, 0), S(d2, 16, 32), OP.min)
    tg = act(f(1), S(st["LP"], 16, 17), scale=-1.0, bias=act(f(1), pg, scale=16.0, bias=float(L)))
    SR = ts(f(1), st["S"], st["R"], OP.subtract)
    b1 = act(f(), b, bias=1.0 - 2048.0)
    ns = ts(f(), st["srs"], z, OP.add, Rb, OP.is_ge)
    ts(fin1[0], PR, z, OP.subtract, Rb, OP.add)
    tt(S(FIN[1], 33, 64, 2), ns, D2, OP.mult)
    scan(FIN[2], FIN[0], FIN[1], 0.0, OP.min, OP.max)
    vi = cp(new("si", 32), fin[1])
    ts(turn0[1], fin[1], L - 0.5, OP.is_lt, 240.0, OP.mult)
    tt(fin[0], ts(new("si", 32), vi, 4, OP.logical_shift_right, 15, OP.bitwise_and), ts(new("si", 32), vi, 8, OP.logical_shift_right),
       OP.subtract)
    scan(TURN[2], TURN[0], FIN[2], 0.0, OP.mult, OP.add)
    tt(IND(HF, cp(new("su", 32), turn[1])), pack[3], spack, OP.add)
    qu = given(2, st)
    q3 = ts(f(1), ts(f(1), Rb, z, OP.subtract, SR, OP.min), tg, OP.add)
    ev = ts(k1, jv, q3, OP.is_ge, float(1024 * TAG - 1), OP.mult)
    room = act(f(), tt(f(), S(FIN[1], 0, 32, 2), PM, OP.min), scale=-1.0, bias=L - 2048.0)
    yh = ts(new("sh", 16), tt(f(), tt(f(), b1, ns, OP.subtract), room, OP.min), -2048.0, OP.max)
    spread(PS[3], yh, 16)
    act(k2, S(PS[3], 0, C), bias=2048.0)
    dma("s", [(T.yn[:], S(k2, 0, C, 1, ROW))])
    HB, run, DG, OUT = tmp, S(sf2, 0, C), G, II[1]
    dma("s", [(HB, S(HF, 0, L, 1, ROW))], 2.8)
    scan(run, inc, HB, 0.0, OP.add, OP.max)

    def turn_(o, x):
        op("v", [x], [o], lambda: [g.vector.transpose(ap(o), ap(x))], cost(o, [x]))
        return o

    tt(S(nb, 0, 16), S(run, 15, C, 16), jend, OP.subtract)
    nt = turn_(f(32), nb)
    for h in (0, 16):
        scan(S(up, h + 1, h + 16), S(nt, h, h + 15), S(zb, 0, 15), 0.0, OP.max, OP.max)
        top_ = f(1)
        op("v", [S(nt, h, h + 16)], [top_], (lambda o, x: lambda: [g.vector.tensor_reduce(ap(o), ap(x), AX_.X, OP.max)])(top_, S(nt, h, h + 16)),
           64 * CY)
        ts(S(up, 32 + h, 48 + h), S(zb, 0, 16), top_, OP.max)
    back = turn_(f(64), up)
    first = tt(f(), tt(f(), S(back, 0, 16), S(back, 31, 47), OP.max), j0, OP.add)
    for k in range(16):
        scan(S(DG, k, C, 16), S(onb, 0, 16), S(HB, 16 * k, 16 * k + 16), S(first, k, k + 1), OP.add, OP.max)
    arrive(2, qu)
    act(slot(4), IND(RW, qu), q="v")
    for q in range(4):
        lo = 1024 * q
        pos = place(S(DG, 64 * q, 64 * q + 64), 64, S(ev, 64 * q, 64 * q + 64))
        for h in range(2):
            o, src = S(OUT, lo + 512 * h, lo + 512 * h + 512), IND(WIN, S(pos, 32 * h, 32 * h + 32))
            act(o, src, bias=SH, q="av"[h])
            dma("s", [(T.yo[i:128:16, :], S(OUT, C * i, C * i + C, 1, ROW)) for i in range(4 * q + 2 * h, 4 * q + 2 * h + 2)])
    return ops, names, sent
